import numpy as np
import ml_dtypes


def mxq(x, axis, fmt="e4m3"):
    dtype, down = {"e4m3": (ml_dtypes.float8_e4m3fn, 7), "e5m2": (ml_dtypes.float8_e5m2, 14)}[fmt]
    v = np.moveaxis(np.asarray(x, np.float32).astype(ml_dtypes.bfloat16).astype(np.float64), axis, -1)
    blocks = v.reshape(v.shape[:-1] + (-1, 32))
    amax = np.abs(blocks).max(-1, keepdims=True)
    byte = np.maximum(np.where(amax > 0, np.frexp(amax)[1] - 1 + 127, 0) - down, 1)
    scale = np.exp2(byte - 127.0)
    codes = (blocks / scale).astype(np.float32).astype(dtype).astype(np.float64)
    return np.moveaxis((codes * scale).reshape(v.shape), -1, axis)


WIDE = False


def mx_kscale(k):
    if not WIDE:
        return np.ones(k)
    levels = np.array([10, -10, 5, -5, 0])
    if k % 512:
        return np.exp2(np.random.permutation(np.resize(levels, k // 32))).repeat(32)
    a = np.empty((k // 512, 16))
    for p in range(k // 512):
        a[p, :8] = np.random.permutation(np.resize(levels, 8))
        for g in range(8):
            far = levels[np.abs(levels - a[p, g]) >= 10]
            a[p, g + 8] = far[np.random.randint(len(far))]
    return np.exp2(a.ravel()).repeat(32)


def f64(x):
    return np.asarray(x).astype(np.float64)


def striped(idx):
    return np.tile(idx.reshape(-1, 16).T, (8, 1)).astype(np.uint16)


def unstriped(offs):
    return offs[:16].T.reshape(-1).astype(np.int64)


def striped8(idx):
    return np.concatenate([x.reshape(-1, 16).T for x in idx]).astype(np.uint16)


def runs(offs, k):
    lists = np.stack([offs[16 * r : 16 * r + 16].T.reshape(-1) for r in range(8)]).astype(np.int64)
    return lists[np.arange(k) % 512 // 64]


def pack_weight(w):
    k, n = w.shape
    w = f64(np.asarray(w, np.float32).astype(ml_dtypes.bfloat16)).reshape(k // 32, 32, n)
    amax = np.abs(w).max(1)
    byte = np.clip(np.where(amax > 0, np.frexp(amax)[1] - 1 + 127 - 7, 1), 1, 254)
    scaled = (w * np.exp2(127.0 - byte)[:, None, :]).reshape(k, n).astype(np.float32)
    words = np.ascontiguousarray(scaled.reshape(k // 512, 128, 4, n).transpose(0, 1, 3, 2)).astype(ml_dtypes.float8_e4m3fn).view(np.uint8)
    return words, np.ascontiguousarray(byte.astype(np.uint8).reshape(k // 512, 16, n))


def unpack_weight(words, scales):
    g, p, n, _ = words.shape
    vals = np.ascontiguousarray(words).view(ml_dtypes.float8_e4m3fn).astype(np.float64) * np.repeat(np.exp2(scales.astype(np.float64) - 127.0), 8, axis=1)[..., None]
    return vals.transpose(0, 1, 3, 2).reshape(g * 512, n)


E2M1 = np.array([0.0, 0.5, 1.0, 1.5, 2.0, 3.0, 4.0, 6.0, -0.0, -0.5, -1.0, -1.5, -2.0, -3.0, -4.0, -6.0])


def pack_fp4(w):
    k, n = w.shape
    w = f64(np.asarray(w, np.float32).astype(ml_dtypes.bfloat16)).reshape(k // 32, 32, n)
    amax = np.abs(w).max(1)
    mant, ex = np.frexp(amax / 6.0)
    byte = np.clip(np.where(amax > 0, np.where(mant > 0.5, ex, ex - 1) + 127, 1), 1, 254)
    scaled = (w * np.exp2(127.0 - byte)[:, None, :]).reshape(k, n).astype(np.float32)
    c = np.ascontiguousarray(scaled.reshape(k // 512, 128, 4, n).transpose(0, 1, 3, 2)).astype(ml_dtypes.float4_e2m1fn).view(np.uint8) & 0xF
    words = (c[..., 0::2] | (c[..., 1::2] << 4)).reshape(k // 512, 128, 2 * n)
    return np.ascontiguousarray(words), np.ascontiguousarray(byte.astype(np.uint8).reshape(k // 512, 16, n))


def unpack_fp4(words, scales):
    g, _, n = scales.shape
    words = np.ascontiguousarray(words).reshape(g, 128, n, 2)
    nib = np.empty((g, 128, n, 4), np.uint8)
    nib[..., 0::2] = words & 0xF
    nib[..., 1::2] = words >> 4
    vals = E2M1[nib] * np.repeat(np.exp2(scales.astype(np.float64) - 127.0), 8, axis=1)[..., None]
    return vals.transpose(0, 1, 3, 2).reshape(g * 512, n)


def silu(v):
    return v / (1.0 + np.exp(-np.maximum(v, -700.0)))

def planes(y):
    n, m = y.shape
    v = y.astype(np.float32).astype(ml_dtypes.bfloat16).astype(np.float64).reshape(n // 32, 32, m)
    top = np.abs(v).max(1)
    byte = np.clip(np.where(top > 0, np.frexp(top)[1] - 1 + 127 - 7, 1), 1, 254)
    codes = (v * np.exp2(127.0 - byte)[:, None, :]).reshape(n, m).astype(np.float32).astype(ml_dtypes.float8_e4m3fn).view(np.uint8)
    words = codes.reshape(n // 512, 128, 4, m).transpose(0, 1, 3, 2)
    return np.ascontiguousarray(words), np.ascontiguousarray(byte.astype(np.uint8).reshape(n // 512, 16, m))


K, T, S, V, N, U, H = 512, 2048, 512, 1024, 512, 1024, 512


def setup_inputs():
    n = np.random.standard_normal
    s = mx_kscale(K)[:, None]
    u = mx_kscale(H)
    packed_xT = pack_weight(n((K, T)) * s)
    packed_w2 = pack_fp4(n((H, N)) / np.sqrt(H) / u[:, None])
    return {
        "x_words": packed_xT[0],
        "x_scales": packed_xT[1],
        "w1": (n((K, H)) / np.sqrt(K) / s * u).astype(np.float32),
        "mem": (n((H, U)) * u[:, None]).astype(np.float32),
        "w2_words": packed_w2[0],
        "w2_scales": packed_w2[1],
        "offs": striped(np.random.permutation(T)[:S]),
        "slot": striped8(np.stack([np.random.permutation(U)[:S] for _ in range(8)])),
        "rd": striped8(np.random.randint(0, U, (8, V))),
    }


def reference(x_words, x_scales, w1, mem, w2_words, w2_scales, offs, slot, rd):
    xq = unpack_weight(x_words, x_scales)[:, unstriped(offs)]
    y = mxq(f64(w1), 0, "e4m3").T @ xq
    pg = f64(mem).copy()
    pg[np.arange(H)[:, None], runs(slot, H)] = y
    z = silu(pg[np.arange(H)[:, None], runs(rd, H)])
    out_0 = unpack_fp4(w2_words, w2_scales).T @ mxq(z, 0, "e4m3")
    return (out_0,) + planes(out_0)

@@ -1,0 +1,229 @@
+from contextlib import ExitStack
+
+import concourse.mybir as mybir
+
+K, T, S, V, N, U, H = 512, 2048, 512, 1024, 512, 1024, 512
+FLOPS = 2 * K * H * S + 2 * H * N * V
+
+F32 = mybir.dt.float32
+BF16 = mybir.dt.bfloat16
+I32 = mybir.dt.int32
+U32 = mybir.dt.uint32
+U16 = mybir.dt.uint16
+U8 = mybir.dt.uint8
+FP8X4 = mybir.dt.float8_e4m3fn_x4
+FP4X4 = mybir.dt.float4_e2m1fn_x4
+SILU = mybir.ActivationFunctionType.Silu
+
+P = 128
+PACK = 4
+QUADS = 4
+PER_COL = 16
+PICK = 256
+READ = 256
+
+
+def tile_picked_pageread_silu_po_kernel(
+    tc, x_words, x_scales, w1, mem, w2_words, w2_scales, offs, slot, rd, out_0, out_1, out_2
+):
+    nc = tc.nc
+    with ExitStack() as ctx:
+        keep = ctx.enter_context(tc.tile_pool(name="keep", bufs=1))
+        psum = ctx.enter_context(tc.psum_pool(name="psum", bufs=1))
+
+        offs_sb = keep.tile([P, S // PER_COL], U16, name="offs_sb")
+        slot_sb = keep.tile([P, S // PER_COL], U16, name="slot_sb")
+        rd_sb = keep.tile([P, V // PER_COL], U16, name="rd_sb")
+        x_codes = keep.tile([P, T], U32, name="x_codes", align_bytes=64)
+        x_bytes = keep.tile([P, T], U8, name="x_bytes", align_bytes=64)
+        w2_raw = keep.tile([P, 2 * N], U8, name="w2_raw", align_bytes=64)
+        w2_raw_bytes = keep.tile([P, N], U8, name="w2_raw_bytes", align_bytes=64)
+        w1_raw = keep.tile([P, PACK, H], F32, name="w1_raw", align_bytes=64)
+        page = [keep.tile([P, U], F32, name="page%d" % t, align_bytes=64) for t in range(PACK)]
+
+        nc.vector.memset(x_bytes[:].bitcast(I32), 0)
+        nc.vector.memset(w2_raw_bytes[:].bitcast(I32), 0)
+
+        nc.sync.dma_start(out=w2_raw[:].bitcast(I32), in_=w2_words[0].bitcast(I32))
+        nc.sync.dma_start(offs_sb[:], offs)
+        nc.sync.dma_start(out=w1_raw[:], in_=w1.rearrange("(p j) c -> p j c", j=PACK))
+        for q in range(QUADS):
+            nc.sync.dma_start(
+                out=x_bytes[32 * q : 32 * q + 4, :].bitcast(I32), in_=x_scales[0, 4 * q : 4 * q + 4, :].bitcast(I32)
+            )
+        nc.sync.dma_start(out=x_codes[:].bitcast(I32), in_=x_words[0].rearrange("p c r -> p (c r)").bitcast(I32))
+        nc.sync.dma_start(slot_sb[:], slot)
+        mem_rows = mem.rearrange("(p t) u -> p t u", t=PACK)
+        for t in range(2):
+            nc.sync.dma_start(out=page[t][:], in_=mem_rows[:, t, :])
+        for q in range(QUADS):
+            nc.sync.dma_start(
+                out=w2_raw_bytes[32 * q : 32 * q + 4, :].bitcast(I32),
+                in_=w2_scales[0, 4 * q : 4 * q + 4, :].bitcast(I32),
+            )
+        for t in range(2, PACK):
+            nc.sync.dma_start(out=page[t][:], in_=mem_rows[:, t, :])
+        nc.sync.dma_start(rd_sb[:], rd)
+
+        w2_codes = keep.tile([P, 2 * N], U8, name="w2_codes", align_bytes=64)
+        w2_bytes = keep.tile([P, N], U8, name="w2_bytes", align_bytes=64)
+        nc.vector.tensor_copy(
+            out=w2_codes[:].rearrange("p (t m b) -> p m t b", t=PACK, b=2),
+            in_=w2_raw[:].rearrange("p (m t b) -> p m t b", t=PACK, b=2),
+        )
+
+        halves = S // PICK
+        picked_bytes = [keep.tile([P, PICK], U8, name="picked_bytes%d" % h, align_bytes=64) for h in range(halves)]
+        picked_codes = [keep.tile([P, PICK], U32, name="picked_codes%d" % h, align_bytes=64) for h in range(halves)]
+
+        def entries(lst, start, count):
+            return lst[:, start // PER_COL : (start + count) // PER_COL]
+
+        w1_bf = keep.tile([P, PACK * H], BF16, name="w1_bf", align_bytes=64)
+        w1_dst = w1_bf[:].rearrange("p (t m j) -> p m j t", t=PACK, j=PACK)
+        half_m = P // 2
+        w1_src = w1_raw[:].rearrange("p j (m t) -> p m j t", t=PACK)
+        nc.scalar.copy(out=w1_dst[:, 0:half_m], in_=w1_src[:, 0:half_m])
+        nc.vector.tensor_copy(out=w1_dst[:, half_m:P], in_=w1_src[:, half_m:P])
+        for h in range(halves):
+            nc.vector.tensor_copy(out=picked_bytes[h][:], in_=x_bytes[:].indirect(entries(offs_sb, h * PICK, PICK)))
+
+        w1_codes = keep.tile([P, H], U32, name="w1_codes", align_bytes=64)
+        w1_bytes = keep.tile([P, H], U8, name="w1_bytes", align_bytes=64)
+        nc.vector.quantize_mx(out=w1_codes[:].bitcast(FP8X4), scales=w1_bytes[:], in_=w1_bf[:])
+
+        for h in range(halves):
+            nc.vector.tensor_copy(out=picked_codes[h][:], in_=x_codes[:].indirect(entries(offs_sb, h * PICK, PICK)))
+
+        y = [keep.tile([P, S], F32, name="y%d" % t, align_bytes=64) for t in range(PACK)]
+        for h in range(halves):
+            for t in range(PACK):
+                acc = psum.tile([P, PICK], F32, name="acc1", bufs=4)
+                cols = slice(t * P, (t + 1) * P)
+                nc.tensor.matmul_mx(
+                    out=acc[:],
+                    lhsT=w1_codes[:, cols].bitcast(FP8X4),
+                    lhsT_scale=w1_bytes[:, cols],
+                    rhs=picked_codes[h][:].bitcast(FP8X4),
+                    rhs_scale=picked_bytes[h][:],
+                    start=True,
+                    stop=True,
+                )
+                nc.scalar.copy(out=y[t][:, h * PICK : (h + 1) * PICK], in_=acc[:])
+
+        def scatter(t, start, count):
+            nc.vector.tensor_copy(
+                out=page[t][:].indirect(entries(slot_sb, start, count)), in_=y[t][:, start : start + count]
+            )
+
+        scatter(0, 0, PICK)
+        scatter(1, 0, S)
+        scatter(0, PICK, PICK)
+        scatter(2, 0, S)
+        scatter(3, 0, S)
+        nc.vector.tensor_copy(
+            out=w2_bytes[:].rearrange("p (t m) -> p m t", t=PACK),
+            in_=w2_raw_bytes[:].rearrange("p (m t) -> p m t", t=PACK),
+        )
+
+        chunks = V // READ
+        last = chunks - 1
+        out_rows = out_0.rearrange("(p t) v -> p t v", t=PACK)
+        out_words = out_1[0].rearrange("p c r -> p (c r)").bitcast(I32)
+        out_bytes = keep.tile([P, V], U8, name="out_bytes", align_bytes=64)
+
+        def woven(ap):
+            return ap.rearrange("p (c i t) -> p c t i", i=4, t=PACK)
+
+        def planes(ap):
+            return ap.rearrange("p t (c i) -> p c t i", i=4)
+
+        got_all = keep.tile([P, 2 * PACK - 1, READ], F32, name="got_all", align_bytes=64)
+
+        def gather(c, part):
+            base = PACK - 1 if c % 2 == 0 else 0
+            order = (1, 2, 3, 0) if c % 2 == 0 else (0, 1, 2, 3)
+            for t in order[:-1] if part == 0 else order[-1:]:
+                nc.vector.tensor_copy(
+                    out=got_all[:, base + t, :], in_=page[t][:].indirect(entries(rd_sb, c * READ, READ))
+                )
+            return got_all[:, base : base + PACK, :]
+
+        def activate(v0, width, got):
+            z_bf = keep.tile([P, PACK * width], BF16, name="z_bf%d" % v0, align_bytes=64)
+            nc.scalar.activation(out=woven(z_bf[:]), in_=planes(got), func=SILU)
+            return z_bf
+
+        def multiply(v0, width, z_bf):
+            z_codes = keep.tile([P, width], U32, name="z_codes%d" % v0, align_bytes=64)
+            z_bytes = keep.tile([P, width], U8, name="z_bytes%d" % v0, align_bytes=64)
+            nc.vector.quantize_mx(out=z_codes[:].bitcast(FP8X4), scales=z_bytes[:], in_=z_bf[:])
+            per_bank = 512 // width
+            banks = []
+            for u in range(PACK // per_bank):
+                acc = psum.tile([P, per_bank, width], F32, name="acc2", bufs=4)
+                for e in range(per_bank):
+                    t = per_bank * u + e
+                    nc.tensor.matmul_mx(
+                        out=acc[:, e, :],
+                        lhsT=w2_codes[:, 2 * t * P : 2 * (t + 1) * P].bitcast(FP4X4),
+                        lhsT_scale=w2_bytes[:, t * P : (t + 1) * P],
+                        rhs=z_codes[:].bitcast(FP8X4),
+                        rhs_scale=z_bytes[:],
+                        start=True,
+                        stop=True,
+                    )
+                banks.append(acc)
+            return banks
+
+        def unload(v0, width, banks, copy):
+            res = keep.tile([P, PACK, width], F32, name="res%d" % v0, align_bytes=64)
+            per_bank = PACK // len(banks)
+            for u in range(len(banks)):
+                copy(out=res[:, per_bank * u : per_bank * (u + 1), :], in_=banks[u][:])
+            nc.sync.dma_start(out=out_rows[:, :, v0 : v0 + width], in_=res[:])
+            return res
+
+        def hand_on(v0, width, res_bf):
+            cols = slice(v0, v0 + width)
+            codes = keep.tile([P, width], U32, name="out_codes%d" % v0, align_bytes=64)
+            nc.vector.quantize_mx(out=codes[:].bitcast(FP8X4), scales=out_bytes[:, cols], in_=res_bf)
+            nc.sync.dma_start(out=out_words[:, cols], in_=codes[:].bitcast(I32))
+
+        gather(0, 0)
+        z_bf = activate(0, READ, gather(0, 1))
+        res = {}
+        half = READ // 2
+        for c in range(last):
+            gather(c + 1, 0)
+            banks = multiply(c * READ, READ, z_bf)
+            got = gather(c + 1, 1)
+            if c + 1 < last:
+                z_bf = activate((c + 1) * READ, READ, got)
+            else:
+                ends = [last * READ, last * READ + half]
+                z_end = [activate(v0, half, got[:, :, v0 % READ : v0 % READ + half]) for v0 in ends]
+                banks_end = [multiply(v0, half, z) for v0, z in zip(ends, z_end)]
+            res[c] = unload(c * READ, READ, banks, nc.scalar.copy)
+
+        early_bf = keep.tile([P, 2, PACK * READ], BF16, name="early_bf", tag="page3", align_bytes=64)
+        for c in range(2):
+            nc.vector.tensor_copy(out=woven(early_bf[:, c, :]), in_=planes(res[c][:]))
+        hand_on(0, 2 * READ, early_bf[:].rearrange("p c w -> p (c w)"))
+        third_bf = keep.tile([P, PACK * READ], BF16, name="third_bf", align_bytes=64)
+        nc.vector.tensor_copy(out=woven(third_bf[:]), in_=planes(res[2][:]))
+        end_bf = keep.tile([P, PACK * READ], BF16, name="end_bf", align_bytes=64)
+        for e in range(2):
+            nc.scalar.copy(
+                out=end_bf[:, e * PACK * half : (e + 1) * PACK * half].rearrange("p (c t) -> p c t", t=PACK),
+                in_=banks_end[e][0][:].rearrange("p t c -> p c t"),
+            )
+        unload(ends[0], half, banks_end[0], nc.vector.tensor_copy)
+        unload(ends[1], half, banks_end[1], nc.scalar.copy)
+        hand_on(2 * READ, READ, third_bf[:])
+        hand_on(last * READ, READ, end_bf[:])
+        for q in range(QUADS):
+            eng = nc.sync if q % 2 == 0 else nc.scalar
+            eng.dma_start(
+                out=out_2[0, 4 * q : 4 * q + 4, :].bitcast(I32), in_=out_bytes[32 * q : 32 * q + 4, :].bitcast(I32)
+            )

@@ -38,38 +38,39 @@ def tile_picked_pageread_silu_po_kernel(
         x_bytes = keep.tile([P, T], U8, name="x_bytes", align_bytes=64)
         w2_raw = keep.tile([P, 2 * N], U8, name="w2_raw", align_bytes=64)
         w2_raw_bytes = keep.tile([P, N], U8, name="w2_raw_bytes", align_bytes=64)
-        w1_raw = keep.tile([P, PACK, H], F32, name="w1_raw", align_bytes=64)
+        w1_raw = [keep.tile([P, PACK, H // 2], F32, name="w1_raw%d" % a, align_bytes=64) for a in range(2)]
         page = [keep.tile([P, U], F32, name="page%d" % t, align_bytes=64) for t in range(PACK)]
 
         nc.vector.memset(x_bytes[:].bitcast(I32), 0)
         nc.vector.memset(w2_raw_bytes[:].bitcast(I32), 0)
 
-        nc.sync.dma_start(out=w2_raw[:].bitcast(I32), in_=w2_words[0].bitcast(I32))
         nc.sync.dma_start(offs_sb[:], offs)
-        nc.sync.dma_start(out=w1_raw[:], in_=w1.rearrange("(p j) c -> p j c", j=PACK))
-        for q in range(QUADS):
-            nc.sync.dma_start(
-                out=x_bytes[32 * q : 32 * q + 4, :].bitcast(I32), in_=x_scales[0, 4 * q : 4 * q + 4, :].bitcast(I32)
-            )
+        w1_rows = w1.rearrange("(p j) c -> p j c", j=PACK)
+        nc.sync.dma_start(out=w1_raw[0][:], in_=w1_rows[:, :, 0 : H // 2])
+        for r in range(4):
+            nc.sync.dma_start(out=x_bytes[r:P:32, :].bitcast(I32), in_=x_scales[0, r:16:4, :].bitcast(I32))
+        nc.sync.dma_start(out=w1_raw[1][:], in_=w1_rows[:, :, H // 2 : H])
         nc.sync.dma_start(out=x_codes[:].bitcast(I32), in_=x_words[0].rearrange("p c r -> p (c r)").bitcast(I32))
         nc.sync.dma_start(slot_sb[:], slot)
         mem_rows = mem.rearrange("(p t) u -> p t u", t=PACK)
         for t in range(2):
             nc.sync.dma_start(out=page[t][:], in_=mem_rows[:, t, :])
-        for q in range(QUADS):
-            nc.sync.dma_start(
-                out=w2_raw_bytes[32 * q : 32 * q + 4, :].bitcast(I32),
-                in_=w2_scales[0, 4 * q : 4 * q + 4, :].bitcast(I32),
-            )
+        nc.sync.dma_start(out=w2_raw[:].bitcast(I32), in_=w2_words[0].bitcast(I32))
+        for r in range(4):
+            nc.sync.dma_start(out=w2_raw_bytes[r:P:32, :].bitcast(I32), in_=w2_scales[0, r:16:4, :].bitcast(I32))
         for t in range(2, PACK):
             nc.sync.dma_start(out=page[t][:], in_=mem_rows[:, t, :])
         nc.sync.dma_start(rd_sb[:], rd)
 
         w2_codes = keep.tile([P, 2 * N], U8, name="w2_codes", align_bytes=64)
         w2_bytes = keep.tile([P, N], U8, name="w2_bytes", align_bytes=64)
-        nc.vector.tensor_copy(
-            out=w2_codes[:].rearrange("p (t m b) -> p m t b", t=PACK, b=2),
-            in_=w2_raw[:].rearrange("p (m t b) -> p m t b", t=PACK, b=2),
+        nc.gpsimd.tensor_copy(
+            out=w2_codes[:].rearrange("p (t m b) -> p t m b", t=PACK, b=2),
+            in_=w2_raw[:].rearrange("p (m t b) -> p t m b", t=PACK, b=2),
+        )
+        nc.gpsimd.tensor_copy(
+            out=w2_bytes[:].rearrange("p (t m) -> p t m", t=PACK),
+            in_=w2_raw_bytes[:].rearrange("p (m t) -> p t m", t=PACK),
         )
 
         halves = S // PICK
@@ -82,9 +83,8 @@ def tile_picked_pageread_silu_po_kernel(
         w1_bf = keep.tile([P, PACK * H], BF16, name="w1_bf", align_bytes=64)
         w1_dst = w1_bf[:].rearrange("p (t m j) -> p m j t", t=PACK, j=PACK)
         half_m = P // 2
-        w1_src = w1_raw[:].rearrange("p j (m t) -> p m j t", t=PACK)
-        nc.scalar.copy(out=w1_dst[:, 0:half_m], in_=w1_src[:, 0:half_m])
-        nc.vector.tensor_copy(out=w1_dst[:, half_m:P], in_=w1_src[:, half_m:P])
+        nc.scalar.copy(out=w1_dst[:, 0:half_m], in_=w1_raw[0][:].rearrange("p j (m t) -> p m j t", t=PACK))
+        nc.vector.tensor_copy(out=w1_dst[:, half_m:P], in_=w1_raw[1][:].rearrange("p j (m t) -> p m j t", t=PACK))
         for h in range(halves):
             nc.vector.tensor_copy(out=picked_bytes[h][:], in_=x_bytes[:].indirect(entries(offs_sb, h * PICK, PICK)))
 
@@ -121,10 +121,6 @@ def tile_picked_pageread_silu_po_kernel(
         scatter(0, PICK, PICK)
         scatter(2, 0, S)
         scatter(3, 0, S)
-        nc.vector.tensor_copy(
-            out=w2_bytes[:].rearrange("p (t m) -> p m t", t=PACK),
-            in_=w2_raw_bytes[:].rearrange("p (m t) -> p m t", t=PACK),
-        )
 
         chunks = V // READ
         last = chunks - 1
@@ -222,8 +218,6 @@ def tile_picked_pageread_silu_po_kernel(
         unload(ends[1], half, banks_end[1], nc.scalar.copy)
         hand_on(2 * READ, READ, third_bf[:])
         hand_on(last * READ, READ, end_bf[:])
-        for q in range(QUADS):
-            eng = nc.sync if q % 2 == 0 else nc.scalar
-            eng.dma_start(
-                out=out_2[0, 4 * q : 4 * q + 4, :].bitcast(I32), in_=out_bytes[32 * q : 32 * q + 4, :].bitcast(I32)
-            )
+        for r in range(4):
+            eng = nc.sync if r % 2 == 0 else nc.scalar
+            eng.dma_start(out=out_2[0, r:16:4, :].bitcast(I32), in_=out_bytes[r:P:32, :].bitcast(I32))

@@ -172,17 +172,17 @@ def tile_picked_pageread_silu_po_kernel(
                 banks.append(acc)
             return banks
 
-        def unload(v0, width, banks, copy):
-            res = keep.tile([P, PACK, width], F32, name="res%d" % v0, align_bytes=64)
-            per_bank = PACK // len(banks)
-            for u in range(len(banks)):
-                copy(out=res[:, per_bank * u : per_bank * (u + 1), :], in_=banks[u][:])
-            nc.sync.dma_start(out=out_rows[:, :, v0 : v0 + width], in_=res[:])
+        def unload(v0, banks, copies):
+            res = keep.tile([P, PACK, READ], F32, name="res%d" % v0, align_bytes=64)
+            for u in range(2):
+                rows = slice(2 * u, 2 * u + 2)
+                copies[u](out=res[:, rows, :], in_=banks[u][:])
+                nc.sync.dma_start(out=out_rows[:, rows, v0 : v0 + READ], in_=res[:, rows, :])
             return res
 
-        def hand_on(v0, width, res_bf):
+        def hand_on(v0, width, res_bf, tag):
             cols = slice(v0, v0 + width)
-            codes = keep.tile([P, width], U32, name="out_codes%d" % v0, align_bytes=64)
+            codes = keep.tile([P, width], U32, name="out_codes%d" % v0, tag=tag, align_bytes=64)
             nc.vector.quantize_mx(out=codes[:].bitcast(FP8X4), scales=out_bytes[:, cols], in_=res_bf)
             nc.sync.dma_start(out=out_words[:, cols], in_=codes[:].bitcast(I32))
 
@@ -200,24 +200,39 @@ def tile_picked_pageread_silu_po_kernel(
                 ends = [last * READ, last * READ + half]
                 z_end = [activate(v0, half, got[:, :, v0 % READ : v0 % READ + half]) for v0 in ends]
                 banks_end = [multiply(v0, half, z) for v0, z in zip(ends, z_end)]
-            res[c] = unload(c * READ, READ, banks, nc.scalar.copy)
+            first_copy = nc.vector.tensor_copy if c + 1 == last else nc.scalar.copy
+            res[c] = unload(c * READ, banks, (first_copy, nc.scalar.copy))
+            if c == 0:
+                first_bf = keep.tile([P, READ, PACK], BF16, name="first_bf", align_bytes=64)
+                nc.gpsimd.tensor_scalar(
+                    out=first_bf[:],
+                    in0=res[0][:].rearrange("p t c -> p c t"),
+                    scalar1=1.0,
+                    scalar2=-0.0,
+                    op0=mybir.AluOpType.mult,
+                    op1=mybir.AluOpType.add,
+                )
+            if c == 1:
+                hand_on(0, READ, first_bf[:].rearrange("p c t -> p (c t)"), "page3")
 
-        early_bf = keep.tile([P, 2, PACK * READ], BF16, name="early_bf", tag="page3", align_bytes=64)
-        for c in range(2):
-            nc.vector.tensor_copy(out=woven(early_bf[:, c, :]), in_=planes(res[c][:]))
-        hand_on(0, 2 * READ, early_bf[:].rearrange("p c w -> p (c w)"))
+        second_bf = keep.tile([P, PACK * READ], BF16, name="second_bf", tag="z_bf%d" % ends[0], align_bytes=64)
+        nc.vector.tensor_copy(out=woven(second_bf[:]), in_=planes(res[1][:]))
+        hand_on(READ, READ, second_bf[:], "second_codes")
         third_bf = keep.tile([P, PACK * READ], BF16, name="third_bf", align_bytes=64)
         nc.vector.tensor_copy(out=woven(third_bf[:]), in_=planes(res[2][:]))
-        end_bf = keep.tile([P, PACK * READ], BF16, name="end_bf", align_bytes=64)
+
+        res_end = [keep.tile([P, PACK, half], F32, name="res_end%d" % e, align_bytes=64) for e in range(2)]
         for e in range(2):
-            nc.scalar.copy(
-                out=end_bf[:, e * PACK * half : (e + 1) * PACK * half].rearrange("p (c t) -> p c t", t=PACK),
-                in_=banks_end[e][0][:].rearrange("p t c -> p c t"),
-            )
-        unload(ends[0], half, banks_end[0], nc.vector.tensor_copy)
-        unload(ends[1], half, banks_end[1], nc.scalar.copy)
-        hand_on(2 * READ, READ, third_bf[:])
-        hand_on(last * READ, READ, end_bf[:])
+            nc.scalar.copy(out=res_end[e][:], in_=banks_end[e][0][:])
+            nc.sync.dma_start(out=out_rows[:, :, ends[e] : ends[e] + half], in_=res_end[e][:])
+        end_bf = keep.tile([P, PACK * READ], BF16, name="end_bf", align_bytes=64)
+        nc.vector.tensor_copy(out=woven(end_bf[:, : PACK * half]), in_=planes(res_end[0][:]))
+        nc.scalar.copy(
+            out=end_bf[:, PACK * half :].rearrange("p (c t) -> p c t", t=PACK),
+            in_=banks_end[1][0][:].rearrange("p t c -> p c t"),
+        )
+        hand_on(2 * READ, READ, third_bf[:], "third_codes")
+        hand_on(last * READ, READ, end_bf[:], "end_codes")
         for r in range(4):
             eng = nc.sync if r % 2 == 0 else nc.scalar
             eng.dma_start(out=out_2[0, r:16:4, :].bitcast(I32), in_=out_bytes[r:P:32, :].bitcast(I32))

@@ -98,7 +98,7 @@ def tile_picked_pageread_silu_po_kernel(
         y = [keep.tile([P, S], F32, name="y%d" % t, align_bytes=64) for t in range(PACK)]
         for h in range(halves):
             for t in range(PACK):
-                acc = psum.tile([P, PICK], F32, name="acc1", bufs=4)
+                acc = psum.tile([P, PICK], F32, name="acc", bufs=8)
                 cols = slice(t * P, (t + 1) * P)
                 nc.tensor.matmul_mx(
                     out=acc[:],
@@ -116,14 +116,24 @@ def tile_picked_pageread_silu_po_kernel(
                 out=page[t][:].indirect(entries(slot_sb, start, count)), in_=y[t][:, start : start + count]
             )
 
+        active = [keep.tile([P, U], F32, name="active%d" % t, align_bytes=64) for t in range(PACK)]
+
+        def activate_page(t):
+            nc.scalar.activation(out=active[t][:], in_=page[t][:], func=SILU)
+
         scatter(0, 0, PICK)
         scatter(1, 0, S)
+        activate_page(1)
         scatter(0, PICK, PICK)
+        activate_page(0)
         scatter(2, 0, S)
+        activate_page(2)
         scatter(3, 0, S)
+        activate_page(3)
 
         chunks = V // READ
         last = chunks - 1
+        half = READ // 2
         out_rows = out_0.rearrange("(p t) v -> p t v", t=PACK)
         out_words = out_1[0].rearrange("p c r -> p (c r)").bitcast(I32)
         out_bytes = keep.tile([P, V], U8, name="out_bytes", align_bytes=64)
@@ -134,105 +144,129 @@ def tile_picked_pageread_silu_po_kernel(
         def planes(ap):
             return ap.rearrange("p t (c i) -> p c t i", i=4)
 
-        got_all = keep.tile([P, 2 * PACK - 1, READ], F32, name="got_all", align_bytes=64)
+        def side_by_side(ap):
+            return ap.rearrange("p (c t) -> p c t", t=PACK)
 
-        def gather(c, part):
-            base = PACK - 1 if c % 2 == 0 else 0
+        got_all = keep.tile([P, (2 * PACK - 1) * READ], F32, name="got_all", align_bytes=64)
+        first_row = ((PACK - 1) * READ, 0, (PACK - 1) * READ, half)
+
+        def rows(c):
+            return got_all[:, first_row[c] : first_row[c] + PACK * READ].rearrange("p (t c) -> p t c", t=PACK)
+
+        def gather(c, first, count):
             order = (1, 2, 3, 0) if c % 2 == 0 else (0, 1, 2, 3)
-            for t in order[:-1] if part == 0 else order[-1:]:
-                nc.vector.tensor_copy(
-                    out=got_all[:, base + t, :], in_=page[t][:].indirect(entries(rd_sb, c * READ, READ))
-                )
-            return got_all[:, base : base + PACK, :]
+            window = page if c == 0 else active
+            for t in order[first : first + count]:
+                nc.vector.tensor_copy(out=rows(c)[:, t, :], in_=window[t][:].indirect(entries(rd_sb, c * READ, READ)))
 
-        def activate(v0, width, got):
+        def weave(v0, width):
+            got = rows(v0 // READ)[:, :, v0 % READ : v0 % READ + width]
             z_bf = keep.tile([P, PACK * width], BF16, name="z_bf%d" % v0, align_bytes=64)
-            nc.scalar.activation(out=woven(z_bf[:]), in_=planes(got), func=SILU)
-            return z_bf
-
-        def multiply(v0, width, z_bf):
-            z_codes = keep.tile([P, width], U32, name="z_codes%d" % v0, align_bytes=64)
-            z_bytes = keep.tile([P, width], U8, name="z_bytes%d" % v0, align_bytes=64)
-            nc.vector.quantize_mx(out=z_codes[:].bitcast(FP8X4), scales=z_bytes[:], in_=z_bf[:])
-            per_bank = 512 // width
-            banks = []
-            for u in range(PACK // per_bank):
-                acc = psum.tile([P, per_bank, width], F32, name="acc2", bufs=4)
-                for e in range(per_bank):
-                    t = per_bank * u + e
-                    nc.tensor.matmul_mx(
-                        out=acc[:, e, :],
-                        lhsT=w2_codes[:, 2 * t * P : 2 * (t + 1) * P].bitcast(FP4X4),
-                        lhsT_scale=w2_bytes[:, t * P : (t + 1) * P],
-                        rhs=z_codes[:].bitcast(FP8X4),
-                        rhs_scale=z_bytes[:],
-                        start=True,
-                        stop=True,
-                    )
-                banks.append(acc)
-            return banks
-
-        def unload(v0, banks, copies):
-            res = keep.tile([P, PACK, READ], F32, name="res%d" % v0, align_bytes=64)
-            for u in range(2):
-                rows = slice(2 * u, 2 * u + 2)
-                copies[u](out=res[:, rows, :], in_=banks[u][:])
-                nc.sync.dma_start(out=out_rows[:, rows, v0 : v0 + READ], in_=res[:, rows, :])
-            return res
-
-        def hand_on(v0, width, res_bf, tag):
-            cols = slice(v0, v0 + width)
-            codes = keep.tile([P, width], U32, name="out_codes%d" % v0, tag=tag, align_bytes=64)
-            nc.vector.quantize_mx(out=codes[:].bitcast(FP8X4), scales=out_bytes[:, cols], in_=res_bf)
-            nc.sync.dma_start(out=out_words[:, cols], in_=codes[:].bitcast(I32))
-
-        gather(0, 0)
-        z_bf = activate(0, READ, gather(0, 1))
-        res = {}
-        half = READ // 2
-        for c in range(last):
-            gather(c + 1, 0)
-            banks = multiply(c * READ, READ, z_bf)
-            got = gather(c + 1, 1)
-            if c + 1 < last:
-                z_bf = activate((c + 1) * READ, READ, got)
-            else:
-                ends = [last * READ, last * READ + half]
-                z_end = [activate(v0, half, got[:, :, v0 % READ : v0 % READ + half]) for v0 in ends]
-                banks_end = [multiply(v0, half, z) for v0, z in zip(ends, z_end)]
-            first_copy = nc.vector.tensor_copy if c + 1 == last else nc.scalar.copy
-            res[c] = unload(c * READ, banks, (first_copy, nc.scalar.copy))
-            if c == 0:
-                first_bf = keep.tile([P, READ, PACK], BF16, name="first_bf", align_bytes=64)
+            if v0 == 0:
+                nc.scalar.activation(out=woven(z_bf[:]), in_=planes(got), func=SILU)
+            elif v0 < last * READ:
                 nc.gpsimd.tensor_scalar(
-                    out=first_bf[:],
-                    in0=res[0][:].rearrange("p t c -> p c t"),
+                    out=side_by_side(z_bf[:]),
+                    in0=got.rearrange("p t c -> p c t"),
                     scalar1=1.0,
                     scalar2=-0.0,
                     op0=mybir.AluOpType.mult,
                     op1=mybir.AluOpType.add,
                 )
-            if c == 1:
-                hand_on(0, READ, first_bf[:].rearrange("p c t -> p (c t)"), "page3")
+            else:
+                nc.vector.tensor_copy(out=woven(z_bf[:]), in_=planes(got))
+            return z_bf
 
-        second_bf = keep.tile([P, PACK * READ], BF16, name="second_bf", tag="z_bf%d" % ends[0], align_bytes=64)
-        nc.vector.tensor_copy(out=woven(second_bf[:]), in_=planes(res[1][:]))
-        hand_on(READ, READ, second_bf[:], "second_codes")
-        third_bf = keep.tile([P, PACK * READ], BF16, name="third_bf", align_bytes=64)
-        nc.vector.tensor_copy(out=woven(third_bf[:]), in_=planes(res[2][:]))
+        def quantise(v0, width, z_bf):
+            z_codes = keep.tile([P, width], U32, name="z_codes%d" % v0, align_bytes=64)
+            z_bytes = keep.tile([P, width], U8, name="z_bytes%d" % v0, align_bytes=64)
+            nc.vector.quantize_mx(out=z_codes[:].bitcast(FP8X4), scales=z_bytes[:], in_=z_bf[:])
+            return z_codes, z_bytes
 
-        res_end = [keep.tile([P, PACK, half], F32, name="res_end%d" % e, align_bytes=64) for e in range(2)]
-        for e in range(2):
-            nc.scalar.copy(out=res_end[e][:], in_=banks_end[e][0][:])
-            nc.sync.dma_start(out=out_rows[:, :, ends[e] : ends[e] + half], in_=res_end[e][:])
-        end_bf = keep.tile([P, PACK * READ], BF16, name="end_bf", align_bytes=64)
-        nc.vector.tensor_copy(out=woven(end_bf[:, : PACK * half]), in_=planes(res_end[0][:]))
-        nc.scalar.copy(
-            out=end_bf[:, PACK * half :].rearrange("p (c t) -> p c t", t=PACK),
-            in_=banks_end[1][0][:].rearrange("p t c -> p c t"),
-        )
-        hand_on(2 * READ, READ, third_bf[:], "third_codes")
-        hand_on(last * READ, READ, end_bf[:], "end_codes")
+        def multiply(z_codes, z_bytes, start, first=0, count=PACK):
+            acc = psum.tile([P, count, half], F32, name="acc", bufs=8)
+            for e in range(count):
+                t = first + e
+                nc.tensor.matmul_mx(
+                    out=acc[:, e, :],
+                    lhsT=w2_codes[:, 2 * t * P : 2 * (t + 1) * P].bitcast(FP4X4),
+                    lhsT_scale=w2_bytes[:, t * P : (t + 1) * P],
+                    rhs=z_codes[:, start : start + half].bitcast(FP8X4),
+                    rhs_scale=z_bytes[:, start : start + half],
+                    start=True,
+                    stop=True,
+                )
+            return acc
+
+        out_bf = keep.tile([P, PACK * V], BF16, name="out_bf", align_bytes=64)
+
+        def hand_on(v0, width, codes):
+            start = v0 % (2 * READ)
+            nc.vector.quantize_mx(
+                out=codes[:, start : start + width].bitcast(FP8X4),
+                scales=out_bytes[:, v0 : v0 + width],
+                in_=out_bf[:, PACK * v0 : PACK * (v0 + width)],
+            )
+
+        def round_out(v0, bank):
+            nc.scalar.copy(
+                out=side_by_side(out_bf[:, PACK * v0 : PACK * (v0 + half)]), in_=bank[:].rearrange("p t c -> p c t")
+            )
+
+        gather(0, 0, PACK)
+        z_bf = weave(0, READ)
+        for c in range(last - 1):
+            gather(c + 1, 0, PACK - 1)
+            operand = quantise(c * READ, READ, z_bf)
+            gather(c + 1, PACK - 1, 1)
+            if c + 2 < last:
+                z_bf = weave((c + 1) * READ, READ)
+            else:
+                z_halves = [weave((c + 1) * READ + h * half, half) for h in range(2)]
+            banks = [multiply(*operand, h * half) for h in range(2)]
+            res = keep.tile([P, PACK, READ], F32, name="res%d" % c, align_bytes=64)
+            for h in range(2):
+                nc.scalar.copy(out=res[:, :, h * half : (h + 1) * half], in_=banks[h][:])
+            nc.sync.dma_start(out=out_rows[:, :, c * READ : (c + 1) * READ], in_=res[:])
+            for h in range(2):
+                round_out(c * READ + h * half, banks[h])
+
+        gather(last, 0, PACK - 2)
+        for h in range(2):
+            v0 = (last - 1) * READ + h * half
+            operand = quantise(v0, half, z_halves[h])
+            gather(last, PACK - 2 + h, 1)
+            bank = multiply(*operand, 0)
+            res = keep.tile([P, PACK, half], F32, name="res_late%d" % h, align_bytes=64)
+            nc.scalar.copy(out=res[:], in_=bank[:])
+            nc.sync.dma_start(out=out_rows[:, :, v0 : v0 + half], in_=res[:])
+            round_out(v0, bank)
+
+        ends = [last * READ, last * READ + half]
+        z_end = [weave(v0, half) for v0 in ends]
+        operands = [quantise(ends[h], half, z_end[h]) for h in range(2)]
+        banks_end = [[multiply(*operand, 0, first, 2) for first in (0, 2)] for operand in operands]
+        early_codes = keep.tile([P, 2 * READ], U32, name="early_codes", tag="got_all", align_bytes=64)
+        hand_on(0, 2 * READ, early_codes)
+        nc.sync.dma_start(out=out_words[:, : 2 * READ], in_=early_codes[:].bitcast(I32))
+        late_codes = keep.tile([P, 2 * READ], U32, name="late_codes", align_bytes=64)
+        hand_on(2 * READ, READ, late_codes)
+
+        res_end = keep.tile([P, PACK, READ], F32, name="res_end", align_bytes=64)
+        for h in range(2):
+            cols = slice(h * half, (h + 1) * half)
+            nc.scalar.copy(out=res_end[:, 0:2, cols], in_=banks_end[h][0][:])
+            second_copy = nc.scalar.copy if h == 0 else nc.vector.tensor_copy
+            second_copy(out=res_end[:, 2:4, cols], in_=banks_end[h][1][:])
+        nc.sync.dma_start(out=out_rows[:, :, ends[0] :], in_=res_end[:])
+        for h in range(2):
+            nc.vector.tensor_copy(
+                out=woven(out_bf[:, PACK * ends[h] : PACK * (ends[h] + half)]),
+                in_=planes(res_end[:, :, h * half : (h + 1) * half]),
+            )
+        for v0 in ends:
+            hand_on(v0, half, late_codes)
+        nc.sync.dma_start(out=out_words[:, 2 * READ :], in_=late_codes[:].bitcast(I32))
         for r in range(4):
             eng = nc.sync if r % 2 == 0 else nc.scalar
             eng.dma_start(out=out_2[0, r:16:4, :].bitcast(I32), in_=out_bytes[r:P:32, :].bitcast(I32))

@@ -21,6 +21,8 @@ QUADS = 4
 PER_COL = 16
 PICK = 256
 READ = 256
+LEAD = 128
+SHARE = 192
 
 
 def tile_picked_pageread_silu_po_kernel(
@@ -44,9 +46,9 @@ def tile_picked_pageread_silu_po_kernel(
         nc.vector.memset(x_bytes[:].bitcast(I32), 0)
         nc.vector.memset(w2_raw_bytes[:].bitcast(I32), 0)
 
-        nc.sync.dma_start(offs_sb[:], offs)
         w1_rows = w1.rearrange("(p j) c -> p j c", j=PACK)
         nc.sync.dma_start(out=w1_raw[0][:], in_=w1_rows[:, :, 0 : H // 2])
+        nc.sync.dma_start(offs_sb[:], offs)
         for r in range(4):
             nc.sync.dma_start(out=x_bytes[r:P:32, :].bitcast(I32), in_=x_scales[0, r:16:4, :].bitcast(I32))
         nc.sync.dma_start(out=w1_raw[1][:], in_=w1_rows[:, :, H // 2 : H])
@@ -96,20 +98,29 @@ def tile_picked_pageread_silu_po_kernel(
             nc.vector.tensor_copy(out=picked_codes[h][:], in_=x_codes[:].indirect(entries(offs_sb, h * PICK, PICK)))
 
         y = [keep.tile([P, S], F32, name="y%d" % t, align_bytes=64) for t in range(PACK)]
+
+        def project(t, start, count):
+            h, cols, picked = start // PICK, slice(t * P, (t + 1) * P), slice(start % PICK, start % PICK + count)
+            acc = psum.tile([P, count], F32, name="acc", bufs=8)
+            nc.tensor.matmul_mx(
+                out=acc[:],
+                lhsT=w1_codes[:, cols].bitcast(FP8X4),
+                lhsT_scale=w1_bytes[:, cols],
+                rhs=picked_codes[h][:, picked].bitcast(FP8X4),
+                rhs_scale=picked_bytes[h][:, picked],
+                start=True,
+                stop=True,
+            )
+            nc.scalar.copy(out=y[t][:, start : start + count], in_=acc[:])
+
+        project(0, 0, LEAD)
         for h in range(halves):
-            for t in range(PACK):
-                acc = psum.tile([P, PICK], F32, name="acc", bufs=8)
-                cols = slice(t * P, (t + 1) * P)
-                nc.tensor.matmul_mx(
-                    out=acc[:],
-                    lhsT=w1_codes[:, cols].bitcast(FP8X4),
-                    lhsT_scale=w1_bytes[:, cols],
-                    rhs=picked_codes[h][:].bitcast(FP8X4),
-                    rhs_scale=picked_bytes[h][:],
-                    start=True,
-                    stop=True,
-                )
-                nc.scalar.copy(out=y[t][:, h * PICK : (h + 1) * PICK], in_=acc[:])
+            project(1, h * PICK, PICK)
+        project(0, LEAD, PICK - LEAD)
+        project(0, PICK, PICK)
+        for t in range(2, PACK):
+            for h in range(halves):
+                project(t, h * PICK, PICK)
 
         def scatter(t, start, count):
             nc.vector.tensor_copy(
@@ -121,10 +132,10 @@ def tile_picked_pageread_silu_po_kernel(
         def activate_page(t):
             nc.scalar.activation(out=active[t][:], in_=page[t][:], func=SILU)
 
-        scatter(0, 0, PICK)
+        scatter(0, 0, LEAD)
         scatter(1, 0, S)
         activate_page(1)
-        scatter(0, PICK, PICK)
+        scatter(0, LEAD, S - LEAD)
         activate_page(0)
         scatter(2, 0, S)
         activate_page(2)
@@ -147,11 +158,11 @@ def tile_picked_pageread_silu_po_kernel(
         def side_by_side(ap):
             return ap.rearrange("p (c t) -> p c t", t=PACK)
 
-        got_all = keep.tile([P, (2 * PACK - 1) * READ], F32, name="got_all", align_bytes=64)
-        first_row = ((PACK - 1) * READ, 0, (PACK - 1) * READ, half)
+        got_all = keep.tile([P, 2 * PACK - 1, READ], F32, name="got_all", align_bytes=64)
 
         def rows(c):
-            return got_all[:, first_row[c] : first_row[c] + PACK * READ].rearrange("p (t c) -> p t c", t=PACK)
+            base = PACK - 1 if c % 2 == 0 else 0
+            return got_all[:, base : base + PACK, :]
 
         def gather(c, first, count):
             order = (1, 2, 3, 0) if c % 2 == 0 else (0, 1, 2, 3)
@@ -159,22 +170,20 @@ def tile_picked_pageread_silu_po_kernel(
             for t in order[first : first + count]:
                 nc.vector.tensor_copy(out=rows(c)[:, t, :], in_=window[t][:].indirect(entries(rd_sb, c * READ, READ)))
 
-        def weave(v0, width):
-            got = rows(v0 // READ)[:, :, v0 % READ : v0 % READ + width]
-            z_bf = keep.tile([P, PACK * width], BF16, name="z_bf%d" % v0, align_bytes=64)
-            if v0 == 0:
-                nc.scalar.activation(out=woven(z_bf[:]), in_=planes(got), func=SILU)
-            elif v0 < last * READ:
+        def weave(c):
+            z_bf = keep.tile([P, PACK * READ], BF16, name="z_bf%d" % c, align_bytes=64)
+            if c == 0:
+                nc.scalar.activation(out=woven(z_bf[:]), in_=planes(rows(c)), func=SILU)
+            else:
+                nc.scalar.copy(out=woven(z_bf[:, PACK * SHARE :]), in_=planes(rows(c)[:, :, SHARE:]))
                 nc.gpsimd.tensor_scalar(
-                    out=side_by_side(z_bf[:]),
-                    in0=got.rearrange("p t c -> p c t"),
+                    out=side_by_side(z_bf[:, : PACK * SHARE]),
+                    in0=rows(c)[:, :, :SHARE].rearrange("p t c -> p c t"),
                     scalar1=1.0,
                     scalar2=-0.0,
                     op0=mybir.AluOpType.mult,
                     op1=mybir.AluOpType.add,
                 )
-            else:
-                nc.vector.tensor_copy(out=woven(z_bf[:]), in_=planes(got))
             return z_bf
 
         def quantise(v0, width, z_bf):
@@ -183,16 +192,16 @@ def tile_picked_pageread_silu_po_kernel(
             nc.vector.quantize_mx(out=z_codes[:].bitcast(FP8X4), scales=z_bytes[:], in_=z_bf[:])
             return z_codes, z_bytes
 
-        def multiply(z_codes, z_bytes, start, first=0, count=PACK):
-            acc = psum.tile([P, count, half], F32, name="acc", bufs=8)
+        def multiply(z_codes, z_bytes, start, width, first, count):
+            acc = psum.tile([P, count, width], F32, name="acc", bufs=8)
             for e in range(count):
                 t = first + e
                 nc.tensor.matmul_mx(
                     out=acc[:, e, :],
                     lhsT=w2_codes[:, 2 * t * P : 2 * (t + 1) * P].bitcast(FP4X4),
                     lhsT_scale=w2_bytes[:, t * P : (t + 1) * P],
-                    rhs=z_codes[:, start : start + half].bitcast(FP8X4),
-                    rhs_scale=z_bytes[:, start : start + half],
+                    rhs=z_codes[:, start : start + width].bitcast(FP8X4),
+                    rhs_scale=z_bytes[:, start : start + width],
                     start=True,
                     stop=True,
                 )
@@ -213,57 +222,50 @@ def tile_picked_pageread_silu_po_kernel(
                 out=side_by_side(out_bf[:, PACK * v0 : PACK * (v0 + half)]), in_=bank[:].rearrange("p t c -> p c t")
             )
 
+        def round_from_sbuf(v0, width, res):
+            nc.vector.tensor_copy(out=woven(out_bf[:, PACK * v0 : PACK * (v0 + width)]), in_=planes(res))
+
         gather(0, 0, PACK)
-        z_bf = weave(0, READ)
-        for c in range(last - 1):
+        z_bf = weave(0)
+        for c in range(last):
             gather(c + 1, 0, PACK - 1)
             operand = quantise(c * READ, READ, z_bf)
             gather(c + 1, PACK - 1, 1)
-            if c + 2 < last:
-                z_bf = weave((c + 1) * READ, READ)
-            else:
-                z_halves = [weave((c + 1) * READ + h * half, half) for h in range(2)]
-            banks = [multiply(*operand, h * half) for h in range(2)]
+            if c + 1 < last:
+                z_bf = weave(c + 1)
             res = keep.tile([P, PACK, READ], F32, name="res%d" % c, align_bytes=64)
-            for h in range(2):
-                nc.scalar.copy(out=res[:, :, h * half : (h + 1) * half], in_=banks[h][:])
-            nc.sync.dma_start(out=out_rows[:, :, c * READ : (c + 1) * READ], in_=res[:])
-            for h in range(2):
-                round_out(c * READ + h * half, banks[h])
-
-        gather(last, 0, PACK - 2)
-        for h in range(2):
-            v0 = (last - 1) * READ + h * half
-            operand = quantise(v0, half, z_halves[h])
-            gather(last, PACK - 2 + h, 1)
-            bank = multiply(*operand, 0)
-            res = keep.tile([P, PACK, half], F32, name="res_late%d" % h, align_bytes=64)
-            nc.scalar.copy(out=res[:], in_=bank[:])
-            nc.sync.dma_start(out=out_rows[:, :, v0 : v0 + half], in_=res[:])
-            round_out(v0, bank)
+            if c + 1 < last:
+                banks = [multiply(*operand, h * half, half, 0, PACK) for h in range(2)]
+                for h in range(2):
+                    nc.scalar.copy(out=res[:, :, h * half : (h + 1) * half], in_=banks[h][:])
+                nc.sync.dma_start(out=out_rows[:, :, c * READ : (c + 1) * READ], in_=res[:])
+                for h in range(2):
+                    round_out(c * READ + h * half, banks[h])
+            else:
+                for first in (0, 2):
+                    pair = slice(first, first + 2)
+                    nc.scalar.copy(out=res[:, pair, :], in_=multiply(*operand, 0, READ, first, 2)[:])
+                    nc.scalar.dma_start(out=out_rows[:, pair, c * READ : (c + 1) * READ], in_=res[:, pair, :])
 
         ends = [last * READ, last * READ + half]
-        z_end = [weave(v0, half) for v0 in ends]
+        z_end = [keep.tile([P, PACK * half], BF16, name="z_end%d" % h, align_bytes=64) for h in range(2)]
+        for h in range(2):
+            nc.vector.tensor_copy(out=woven(z_end[h][:]), in_=planes(rows(last)[:, :, h * half : (h + 1) * half]))
         operands = [quantise(ends[h], half, z_end[h]) for h in range(2)]
-        banks_end = [[multiply(*operand, 0, first, 2) for first in (0, 2)] for operand in operands]
+        banks_end = [multiply(*operand, 0, half, 0, PACK) for operand in operands]
         early_codes = keep.tile([P, 2 * READ], U32, name="early_codes", tag="got_all", align_bytes=64)
         hand_on(0, 2 * READ, early_codes)
         nc.sync.dma_start(out=out_words[:, : 2 * READ], in_=early_codes[:].bitcast(I32))
-        late_codes = keep.tile([P, 2 * READ], U32, name="late_codes", align_bytes=64)
-        hand_on(2 * READ, READ, late_codes)
+        round_from_sbuf(ends[0] - READ, READ, res[:])
 
         res_end = keep.tile([P, PACK, READ], F32, name="res_end", align_bytes=64)
         for h in range(2):
-            cols = slice(h * half, (h + 1) * half)
-            nc.scalar.copy(out=res_end[:, 0:2, cols], in_=banks_end[h][0][:])
-            second_copy = nc.scalar.copy if h == 0 else nc.vector.tensor_copy
-            second_copy(out=res_end[:, 2:4, cols], in_=banks_end[h][1][:])
+            nc.scalar.copy(out=res_end[:, :, h * half : (h + 1) * half], in_=banks_end[h][:])
         nc.sync.dma_start(out=out_rows[:, :, ends[0] :], in_=res_end[:])
-        for h in range(2):
-            nc.vector.tensor_copy(
-                out=woven(out_bf[:, PACK * ends[h] : PACK * (ends[h] + half)]),
-                in_=planes(res_end[:, :, h * half : (h + 1) * half]),
-            )
+        round_out(ends[1], banks_end[1])
+        round_from_sbuf(ends[0], half, res_end[:, :, :half])
+        late_codes = keep.tile([P, 2 * READ], U32, name="late_codes", align_bytes=64)
+        hand_on(2 * READ, READ, late_codes)
         for v0 in ends:
             hand_on(v0, half, late_codes)
         nc.sync.dma_start(out=out_words[:, 2 * READ :], in_=late_codes[:].bitcast(I32))

@@ -22,7 +22,6 @@ PER_COL = 16
 PICK = 256
 READ = 256
 LEAD = 128
-SHARE = 192
 
 
 def tile_picked_pageread_silu_po_kernel(
@@ -159,37 +158,42 @@ def tile_picked_pageread_silu_po_kernel(
             return ap.rearrange("p (c t) -> p c t", t=PACK)
 
         got_all = keep.tile([P, 2 * PACK - 1, READ], F32, name="got_all", align_bytes=64)
+        first_row = (3, 0, 2, 0)
+        read_order = ((1, 2, 3, 0), (0, 1, 2, 3), (2, 3, 0, 1), (0, 1, 2, 3))
+        out_bf = keep.tile([P, PACK * V], BF16, name="out_bf", align_bytes=64)
 
         def rows(c):
-            base = PACK - 1 if c % 2 == 0 else 0
-            return got_all[:, base : base + PACK, :]
+            return got_all[:, first_row[c] : first_row[c] + PACK, :]
 
         def gather(c, first, count):
-            order = (1, 2, 3, 0) if c % 2 == 0 else (0, 1, 2, 3)
             window = page if c == 0 else active
-            for t in order[first : first + count]:
+            for t in read_order[c][first : first + count]:
                 nc.vector.tensor_copy(out=rows(c)[:, t, :], in_=window[t][:].indirect(entries(rd_sb, c * READ, READ)))
 
+        def weave_on_gpsimd(dst, src):
+            nc.gpsimd.tensor_scalar(
+                out=side_by_side(dst),
+                in0=src.rearrange("p t c -> p c t"),
+                scalar1=1.0,
+                scalar2=-0.0,
+                op0=mybir.AluOpType.mult,
+                op1=mybir.AluOpType.add,
+            )
+
         def weave(c):
-            z_bf = keep.tile([P, PACK * READ], BF16, name="z_bf%d" % c, align_bytes=64)
             if c == 0:
-                nc.scalar.activation(out=woven(z_bf[:]), in_=planes(rows(c)), func=SILU)
-            else:
-                nc.scalar.copy(out=woven(z_bf[:, PACK * SHARE :]), in_=planes(rows(c)[:, :, SHARE:]))
-                nc.gpsimd.tensor_scalar(
-                    out=side_by_side(z_bf[:, : PACK * SHARE]),
-                    in0=rows(c)[:, :, :SHARE].rearrange("p t c -> p c t"),
-                    scalar1=1.0,
-                    scalar2=-0.0,
-                    op0=mybir.AluOpType.mult,
-                    op1=mybir.AluOpType.add,
-                )
+                z_first = keep.tile([P, PACK * READ], BF16, name="z_first", align_bytes=64)
+                nc.scalar.activation(out=woven(z_first[:]), in_=planes(rows(c)), func=SILU)
+                return z_first[:]
+            z_bf = out_bf[:, (c - 1) * PACK * READ : c * PACK * READ]
+            nc.scalar.copy(out=woven(z_bf[:, PACK * half :]), in_=planes(rows(c)[:, :, half:]))
+            weave_on_gpsimd(z_bf[:, : PACK * half], rows(c)[:, :, :half])
             return z_bf
 
         def quantise(v0, width, z_bf):
             z_codes = keep.tile([P, width], U32, name="z_codes%d" % v0, align_bytes=64)
             z_bytes = keep.tile([P, width], U8, name="z_bytes%d" % v0, align_bytes=64)
-            nc.vector.quantize_mx(out=z_codes[:].bitcast(FP8X4), scales=z_bytes[:], in_=z_bf[:])
+            nc.vector.quantize_mx(out=z_codes[:].bitcast(FP8X4), scales=z_bytes[:], in_=z_bf)
             return z_codes, z_bytes
 
         def multiply(z_codes, z_bytes, start, width, first, count):
@@ -206,8 +210,6 @@ def tile_picked_pageread_silu_po_kernel(
                     stop=True,
                 )
             return acc
-
-        out_bf = keep.tile([P, PACK * V], BF16, name="out_bf", align_bytes=64)
 
         def hand_on(v0, width, codes):
             start = v0 % (2 * READ)
@@ -228,47 +230,54 @@ def tile_picked_pageread_silu_po_kernel(
         gather(0, 0, PACK)
         z_bf = weave(0)
         for c in range(last):
-            gather(c + 1, 0, PACK - 1)
+            ahead = PACK - 1 if c == 0 else PACK - 2
+            gather(c + 1, 0, ahead)
             operand = quantise(c * READ, READ, z_bf)
-            gather(c + 1, PACK - 1, 1)
-            if c + 1 < last:
-                z_bf = weave(c + 1)
+            if c > 0:
+                v0, res, bank = late
+                weave_on_gpsimd(out_bf[:, PACK * v0 : PACK * (v0 + half)], res[:, :, :half])
+                round_out(v0 + half, bank)
+            gather(c + 1, ahead, PACK - ahead)
+            banks = [multiply(*operand, h * half, half, 0, PACK) for h in range(2)]
             res = keep.tile([P, PACK, READ], F32, name="res%d" % c, align_bytes=64)
             if c + 1 < last:
-                banks = [multiply(*operand, h * half, half, 0, PACK) for h in range(2)]
+                z_bf = weave(c + 1)
                 for h in range(2):
                     nc.scalar.copy(out=res[:, :, h * half : (h + 1) * half], in_=banks[h][:])
                 nc.sync.dma_start(out=out_rows[:, :, c * READ : (c + 1) * READ], in_=res[:])
-                for h in range(2):
-                    round_out(c * READ + h * half, banks[h])
+                late = (c * READ, res, banks[1])
             else:
-                for first in (0, 2):
-                    pair = slice(first, first + 2)
-                    nc.scalar.copy(out=res[:, pair, :], in_=multiply(*operand, 0, READ, first, 2)[:])
-                    nc.scalar.dma_start(out=out_rows[:, pair, c * READ : (c + 1) * READ], in_=res[:, pair, :])
+                for h in range(2):
+                    cols = slice(h * half, (h + 1) * half)
+                    v0 = c * READ + h * half
+                    nc.scalar.copy(out=res[:, :, cols], in_=banks[h][:])
+                    nc.scalar.dma_start(out=out_rows[:, :, v0 : v0 + half], in_=res[:, :, cols])
+                round_out(c * READ + half, banks[1])
 
         ends = [last * READ, last * READ + half]
         z_end = [keep.tile([P, PACK * half], BF16, name="z_end%d" % h, align_bytes=64) for h in range(2)]
         for h in range(2):
             nc.vector.tensor_copy(out=woven(z_end[h][:]), in_=planes(rows(last)[:, :, h * half : (h + 1) * half]))
-        operands = [quantise(ends[h], half, z_end[h]) for h in range(2)]
+        operands = [quantise(ends[h], half, z_end[h][:]) for h in range(2)]
         banks_end = [multiply(*operand, 0, half, 0, PACK) for operand in operands]
         early_codes = keep.tile([P, 2 * READ], U32, name="early_codes", tag="got_all", align_bytes=64)
         hand_on(0, 2 * READ, early_codes)
         nc.sync.dma_start(out=out_words[:, : 2 * READ], in_=early_codes[:].bitcast(I32))
-        round_from_sbuf(ends[0] - READ, READ, res[:])
+        round_from_sbuf(ends[0] - READ, half, res[:, :, :half])
 
         res_end = keep.tile([P, PACK, READ], F32, name="res_end", align_bytes=64)
         for h in range(2):
-            nc.scalar.copy(out=res_end[:, :, h * half : (h + 1) * half], in_=banks_end[h][:])
-        nc.sync.dma_start(out=out_rows[:, :, ends[0] :], in_=res_end[:])
+            cols = slice(h * half, (h + 1) * half)
+            nc.scalar.copy(out=res_end[:, :, cols], in_=banks_end[h][:])
+            nc.sync.dma_start(out=out_rows[:, :, ends[h] : ends[h] + half], in_=res_end[:, :, cols])
         round_out(ends[1], banks_end[1])
         round_from_sbuf(ends[0], half, res_end[:, :, :half])
         late_codes = keep.tile([P, 2 * READ], U32, name="late_codes", align_bytes=64)
         hand_on(2 * READ, READ, late_codes)
+        nc.sync.dma_start(out=out_words[:, 2 * READ : ends[0]], in_=late_codes[:, :READ].bitcast(I32))
         for v0 in ends:
             hand_on(v0, half, late_codes)
-        nc.sync.dma_start(out=out_words[:, 2 * READ :], in_=late_codes[:].bitcast(I32))
+        nc.sync.dma_start(out=out_words[:, ends[0] :], in_=late_codes[:, READ:].bitcast(I32))
         for r in range(4):
             eng = nc.sync if r % 2 == 0 else nc.scalar
             eng.dma_start(out=out_2[0, r:16:4, :].bitcast(I32), in_=out_bytes[r:P:32, :].bitcast(I32))

@@ -22,6 +22,7 @@ PER_COL = 16
 PICK = 256
 READ = 256
 LEAD = 128
+CAST = 80
 
 
 def tile_picked_pageread_silu_po_kernel(
@@ -39,18 +40,18 @@ def tile_picked_pageread_silu_po_kernel(
         x_bytes = keep.tile([P, T], U8, name="x_bytes", align_bytes=64)
         w2_raw = keep.tile([P, 2 * N], U8, name="w2_raw", align_bytes=64)
         w2_raw_bytes = keep.tile([P, N], U8, name="w2_raw_bytes", align_bytes=64)
-        w1_raw = [keep.tile([P, PACK, H // 2], F32, name="w1_raw%d" % a, align_bytes=64) for a in range(2)]
+        w1_raw = keep.tile([P, PACK, H], F32, name="w1_raw", align_bytes=64)
         page = [keep.tile([P, U], F32, name="page%d" % t, align_bytes=64) for t in range(PACK)]
 
         nc.vector.memset(x_bytes[:].bitcast(I32), 0)
         nc.vector.memset(w2_raw_bytes[:].bitcast(I32), 0)
 
         w1_rows = w1.rearrange("(p j) c -> p j c", j=PACK)
-        nc.sync.dma_start(out=w1_raw[0][:], in_=w1_rows[:, :, 0 : H // 2])
+        nc.sync.dma_start(out=w1_raw[:, 0:2, :], in_=w1_rows[:, 0:2, :])
         nc.sync.dma_start(offs_sb[:], offs)
         for r in range(4):
             nc.sync.dma_start(out=x_bytes[r:P:32, :].bitcast(I32), in_=x_scales[0, r:16:4, :].bitcast(I32))
-        nc.sync.dma_start(out=w1_raw[1][:], in_=w1_rows[:, :, H // 2 : H])
+        nc.sync.dma_start(out=w1_raw[:, 2:4, :], in_=w1_rows[:, 2:4, :])
         nc.sync.dma_start(out=x_codes[:].bitcast(I32), in_=x_words[0].rearrange("p c r -> p (c r)").bitcast(I32))
         nc.sync.dma_start(slot_sb[:], slot)
         mem_rows = mem.rearrange("(p t) u -> p t u", t=PACK)
@@ -81,13 +82,15 @@ def tile_picked_pageread_silu_po_kernel(
         def entries(lst, start, count):
             return lst[:, start // PER_COL : (start + count) // PER_COL]
 
-        w1_bf = keep.tile([P, PACK * H], BF16, name="w1_bf", align_bytes=64)
-        w1_dst = w1_bf[:].rearrange("p (t m j) -> p m j t", t=PACK, j=PACK)
-        half_m = P // 2
-        nc.scalar.copy(out=w1_dst[:, 0:half_m], in_=w1_raw[0][:].rearrange("p j (m t) -> p m j t", t=PACK))
-        nc.vector.tensor_copy(out=w1_dst[:, half_m:P], in_=w1_raw[1][:].rearrange("p j (m t) -> p m j t", t=PACK))
         for h in range(halves):
             nc.vector.tensor_copy(out=picked_bytes[h][:], in_=x_bytes[:].indirect(entries(offs_sb, h * PICK, PICK)))
+
+        w1_bf = keep.tile([P, PACK * H], BF16, name="w1_bf", align_bytes=64)
+        w1_dst = w1_bf[:].rearrange("p (t m j) -> p m j t", t=PACK, j=PACK)
+        w1_src = w1_raw[:].rearrange("p j (m t) -> p m j t", t=PACK)
+        nc.vector.tensor_copy(out=w1_dst[:, :CAST], in_=w1_src[:, :CAST])
+        for pair in (slice(0, 2), slice(2, 4)):
+            nc.scalar.copy(out=w1_dst[:, CAST:, pair], in_=w1_src[:, CAST:, pair])
 
         w1_codes = keep.tile([P, H], U32, name="w1_codes", align_bytes=64)
         w1_bytes = keep.tile([P, H], U8, name="w1_bytes", align_bytes=64)
@@ -238,21 +241,22 @@ def tile_picked_pageread_silu_po_kernel(
                 weave_on_gpsimd(out_bf[:, PACK * v0 : PACK * (v0 + half)], res[:, :, :half])
                 round_out(v0 + half, bank)
             gather(c + 1, ahead, PACK - ahead)
-            banks = [multiply(*operand, h * half, half, 0, PACK) for h in range(2)]
             res = keep.tile([P, PACK, READ], F32, name="res%d" % c, align_bytes=64)
             if c + 1 < last:
+                banks = [multiply(*operand, h * half, half, 0, PACK) for h in range(2)]
                 z_bf = weave(c + 1)
                 for h in range(2):
                     nc.scalar.copy(out=res[:, :, h * half : (h + 1) * half], in_=banks[h][:])
                 nc.sync.dma_start(out=out_rows[:, :, c * READ : (c + 1) * READ], in_=res[:])
                 late = (c * READ, res, banks[1])
             else:
-                for h in range(2):
-                    cols = slice(h * half, (h + 1) * half)
-                    v0 = c * READ + h * half
-                    nc.scalar.copy(out=res[:, :, cols], in_=banks[h][:])
-                    nc.scalar.dma_start(out=out_rows[:, :, v0 : v0 + half], in_=res[:, :, cols])
-                round_out(c * READ + half, banks[1])
+                for first in (0, 2):
+                    pair = slice(first, first + 2)
+                    nc.scalar.copy(out=res[:, pair, :], in_=multiply(*operand, 0, READ, first, 2)[:])
+                    nc.scalar.dma_start(out=out_rows[:, pair, c * READ : (c + 1) * READ], in_=res[:, pair, :])
+                nc.scalar.copy(
+                    out=woven(out_bf[:, PACK * (c * READ + half) : PACK * (c + 1) * READ]), in_=planes(res[:, :, half:])
+                )
 
         ends = [last * READ, last * READ + half]
         z_end = [keep.tile([P, PACK * half], BF16, name="z_end%d" % h, align_bytes=64) for h in range(2)]
@@ -269,7 +273,7 @@ def tile_picked_pageread_silu_po_kernel(
         for h in range(2):
             cols = slice(h * half, (h + 1) * half)
             nc.scalar.copy(out=res_end[:, :, cols], in_=banks_end[h][:])
-            nc.sync.dma_start(out=out_rows[:, :, ends[h] : ends[h] + half], in_=res_end[:, :, cols])
+        nc.sync.dma_start(out=out_rows[:, :, ends[0] :], in_=res_end[:])
         round_out(ends[1], banks_end[1])
         round_from_sbuf(ends[0], half, res_end[:, :, :half])
         late_codes = keep.tile([P, 2 * READ], U32, name="late_codes", align_bytes=64)

@@ -23,6 +23,7 @@ PICK = 256
 READ = 256
 LEAD = 128
 CAST = 80
+SHARE = 192
 
 
 def tile_picked_pageread_silu_po_kernel(
@@ -161,8 +162,8 @@ def tile_picked_pageread_silu_po_kernel(
             return ap.rearrange("p (c t) -> p c t", t=PACK)
 
         got_all = keep.tile([P, 2 * PACK - 1, READ], F32, name="got_all", align_bytes=64)
-        first_row = (3, 0, 2, 0)
-        read_order = ((1, 2, 3, 0), (0, 1, 2, 3), (2, 3, 0, 1), (0, 1, 2, 3))
+        first_row = (3, 0, 3, 1)
+        read_order = ((1, 2, 3, 0), (0, 1, 2, 3), (1, 2, 3, 0), (0, 1, 2, 3))
         out_bf = keep.tile([P, PACK * V], BF16, name="out_bf", align_bytes=64)
 
         def rows(c):
@@ -188,9 +189,13 @@ def tile_picked_pageread_silu_po_kernel(
                 z_first = keep.tile([P, PACK * READ], BF16, name="z_first", align_bytes=64)
                 nc.scalar.activation(out=woven(z_first[:]), in_=planes(rows(c)), func=SILU)
                 return z_first[:]
-            z_bf = out_bf[:, (c - 1) * PACK * READ : c * PACK * READ]
-            nc.scalar.copy(out=woven(z_bf[:, PACK * half :]), in_=planes(rows(c)[:, :, half:]))
-            weave_on_gpsimd(z_bf[:, : PACK * half], rows(c)[:, :, :half])
+            if c == 1:
+                z_second = keep.tile([P, PACK * READ], BF16, name="z_second", align_bytes=64)
+                z_bf, share = z_second[:], SHARE
+            else:
+                z_bf, share = out_bf[:, PACK * READ : 2 * PACK * READ], half
+            nc.scalar.copy(out=woven(z_bf[:, PACK * share :]), in_=planes(rows(c)[:, :, share:]))
+            weave_on_gpsimd(z_bf[:, : PACK * share], rows(c)[:, :, :share])
             return z_bf
 
         def quantise(v0, width, z_bf):
@@ -233,10 +238,10 @@ def tile_picked_pageread_silu_po_kernel(
         gather(0, 0, PACK)
         z_bf = weave(0)
         for c in range(last):
-            ahead = PACK - 1 if c == 0 else PACK - 2
+            ahead = PACK - 1 if c + 1 < last else PACK - 2
             gather(c + 1, 0, ahead)
             operand = quantise(c * READ, READ, z_bf)
-            if c > 0:
+            if c + 1 == last:
                 v0, res, bank = late
                 weave_on_gpsimd(out_bf[:, PACK * v0 : PACK * (v0 + half)], res[:, :, :half])
                 round_out(v0 + half, bank)
@@ -249,6 +254,9 @@ def tile_picked_pageread_silu_po_kernel(
                     nc.scalar.copy(out=res[:, :, h * half : (h + 1) * half], in_=banks[h][:])
                 nc.sync.dma_start(out=out_rows[:, :, c * READ : (c + 1) * READ], in_=res[:])
                 late = (c * READ, res, banks[1])
+                if c == 0:
+                    for h in range(2):
+                        round_out(h * half, banks[h])
             else:
                 for first in (0, 2):
                     pair = slice(first, first + 2)
@@ -263,22 +271,24 @@ def tile_picked_pageread_silu_po_kernel(
         for h in range(2):
             nc.vector.tensor_copy(out=woven(z_end[h][:]), in_=planes(rows(last)[:, :, h * half : (h + 1) * half]))
         operands = [quantise(ends[h], half, z_end[h][:]) for h in range(2)]
-        banks_end = [multiply(*operand, 0, half, 0, PACK) for operand in operands]
+        banks_end = [[multiply(*operand, 0, half, first, 2) for operand in operands] for first in (0, 2)]
         early_codes = keep.tile([P, 2 * READ], U32, name="early_codes", tag="got_all", align_bytes=64)
         hand_on(0, 2 * READ, early_codes)
         nc.sync.dma_start(out=out_words[:, : 2 * READ], in_=early_codes[:].bitcast(I32))
         round_from_sbuf(ends[0] - READ, half, res[:, :, :half])
 
-        res_end = keep.tile([P, PACK, READ], F32, name="res_end", align_bytes=64)
-        for h in range(2):
-            cols = slice(h * half, (h + 1) * half)
-            nc.scalar.copy(out=res_end[:, :, cols], in_=banks_end[h][:])
-        nc.sync.dma_start(out=out_rows[:, :, ends[0] :], in_=res_end[:])
-        round_out(ends[1], banks_end[1])
-        round_from_sbuf(ends[0], half, res_end[:, :, :half])
         late_codes = keep.tile([P, 2 * READ], U32, name="late_codes", align_bytes=64)
         hand_on(2 * READ, READ, late_codes)
         nc.sync.dma_start(out=out_words[:, 2 * READ : ends[0]], in_=late_codes[:, :READ].bitcast(I32))
+
+        res_end = keep.tile([P, PACK, READ], F32, name="res_end", align_bytes=64)
+        for e in range(2):
+            pair = slice(2 * e, 2 * e + 2)
+            for h in range(2):
+                nc.scalar.copy(out=res_end[:, pair, h * half : (h + 1) * half], in_=banks_end[e][h][:])
+            nc.sync.dma_start(out=out_rows[:, pair, ends[0] :], in_=res_end[:, pair, :])
+        for h in range(2):
+            round_from_sbuf(ends[h], half, res_end[:, :, h * half : (h + 1) * half])
         for v0 in ends:
             hand_on(v0, half, late_codes)
         nc.sync.dma_start(out=out_words[:, ends[0] :], in_=late_codes[:, READ:].bitcast(I32))

@@ -17,12 +17,15 @@ SILU = mybir.ActivationFunctionType.Silu
 
 P = 128
 PACK = 4
-QUADS = 4
+QUADRANT = 32
+SCALE_ROWS = 16
 PER_COL = 16
+BANKS = 8
 PICK = 256
-READ = 256
 LEAD = 128
 CAST = 80
+READ = 256
+HALF = READ // 2
 SHARE = 192
 
 
@@ -44,25 +47,32 @@ def tile_picked_pageread_silu_po_kernel(
         w1_raw = keep.tile([P, PACK, H], F32, name="w1_raw", align_bytes=64)
         page = [keep.tile([P, U], F32, name="page%d" % t, align_bytes=64) for t in range(PACK)]
 
+        def scale_rows(tile, r):
+            return tile[r:P:QUADRANT, :].bitcast(I32)
+
+        def dram_scale_rows(scales, r):
+            return scales[0, r:SCALE_ROWS:PACK, :].bitcast(I32)
+
         nc.vector.memset(x_bytes[:].bitcast(I32), 0)
         nc.vector.memset(w2_raw_bytes[:].bitcast(I32), 0)
 
+        row_pairs = (slice(0, 2), slice(2, PACK))
         w1_rows = w1.rearrange("(p j) c -> p j c", j=PACK)
-        nc.sync.dma_start(out=w1_raw[:, 0:2, :], in_=w1_rows[:, 0:2, :])
+        nc.sync.dma_start(out=w1_raw[:, row_pairs[0], :], in_=w1_rows[:, row_pairs[0], :])
         nc.sync.dma_start(offs_sb[:], offs)
-        for r in range(4):
-            nc.sync.dma_start(out=x_bytes[r:P:32, :].bitcast(I32), in_=x_scales[0, r:16:4, :].bitcast(I32))
-        nc.sync.dma_start(out=w1_raw[:, 2:4, :], in_=w1_rows[:, 2:4, :])
+        for r in range(PACK):
+            nc.sync.dma_start(out=scale_rows(x_bytes, r), in_=dram_scale_rows(x_scales, r))
+        nc.sync.dma_start(out=w1_raw[:, row_pairs[1], :], in_=w1_rows[:, row_pairs[1], :])
         nc.sync.dma_start(out=x_codes[:].bitcast(I32), in_=x_words[0].rearrange("p c r -> p (c r)").bitcast(I32))
         nc.sync.dma_start(slot_sb[:], slot)
-        mem_rows = mem.rearrange("(p t) u -> p t u", t=PACK)
+        mem_planes = mem.rearrange("(p t) u -> p t u", t=PACK)
         for t in range(2):
-            nc.sync.dma_start(out=page[t][:], in_=mem_rows[:, t, :])
+            nc.sync.dma_start(out=page[t][:], in_=mem_planes[:, t, :])
         nc.sync.dma_start(out=w2_raw[:].bitcast(I32), in_=w2_words[0].bitcast(I32))
-        for r in range(4):
-            nc.sync.dma_start(out=w2_raw_bytes[r:P:32, :].bitcast(I32), in_=w2_scales[0, r:16:4, :].bitcast(I32))
+        for r in range(PACK):
+            nc.sync.dma_start(out=scale_rows(w2_raw_bytes, r), in_=dram_scale_rows(w2_scales, r))
         for t in range(2, PACK):
-            nc.sync.dma_start(out=page[t][:], in_=mem_rows[:, t, :])
+            nc.sync.dma_start(out=page[t][:], in_=mem_planes[:, t, :])
         nc.sync.dma_start(rd_sb[:], rd)
 
         w2_codes = keep.tile([P, 2 * N], U8, name="w2_codes", align_bytes=64)
@@ -76,54 +86,54 @@ def tile_picked_pageread_silu_po_kernel(
             in_=w2_raw_bytes[:].rearrange("p (m t) -> p t m", t=PACK),
         )
 
-        halves = S // PICK
-        picked_bytes = [keep.tile([P, PICK], U8, name="picked_bytes%d" % h, align_bytes=64) for h in range(halves)]
-        picked_codes = [keep.tile([P, PICK], U32, name="picked_codes%d" % h, align_bytes=64) for h in range(halves)]
+        picks = S // PICK
+        picked_bytes = [keep.tile([P, PICK], U8, name="picked_bytes%d" % g, align_bytes=64) for g in range(picks)]
+        picked_codes = [keep.tile([P, PICK], U32, name="picked_codes%d" % g, align_bytes=64) for g in range(picks)]
 
         def entries(lst, start, count):
             return lst[:, start // PER_COL : (start + count) // PER_COL]
 
-        for h in range(halves):
-            nc.vector.tensor_copy(out=picked_bytes[h][:], in_=x_bytes[:].indirect(entries(offs_sb, h * PICK, PICK)))
+        for g in range(picks):
+            nc.vector.tensor_copy(out=picked_bytes[g][:], in_=x_bytes[:].indirect(entries(offs_sb, g * PICK, PICK)))
 
         w1_bf = keep.tile([P, PACK * H], BF16, name="w1_bf", align_bytes=64)
         w1_dst = w1_bf[:].rearrange("p (t m j) -> p m j t", t=PACK, j=PACK)
         w1_src = w1_raw[:].rearrange("p j (m t) -> p m j t", t=PACK)
         nc.vector.tensor_copy(out=w1_dst[:, :CAST], in_=w1_src[:, :CAST])
-        for pair in (slice(0, 2), slice(2, 4)):
+        for pair in row_pairs:
             nc.scalar.copy(out=w1_dst[:, CAST:, pair], in_=w1_src[:, CAST:, pair])
 
         w1_codes = keep.tile([P, H], U32, name="w1_codes", align_bytes=64)
         w1_bytes = keep.tile([P, H], U8, name="w1_bytes", align_bytes=64)
         nc.vector.quantize_mx(out=w1_codes[:].bitcast(FP8X4), scales=w1_bytes[:], in_=w1_bf[:])
 
-        for h in range(halves):
-            nc.vector.tensor_copy(out=picked_codes[h][:], in_=x_codes[:].indirect(entries(offs_sb, h * PICK, PICK)))
+        for g in range(picks):
+            nc.vector.tensor_copy(out=picked_codes[g][:], in_=x_codes[:].indirect(entries(offs_sb, g * PICK, PICK)))
 
         y = [keep.tile([P, S], F32, name="y%d" % t, align_bytes=64) for t in range(PACK)]
 
         def project(t, start, count):
-            h, cols, picked = start // PICK, slice(t * P, (t + 1) * P), slice(start % PICK, start % PICK + count)
-            acc = psum.tile([P, count], F32, name="acc", bufs=8)
+            g, cols, tokens = start // PICK, slice(t * P, (t + 1) * P), slice(start % PICK, start % PICK + count)
+            acc = psum.tile([P, count], F32, name="acc", bufs=BANKS)
             nc.tensor.matmul_mx(
                 out=acc[:],
                 lhsT=w1_codes[:, cols].bitcast(FP8X4),
                 lhsT_scale=w1_bytes[:, cols],
-                rhs=picked_codes[h][:, picked].bitcast(FP8X4),
-                rhs_scale=picked_bytes[h][:, picked],
+                rhs=picked_codes[g][:, tokens].bitcast(FP8X4),
+                rhs_scale=picked_bytes[g][:, tokens],
                 start=True,
                 stop=True,
             )
             nc.scalar.copy(out=y[t][:, start : start + count], in_=acc[:])
 
         project(0, 0, LEAD)
-        for h in range(halves):
-            project(1, h * PICK, PICK)
+        for g in range(picks):
+            project(1, g * PICK, PICK)
         project(0, LEAD, PICK - LEAD)
         project(0, PICK, PICK)
         for t in range(2, PACK):
-            for h in range(halves):
-                project(t, h * PICK, PICK)
+            for g in range(picks):
+                project(t, g * PICK, PICK)
 
         def scatter(t, start, count):
             nc.vector.tensor_copy(
@@ -140,15 +150,11 @@ def tile_picked_pageread_silu_po_kernel(
         activate_page(1)
         scatter(0, LEAD, S - LEAD)
         activate_page(0)
-        scatter(2, 0, S)
-        activate_page(2)
-        scatter(3, 0, S)
-        activate_page(3)
+        for t in range(2, PACK):
+            scatter(t, 0, S)
+            activate_page(t)
 
-        chunks = V // READ
-        last = chunks - 1
-        half = READ // 2
-        out_rows = out_0.rearrange("(p t) v -> p t v", t=PACK)
+        out_planes = out_0.rearrange("(p t) v -> p t v", t=PACK)
         out_words = out_1[0].rearrange("p c r -> p (c r)").bitcast(I32)
         out_bytes = keep.tile([P, V], U8, name="out_bytes", align_bytes=64)
 
@@ -163,16 +169,18 @@ def tile_picked_pageread_silu_po_kernel(
 
         got_all = keep.tile([P, 2 * PACK - 1, READ], F32, name="got_all", align_bytes=64)
         first_row = (3, 0, 3, 1)
-        read_order = ((1, 2, 3, 0), (0, 1, 2, 3), (1, 2, 3, 0), (0, 1, 2, 3))
         out_bf = keep.tile([P, PACK * V], BF16, name="out_bf", align_bytes=64)
 
         def rows(c):
             return got_all[:, first_row[c] : first_row[c] + PACK, :]
 
-        def gather(c, first, count):
-            window = page if c == 0 else active
-            for t in read_order[c][first : first + count]:
+        def gather(c, window, first, count):
+            for step in range(first, first + count):
+                t = (step + 1 - c % 2) % PACK
                 nc.vector.tensor_copy(out=rows(c)[:, t, :], in_=window[t][:].indirect(entries(rd_sb, c * READ, READ)))
+
+        def rounded(v0, width):
+            return out_bf[:, PACK * v0 : PACK * (v0 + width)]
 
         def weave_on_gpsimd(dst, src):
             nc.gpsimd.tensor_scalar(
@@ -184,19 +192,9 @@ def tile_picked_pageread_silu_po_kernel(
                 op1=mybir.AluOpType.add,
             )
 
-        def weave(c):
-            if c == 0:
-                z_first = keep.tile([P, PACK * READ], BF16, name="z_first", align_bytes=64)
-                nc.scalar.activation(out=woven(z_first[:]), in_=planes(rows(c)), func=SILU)
-                return z_first[:]
-            if c == 1:
-                z_second = keep.tile([P, PACK * READ], BF16, name="z_second", align_bytes=64)
-                z_bf, share = z_second[:], SHARE
-            else:
-                z_bf, share = out_bf[:, PACK * READ : 2 * PACK * READ], half
+        def weave_shared(c, z_bf, share):
             nc.scalar.copy(out=woven(z_bf[:, PACK * share :]), in_=planes(rows(c)[:, :, share:]))
             weave_on_gpsimd(z_bf[:, : PACK * share], rows(c)[:, :, :share])
-            return z_bf
 
         def quantise(v0, width, z_bf):
             z_codes = keep.tile([P, width], U32, name="z_codes%d" % v0, align_bytes=64)
@@ -204,8 +202,9 @@ def tile_picked_pageread_silu_po_kernel(
             nc.vector.quantize_mx(out=z_codes[:].bitcast(FP8X4), scales=z_bytes[:], in_=z_bf)
             return z_codes, z_bytes
 
-        def multiply(z_codes, z_bytes, start, width, first, count):
-            acc = psum.tile([P, count, width], F32, name="acc", bufs=8)
+        def multiply(operand, start, width, first, count):
+            z_codes, z_bytes = operand
+            acc = psum.tile([P, count, width], F32, name="acc", bufs=BANKS)
             for e in range(count):
                 t = first + e
                 nc.tensor.matmul_mx(
@@ -219,79 +218,94 @@ def tile_picked_pageread_silu_po_kernel(
                 )
             return acc
 
-        def hand_on(v0, width, codes):
-            start = v0 % (2 * READ)
-            nc.vector.quantize_mx(
-                out=codes[:, start : start + width].bitcast(FP8X4),
-                scales=out_bytes[:, v0 : v0 + width],
-                in_=out_bf[:, PACK * v0 : PACK * (v0 + width)],
-            )
+        def result_tile(name):
+            return keep.tile([P, PACK, READ], F32, name=name, align_bytes=64)
 
-        def round_out(v0, bank):
-            nc.scalar.copy(
-                out=side_by_side(out_bf[:, PACK * v0 : PACK * (v0 + half)]), in_=bank[:].rearrange("p t c -> p c t")
-            )
+        def column_banks(operand):
+            return [multiply(operand, h * HALF, HALF, 0, PACK) for h in range(2)]
 
-        def round_from_sbuf(v0, width, res):
-            nc.vector.tensor_copy(out=woven(out_bf[:, PACK * v0 : PACK * (v0 + width)]), in_=planes(res))
-
-        gather(0, 0, PACK)
-        z_bf = weave(0)
-        for c in range(last):
-            ahead = PACK - 1 if c + 1 < last else PACK - 2
-            gather(c + 1, 0, ahead)
-            operand = quantise(c * READ, READ, z_bf)
-            if c + 1 == last:
-                v0, res, bank = late
-                weave_on_gpsimd(out_bf[:, PACK * v0 : PACK * (v0 + half)], res[:, :, :half])
-                round_out(v0 + half, bank)
-            gather(c + 1, ahead, PACK - ahead)
-            res = keep.tile([P, PACK, READ], F32, name="res%d" % c, align_bytes=64)
-            if c + 1 < last:
-                banks = [multiply(*operand, h * half, half, 0, PACK) for h in range(2)]
-                z_bf = weave(c + 1)
-                for h in range(2):
-                    nc.scalar.copy(out=res[:, :, h * half : (h + 1) * half], in_=banks[h][:])
-                nc.sync.dma_start(out=out_rows[:, :, c * READ : (c + 1) * READ], in_=res[:])
-                late = (c * READ, res, banks[1])
-                if c == 0:
-                    for h in range(2):
-                        round_out(h * half, banks[h])
-            else:
-                for first in (0, 2):
-                    pair = slice(first, first + 2)
-                    nc.scalar.copy(out=res[:, pair, :], in_=multiply(*operand, 0, READ, first, 2)[:])
-                    nc.scalar.dma_start(out=out_rows[:, pair, c * READ : (c + 1) * READ], in_=res[:, pair, :])
-                nc.scalar.copy(
-                    out=woven(out_bf[:, PACK * (c * READ + half) : PACK * (c + 1) * READ]), in_=planes(res[:, :, half:])
-                )
-
-        ends = [last * READ, last * READ + half]
-        z_end = [keep.tile([P, PACK * half], BF16, name="z_end%d" % h, align_bytes=64) for h in range(2)]
-        for h in range(2):
-            nc.vector.tensor_copy(out=woven(z_end[h][:]), in_=planes(rows(last)[:, :, h * half : (h + 1) * half]))
-        operands = [quantise(ends[h], half, z_end[h][:]) for h in range(2)]
-        banks_end = [[multiply(*operand, 0, half, first, 2) for operand in operands] for first in (0, 2)]
-        early_codes = keep.tile([P, 2 * READ], U32, name="early_codes", tag="got_all", align_bytes=64)
-        hand_on(0, 2 * READ, early_codes)
-        nc.sync.dma_start(out=out_words[:, : 2 * READ], in_=early_codes[:].bitcast(I32))
-        round_from_sbuf(ends[0] - READ, half, res[:, :, :half])
-
-        late_codes = keep.tile([P, 2 * READ], U32, name="late_codes", align_bytes=64)
-        hand_on(2 * READ, READ, late_codes)
-        nc.sync.dma_start(out=out_words[:, 2 * READ : ends[0]], in_=late_codes[:, :READ].bitcast(I32))
-
-        res_end = keep.tile([P, PACK, READ], F32, name="res_end", align_bytes=64)
-        for e in range(2):
-            pair = slice(2 * e, 2 * e + 2)
+        def unload(c, banks, res):
             for h in range(2):
-                nc.scalar.copy(out=res_end[:, pair, h * half : (h + 1) * half], in_=banks_end[e][h][:])
-            nc.sync.dma_start(out=out_rows[:, pair, ends[0] :], in_=res_end[:, pair, :])
+                nc.scalar.copy(out=res[:, :, h * HALF : (h + 1) * HALF], in_=banks[h][:])
+            nc.sync.dma_start(out=out_planes[:, :, c * READ : (c + 1) * READ], in_=res[:])
+
+        def round_from_psum(v0, bank):
+            nc.scalar.copy(out=side_by_side(rounded(v0, HALF)), in_=bank[:].rearrange("p t c -> p c t"))
+
+        def round_on_vector(v0, src):
+            nc.vector.tensor_copy(out=woven(rounded(v0, HALF)), in_=planes(src))
+
+        gather(0, page, 0, PACK)
+        z_first = keep.tile([P, PACK * READ], BF16, name="z_first", align_bytes=64)
+        nc.scalar.activation(out=woven(z_first[:]), in_=planes(rows(0)), func=SILU)
+
+        gather(1, active, 0, PACK - 1)
+        operand = quantise(0, READ, z_first[:])
+        gather(1, active, PACK - 1, 1)
+        res0 = result_tile("res0")
+        banks0 = column_banks(operand)
+        z_second = keep.tile([P, PACK * READ], BF16, name="z_second", align_bytes=64)
+        weave_shared(1, z_second[:], SHARE)
+        unload(0, banks0, res0)
         for h in range(2):
-            round_from_sbuf(ends[h], half, res_end[:, :, h * half : (h + 1) * half])
+            round_from_psum(h * HALF, banks0[h])
+
+        gather(2, active, 0, PACK - 1)
+        operand = quantise(READ, READ, z_second[:])
+        gather(2, active, PACK - 1, 1)
+        res1 = result_tile("res1")
+        banks1 = column_banks(operand)
+        z_third = rounded(READ, READ)
+        weave_shared(2, z_third, HALF)
+        unload(1, banks1, res1)
+
+        gather(3, active, 0, PACK - 2)
+        operand = quantise(2 * READ, READ, z_third)
+        weave_on_gpsimd(rounded(READ, HALF), res1[:, :, :HALF])
+        round_from_psum(READ + HALF, banks1[1])
+        gather(3, active, PACK - 2, 2)
+        res2 = result_tile("res2")
+        for pair in row_pairs:
+            nc.scalar.copy(out=res2[:, pair, :], in_=multiply(operand, 0, READ, pair.start, 2)[:])
+            nc.scalar.dma_start(out=out_planes[:, pair, 2 * READ : 3 * READ], in_=res2[:, pair, :])
+        nc.scalar.copy(out=woven(rounded(2 * READ + HALF, HALF)), in_=planes(res2[:, :, HALF:]))
+
+        ends = (3 * READ, 3 * READ + HALF)
+        z_end = [keep.tile([P, PACK * HALF], BF16, name="z_end%d" % h, align_bytes=64) for h in range(2)]
+        for h in range(2):
+            nc.vector.tensor_copy(out=woven(z_end[h][:]), in_=planes(rows(3)[:, :, h * HALF : (h + 1) * HALF]))
+        operands = [quantise(ends[h], HALF, z_end[h][:]) for h in range(2)]
+        banks_end = [[multiply(operand, 0, HALF, pair.start, 2) for operand in operands] for pair in row_pairs]
+
+        codes = keep.tile([P, V], U32, name="codes", tag="got_all", align_bytes=64)
+
+        def hand_on(v0, width):
+            nc.vector.quantize_mx(
+                out=codes[:, v0 : v0 + width].bitcast(FP8X4),
+                scales=out_bytes[:, v0 : v0 + width],
+                in_=rounded(v0, width),
+            )
+
+        def store_words(v0, width):
+            nc.sync.dma_start(out=out_words[:, v0 : v0 + width], in_=codes[:, v0 : v0 + width].bitcast(I32))
+
+        hand_on(0, READ)
+        store_words(0, READ)
+        round_on_vector(2 * READ, res2[:, :, :HALF])
+        hand_on(READ, 2 * READ)
+        store_words(READ, 2 * READ)
+
+        res3 = result_tile("res_end")
+        for pair, pair_banks in zip(row_pairs, banks_end):
+            for h in range(2):
+                nc.scalar.copy(out=res3[:, pair, h * HALF : (h + 1) * HALF], in_=pair_banks[h][:])
+            nc.sync.dma_start(out=out_planes[:, pair, ends[0] :], in_=res3[:, pair, :])
+        for h in range(2):
+            round_on_vector(ends[h], res3[:, :, h * HALF : (h + 1) * HALF])
         for v0 in ends:
-            hand_on(v0, half, late_codes)
-        nc.sync.dma_start(out=out_words[:, ends[0] :], in_=late_codes[:, READ:].bitcast(I32))
-        for r in range(4):
-            eng = nc.sync if r % 2 == 0 else nc.scalar
-            eng.dma_start(out=out_2[0, r:16:4, :].bitcast(I32), in_=out_bytes[r:P:32, :].bitcast(I32))
+            hand_on(v0, HALF)
+        store_words(ends[0], READ)
+
+        for r in range(PACK):
+            queue = nc.sync if r % 2 == 0 else nc.scalar
+            queue.dma_start(out=dram_scale_rows(out_2, r), in_=scale_rows(out_bytes, r))

@@ -156,7 +156,7 @@ def tile_picked_pageread_silu_po_kernel(
 
         out_planes = out_0.rearrange("(p t) v -> p t v", t=PACK)
         out_words = out_1[0].rearrange("p c r -> p (c r)").bitcast(I32)
-        out_bytes = keep.tile([P, V], U8, name="out_bytes", align_bytes=64)
+        out_bytes = keep.tile([P, READ], U8, name="out_bytes", align_bytes=64)
 
         def woven(ap):
             return ap.rearrange("p (c i t) -> p c t i", i=4, t=PACK)
@@ -271,18 +271,13 @@ def tile_picked_pageread_silu_po_kernel(
         nc.scalar.copy(out=woven(rounded(2 * READ + HALF, HALF)), in_=planes(res2[:, :, HALF:]))
 
         ends = (3 * READ, 3 * READ + HALF)
-        z_end = [keep.tile([P, PACK * HALF], BF16, name="z_end%d" % h, align_bytes=64) for h in range(2)]
-        for h in range(2):
-            nc.vector.tensor_copy(out=woven(z_end[h][:]), in_=planes(rows(3)[:, :, h * HALF : (h + 1) * HALF]))
-        operands = [quantise(ends[h], HALF, z_end[h][:]) for h in range(2)]
-        banks_end = [[multiply(operand, 0, HALF, pair.start, 2) for operand in operands] for pair in row_pairs]
 
-        codes = keep.tile([P, V], U32, name="codes", tag="got_all", align_bytes=64)
+        codes = keep.tile([P, V], U32, name="codes", tag="active2", align_bytes=64)
 
         def hand_on(v0, width):
             nc.vector.quantize_mx(
                 out=codes[:, v0 : v0 + width].bitcast(FP8X4),
-                scales=out_bytes[:, v0 : v0 + width],
+                scales=out_bytes[PACK * (v0 // READ) :, v0 % READ : v0 % READ + width],
                 in_=rounded(v0, width),
             )
 
@@ -291,9 +286,16 @@ def tile_picked_pageread_silu_po_kernel(
 
         hand_on(0, READ)
         store_words(0, READ)
+        z_end = [keep.tile([P, PACK * HALF], BF16, name="z_end%d" % h, align_bytes=64) for h in range(2)]
+        for h in range(2):
+            nc.vector.tensor_copy(out=woven(z_end[h][:]), in_=planes(rows(3)[:, :, h * HALF : (h + 1) * HALF]))
+        operands = [quantise(ends[h], HALF, z_end[h][:]) for h in range(2)]
+        banks_end = [[multiply(operand, 0, HALF, pair.start, 2) for operand in operands] for pair in row_pairs]
+        hand_on(READ, READ)
+        store_words(READ, READ)
         round_on_vector(2 * READ, res2[:, :, :HALF])
-        hand_on(READ, 2 * READ)
-        store_words(READ, 2 * READ)
+        hand_on(2 * READ, READ)
+        store_words(2 * READ, READ)
 
         res3 = result_tile("res_end")
         for pair, pair_banks in zip(row_pairs, banks_end):
@@ -306,6 +308,9 @@ def tile_picked_pageread_silu_po_kernel(
             hand_on(v0, HALF)
         store_words(ends[0], READ)
 
-        for r in range(PACK):
-            queue = nc.sync if r % 2 == 0 else nc.scalar
-            queue.dma_start(out=dram_scale_rows(out_2, r), in_=scale_rows(out_bytes, r))
+        for q in range(PACK):
+            queue = nc.sync if q % 2 == 0 else nc.scalar
+            queue.dma_start(
+                out=out_2[0, PACK * q : PACK * (q + 1), :].bitcast(I32).rearrange("r (c v) -> c r v", c=PACK),
+                in_=out_bytes[QUADRANT * q : QUADRANT * q + SCALE_ROWS, :].bitcast(I32),
+            )

@@ -26,7 +26,6 @@ LEAD = 128
 CAST = 80
 READ = 256
 HALF = READ // 2
-SHARE = 192
 
 
 def tile_picked_pageread_silu_po_kernel(
@@ -167,24 +166,30 @@ def tile_picked_pageread_silu_po_kernel(
         def side_by_side(ap):
             return ap.rearrange("p (c t) -> p c t", t=PACK)
 
-        got_all = keep.tile([P, 2 * PACK - 1, READ], F32, name="got_all", align_bytes=64)
-        first_row = (3, 0, 3, 1)
+        got_all = keep.tile([P, 2 * PACK + 1, READ], F32, name="got_all", align_bytes=64)
+        plane_rows = ((3, 4, 5, 6), (7, 8, 2, 3), (2, 3, 4, 5), (0, 1, 2, 3))
+        first_plane = (1, 0, 2, 0)
         out_bf = keep.tile([P, PACK * V], BF16, name="out_bf", align_bytes=64)
 
         def rows(c):
-            return got_all[:, first_row[c] : first_row[c] + PACK, :]
+            return got_all[:, plane_rows[c][0] : plane_rows[c][0] + PACK, :]
+
+        def pair_rows(c, pair):
+            return got_all[:, plane_rows[c][pair.start] : plane_rows[c][pair.start] + 2, :]
 
         def gather(c, window, first, count):
             for step in range(first, first + count):
-                t = (step + 1 - c % 2) % PACK
-                nc.vector.tensor_copy(out=rows(c)[:, t, :], in_=window[t][:].indirect(entries(rd_sb, c * READ, READ)))
+                t = (step + first_plane[c]) % PACK
+                nc.vector.tensor_copy(
+                    out=got_all[:, plane_rows[c][t], :], in_=window[t][:].indirect(entries(rd_sb, c * READ, READ))
+                )
 
         def rounded(v0, width):
             return out_bf[:, PACK * v0 : PACK * (v0 + width)]
 
-        def weave_on_gpsimd(dst, src):
+        def weave_on_gpsimd(dst, src, pair=slice(0, PACK)):
             nc.gpsimd.tensor_scalar(
-                out=side_by_side(dst),
+                out=side_by_side(dst)[:, :, pair],
                 in0=src.rearrange("p t c -> p c t"),
                 scalar1=1.0,
                 scalar2=-0.0,
@@ -192,9 +197,10 @@ def tile_picked_pageread_silu_po_kernel(
                 op1=mybir.AluOpType.add,
             )
 
-        def weave_shared(c, z_bf, share):
-            nc.scalar.copy(out=woven(z_bf[:, PACK * share :]), in_=planes(rows(c)[:, :, share:]))
-            weave_on_gpsimd(z_bf[:, : PACK * share], rows(c)[:, :, :share])
+        def weave_shared(c, z_bf, pair):
+            src = pair_rows(c, pair)
+            nc.scalar.copy(out=woven(z_bf[:, PACK * HALF :])[:, :, pair], in_=planes(src[:, :, HALF:]))
+            weave_on_gpsimd(z_bf[:, : PACK * HALF], src[:, :, :HALF], pair)
 
         def quantise(v0, width, z_bf):
             z_codes = keep.tile([P, width], U32, name="z_codes%d" % v0, align_bytes=64)
@@ -224,9 +230,10 @@ def tile_picked_pageread_silu_po_kernel(
         def column_banks(operand):
             return [multiply(operand, h * HALF, HALF, 0, PACK) for h in range(2)]
 
-        def unload(c, banks, res):
-            for h in range(2):
-                nc.scalar.copy(out=res[:, :, h * HALF : (h + 1) * HALF], in_=banks[h][:])
+        def unload(banks, res, h):
+            nc.scalar.copy(out=res[:, :, h * HALF : (h + 1) * HALF], in_=banks[h][:])
+
+        def store_chunk(c, res):
             nc.sync.dma_start(out=out_planes[:, :, c * READ : (c + 1) * READ], in_=res[:])
 
         def round_from_psum(v0, bank):
@@ -240,24 +247,30 @@ def tile_picked_pageread_silu_po_kernel(
         nc.scalar.activation(out=woven(z_first[:]), in_=planes(rows(0)), func=SILU)
 
         gather(1, active, 0, PACK - 1)
+        z_second = got_all[:, 0:2, :].rearrange("p r c -> p (r c)").bitcast(BF16)
+        nc.scalar.copy(out=woven(z_second)[:, :, row_pairs[0]], in_=planes(pair_rows(1, row_pairs[0])))
         operand = quantise(0, READ, z_first[:])
         gather(1, active, PACK - 1, 1)
         res0 = result_tile("res0")
         banks0 = column_banks(operand)
-        z_second = keep.tile([P, PACK * READ], BF16, name="z_second", align_bytes=64)
-        weave_shared(1, z_second[:], SHARE)
-        unload(0, banks0, res0)
+        weave_shared(1, z_second, row_pairs[1])
         for h in range(2):
-            round_from_psum(h * HALF, banks0[h])
+            unload(banks0, res0, h)
+        store_chunk(0, res0)
+        round_from_psum(0, banks0[0])
 
-        gather(2, active, 0, PACK - 1)
-        operand = quantise(READ, READ, z_second[:])
-        gather(2, active, PACK - 1, 1)
+        gather(2, active, 0, PACK - 2)
+        operand = quantise(READ, READ, z_second)
+        z_third = rounded(READ, READ)
+        weave_on_gpsimd(z_third, pair_rows(2, row_pairs[1]), row_pairs[1])
+        gather(2, active, PACK - 2, 2)
         res1 = result_tile("res1")
         banks1 = column_banks(operand)
-        z_third = rounded(READ, READ)
-        weave_shared(2, z_third, HALF)
-        unload(1, banks1, res1)
+        unload(banks1, res1, 0)
+        weave_shared(2, z_third, row_pairs[0])
+        unload(banks1, res1, 1)
+        store_chunk(1, res1)
+        round_from_psum(HALF, banks0[1])
 
         gather(3, active, 0, PACK - 2)
         operand = quantise(2 * READ, READ, z_third)
@@ -269,8 +282,6 @@ def tile_picked_pageread_silu_po_kernel(
             nc.scalar.copy(out=res2[:, pair, :], in_=multiply(operand, 0, READ, pair.start, 2)[:])
             nc.scalar.dma_start(out=out_planes[:, pair, 2 * READ : 3 * READ], in_=res2[:, pair, :])
         nc.scalar.copy(out=woven(rounded(2 * READ + HALF, HALF)), in_=planes(res2[:, :, HALF:]))
-
-        ends = (3 * READ, 3 * READ + HALF)
 
         codes = keep.tile([P, V], U32, name="codes", tag="active2", align_bytes=64)
 
@@ -286,16 +297,18 @@ def tile_picked_pageread_silu_po_kernel(
 
         hand_on(0, READ)
         store_words(0, READ)
+
+        ends = (3 * READ, 3 * READ + HALF)
         z_end = [keep.tile([P, PACK * HALF], BF16, name="z_end%d" % h, align_bytes=64) for h in range(2)]
         for h in range(2):
             nc.vector.tensor_copy(out=woven(z_end[h][:]), in_=planes(rows(3)[:, :, h * HALF : (h + 1) * HALF]))
         operands = [quantise(ends[h], HALF, z_end[h][:]) for h in range(2)]
         banks_end = [[multiply(operand, 0, HALF, pair.start, 2) for operand in operands] for pair in row_pairs]
+
         hand_on(READ, READ)
-        store_words(READ, READ)
         round_on_vector(2 * READ, res2[:, :, :HALF])
         hand_on(2 * READ, READ)
-        store_words(2 * READ, READ)
+        store_words(READ, 2 * READ)
 
         res3 = result_tile("res_end")
         for pair, pair_banks in zip(row_pairs, banks_end):

@@ -14,6 +14,7 @@ U8 = mybir.dt.uint8
 FP8X4 = mybir.dt.float8_e4m3fn_x4
 FP4X4 = mybir.dt.float4_e2m1fn_x4
 SILU = mybir.ActivationFunctionType.Silu
+COPY = mybir.ActivationFunctionType.Copy
 
 P = 128
 PACK = 4
@@ -24,6 +25,7 @@ BANKS = 8
 PICK = 256
 LEAD = 128
 CAST = 80
+WIDE = 512
 READ = 256
 HALF = READ // 2
 
@@ -67,12 +69,12 @@ def tile_picked_pageread_silu_po_kernel(
         mem_planes = mem.rearrange("(p t) u -> p t u", t=PACK)
         for t in range(2):
             nc.sync.dma_start(out=page[t][:], in_=mem_planes[:, t, :])
+        nc.sync.dma_start(rd_sb[:], rd)
         nc.sync.dma_start(out=w2_raw[:].bitcast(I32), in_=w2_words[0].bitcast(I32))
         for r in range(PACK):
             nc.sync.dma_start(out=scale_rows(w2_raw_bytes, r), in_=dram_scale_rows(w2_scales, r))
         for t in range(2, PACK):
             nc.sync.dma_start(out=page[t][:], in_=mem_planes[:, t, :])
-        nc.sync.dma_start(rd_sb[:], rd)
 
         w2_codes = keep.tile([P, 2 * N], U8, name="w2_codes", align_bytes=64)
         w2_bytes = keep.tile([P, N], U8, name="w2_bytes", align_bytes=64)
@@ -126,11 +128,9 @@ def tile_picked_pageread_silu_po_kernel(
             nc.scalar.copy(out=y[t][:, start : start + count], in_=acc[:])
 
         project(0, 0, LEAD)
-        for g in range(picks):
-            project(1, g * PICK, PICK)
         project(0, LEAD, PICK - LEAD)
         project(0, PICK, PICK)
-        for t in range(2, PACK):
+        for t in range(1, PACK):
             for g in range(picks):
                 project(t, g * PICK, PICK)
 
@@ -139,23 +139,16 @@ def tile_picked_pageread_silu_po_kernel(
                 out=page[t][:].indirect(entries(slot_sb, start, count)), in_=y[t][:, start : start + count]
             )
 
-        active = [keep.tile([P, U], F32, name="active%d" % t, align_bytes=64) for t in range(PACK)]
-
-        def activate_page(t):
-            nc.scalar.activation(out=active[t][:], in_=page[t][:], func=SILU)
-
         scatter(0, 0, LEAD)
-        scatter(1, 0, S)
-        activate_page(1)
         scatter(0, LEAD, S - LEAD)
-        activate_page(0)
-        for t in range(2, PACK):
+        for t in range(1, PACK):
             scatter(t, 0, S)
-            activate_page(t)
 
-        out_planes = out_0.rearrange("(p t) v -> p t v", t=PACK)
-        out_words = out_1[0].rearrange("p c r -> p (c r)").bitcast(I32)
-        out_bytes = keep.tile([P, READ], U8, name="out_bytes", align_bytes=64)
+        def read_on_scalar(dst, t, start, count):
+            nc.scalar.activation(out=dst, in_=page[t][:].indirect(entries(rd_sb, start, count)), func=COPY)
+
+        def side_by_side(ap):
+            return ap.rearrange("p (c t) -> p c t", t=PACK)
 
         def woven(ap):
             return ap.rearrange("p (c i t) -> p c t i", i=4, t=PACK)
@@ -163,163 +156,114 @@ def tile_picked_pageread_silu_po_kernel(
         def planes(ap):
             return ap.rearrange("p t (c i) -> p c t i", i=4)
 
-        def side_by_side(ap):
-            return ap.rearrange("p (c t) -> p c t", t=PACK)
+        chunks = V // READ
+        z = [keep.tile([P, PACK * READ], BF16, name="z%d" % c, align_bytes=64) for c in range(chunks)]
 
-        got_all = keep.tile([P, 2 * PACK + 1, READ], F32, name="got_all", align_bytes=64)
-        plane_rows = ((3, 4, 5, 6), (7, 8, 2, 3), (2, 3, 4, 5), (0, 1, 2, 3))
-        first_plane = (1, 0, 2, 0)
-        out_bf = keep.tile([P, PACK * V], BF16, name="out_bf", align_bytes=64)
-
-        def rows(c):
-            return got_all[:, plane_rows[c][0] : plane_rows[c][0] + PACK, :]
-
-        def pair_rows(c, pair):
-            return got_all[:, plane_rows[c][pair.start] : plane_rows[c][pair.start] + 2, :]
-
-        def gather(c, window, first, count):
-            for step in range(first, first + count):
-                t = (step + first_plane[c]) % PACK
-                nc.vector.tensor_copy(
-                    out=got_all[:, plane_rows[c][t], :], in_=window[t][:].indirect(entries(rd_sb, c * READ, READ))
-                )
-
-        def rounded(v0, width):
-            return out_bf[:, PACK * v0 : PACK * (v0 + width)]
-
-        def weave_on_gpsimd(dst, src, pair=slice(0, PACK)):
+        late = keep.tile([P, 2 * chunks - 1, READ], F32, name="late", tag="w1_codes", align_bytes=64)
+        early = keep.tile([P, 2, chunks, READ], F32, name="early", align_bytes=64)
+        for t in range(2):
+            read_on_scalar(late[:, 0:2, :].rearrange("p r c -> p (r c)"), t, 0, WIDE)
+            read_on_scalar(late[:, 3, :], t, 2 * READ, READ)
+            read_on_scalar(late[:, 5, :], t, 3 * READ, READ)
+            nc.scalar.activation(out=early[:, t, 0:2, :], in_=late[:, 0:2, :], func=SILU)
+            nc.scalar.activation(out=early[:, t, 2:4, :], in_=late[:, 3:6:2, :], func=SILU)
+        for c in range(chunks):
             nc.gpsimd.tensor_scalar(
-                out=side_by_side(dst)[:, :, pair],
-                in0=src.rearrange("p t c -> p c t"),
+                out=side_by_side(z[c][:])[:, :, row_pairs[0]],
+                in0=early[:, :, c, :].rearrange("p t c -> p c t"),
                 scalar1=1.0,
                 scalar2=-0.0,
                 op0=mybir.AluOpType.mult,
                 op1=mybir.AluOpType.add,
             )
 
-        def weave_shared(c, z_bf, pair):
-            src = pair_rows(c, pair)
-            nc.scalar.copy(out=woven(z_bf[:, PACK * HALF :])[:, :, pair], in_=planes(src[:, :, HALF:]))
-            weave_on_gpsimd(z_bf[:, : PACK * HALF], src[:, :, :HALF], pair)
+        late_row = (1, 3, 5, 0)
+        for c in (0, 3, 1, 2):
+            read_on_scalar(late[:, late_row[c], :], 2, c * READ, READ)
 
-        def quantise(v0, width, z_bf):
-            z_codes = keep.tile([P, width], U32, name="z_codes%d" % v0, align_bytes=64)
-            z_bytes = keep.tile([P, width], U8, name="z_bytes%d" % v0, align_bytes=64)
-            nc.vector.quantize_mx(out=z_codes[:].bitcast(FP8X4), scales=z_bytes[:], in_=z_bf)
-            return z_codes, z_bytes
+        def read_last(c):
+            nc.vector.tensor_copy(out=late[:, late_row[c] + 1, :], in_=page[3][:].indirect(entries(rd_sb, c * READ, READ)))
 
-        def multiply(operand, start, width, first, count):
-            z_codes, z_bytes = operand
-            acc = psum.tile([P, count, width], F32, name="acc", bufs=BANKS)
-            for e in range(count):
-                t = first + e
-                nc.tensor.matmul_mx(
-                    out=acc[:, e, :],
-                    lhsT=w2_codes[:, 2 * t * P : 2 * (t + 1) * P].bitcast(FP4X4),
-                    lhsT_scale=w2_bytes[:, t * P : (t + 1) * P],
-                    rhs=z_codes[:, start : start + width].bitcast(FP8X4),
-                    rhs_scale=z_bytes[:, start : start + width],
-                    start=True,
-                    stop=True,
-                )
-            return acc
+        def activate(c):
+            src = late[:, late_row[c] : late_row[c] + 2, :]
+            nc.scalar.activation(
+                out=side_by_side(z[c][:])[:, :, row_pairs[1]], in_=src.rearrange("p t c -> p c t"), func=SILU
+            )
 
-        def result_tile(name):
-            return keep.tile([P, PACK, READ], F32, name=name, align_bytes=64)
+        out_planes = out_0.rearrange("(p t) v -> p t v", t=PACK)
+        out_words = out_1[0].rearrange("p c r -> p (c r)").bitcast(I32)
+        out_bytes = keep.tile([P, READ], U8, name="out_bytes", align_bytes=64)
+        codes = keep.tile([P, V], U32, name="codes", align_bytes=64)
+        res = [keep.tile([P, PACK, READ], F32, name="res%d" % c, align_bytes=64) for c in range(chunks)]
+        rounded = [keep.tile([P, PACK * READ], BF16, name="rounded%d" % c, align_bytes=64) for c in range(chunks)]
 
-        def column_banks(operand):
-            return [multiply(operand, h * HALF, HALF, 0, PACK) for h in range(2)]
+        def multiply(c):
+            z_codes = keep.tile([P, READ], U32, name="z_codes%d" % c, align_bytes=64)
+            z_bytes = keep.tile([P, READ], U8, name="z_bytes%d" % c, align_bytes=64)
+            nc.vector.quantize_mx(out=z_codes[:].bitcast(FP8X4), scales=z_bytes[:], in_=z[c][:])
+            banks = []
+            for pair in row_pairs:
+                acc = psum.tile([P, 2, READ], F32, name="acc", bufs=BANKS)
+                for e in range(2):
+                    t = pair.start + e
+                    nc.tensor.matmul_mx(
+                        out=acc[:, e, :],
+                        lhsT=w2_codes[:, 2 * t * P : 2 * (t + 1) * P].bitcast(FP4X4),
+                        lhsT_scale=w2_bytes[:, t * P : (t + 1) * P],
+                        rhs=z_codes[:].bitcast(FP8X4),
+                        rhs_scale=z_bytes[:],
+                        start=True,
+                        stop=True,
+                    )
+                banks.append(acc)
+            return banks
 
-        def unload(banks, res, h):
-            nc.scalar.copy(out=res[:, :, h * HALF : (h + 1) * HALF], in_=banks[h][:])
+        def unload(c, banks, b, copy):
+            copy(out=res[c][:, row_pairs[b], :], in_=banks[b][:])
 
-        def store_chunk(c, res):
-            nc.sync.dma_start(out=out_planes[:, :, c * READ : (c + 1) * READ], in_=res[:])
+        def store(c, rows):
+            nc.sync.dma_start(out=out_planes[:, rows, c * READ : (c + 1) * READ], in_=res[c][:, rows, :])
 
-        def round_from_psum(v0, bank):
-            nc.scalar.copy(out=side_by_side(rounded(v0, HALF)), in_=bank[:].rearrange("p t c -> p c t"))
+        def round_chunk(c):
+            nc.vector.tensor_copy(out=woven(rounded[c][:]), in_=planes(res[c][:]))
 
-        def round_on_vector(v0, src):
-            nc.vector.tensor_copy(out=woven(rounded(v0, HALF)), in_=planes(src))
-
-        gather(0, page, 0, PACK)
-        z_first = keep.tile([P, PACK * READ], BF16, name="z_first", align_bytes=64)
-        nc.scalar.activation(out=woven(z_first[:]), in_=planes(rows(0)), func=SILU)
-
-        gather(1, active, 0, PACK - 1)
-        z_second = got_all[:, 0:2, :].rearrange("p r c -> p (r c)").bitcast(BF16)
-        nc.scalar.copy(out=woven(z_second)[:, :, row_pairs[0]], in_=planes(pair_rows(1, row_pairs[0])))
-        operand = quantise(0, READ, z_first[:])
-        gather(1, active, PACK - 1, 1)
-        res0 = result_tile("res0")
-        banks0 = column_banks(operand)
-        weave_shared(1, z_second, row_pairs[1])
-        for h in range(2):
-            unload(banks0, res0, h)
-        store_chunk(0, res0)
-        round_from_psum(0, banks0[0])
-
-        gather(2, active, 0, PACK - 2)
-        operand = quantise(READ, READ, z_second)
-        z_third = rounded(READ, READ)
-        weave_on_gpsimd(z_third, pair_rows(2, row_pairs[1]), row_pairs[1])
-        gather(2, active, PACK - 2, 2)
-        res1 = result_tile("res1")
-        banks1 = column_banks(operand)
-        unload(banks1, res1, 0)
-        weave_shared(2, z_third, row_pairs[0])
-        unload(banks1, res1, 1)
-        store_chunk(1, res1)
-        round_from_psum(HALF, banks0[1])
-
-        gather(3, active, 0, PACK - 2)
-        operand = quantise(2 * READ, READ, z_third)
-        weave_on_gpsimd(rounded(READ, HALF), res1[:, :, :HALF])
-        round_from_psum(READ + HALF, banks1[1])
-        gather(3, active, PACK - 2, 2)
-        res2 = result_tile("res2")
-        for pair in row_pairs:
-            nc.scalar.copy(out=res2[:, pair, :], in_=multiply(operand, 0, READ, pair.start, 2)[:])
-            nc.scalar.dma_start(out=out_planes[:, pair, 2 * READ : 3 * READ], in_=res2[:, pair, :])
-        nc.scalar.copy(out=woven(rounded(2 * READ + HALF, HALF)), in_=planes(res2[:, :, HALF:]))
-
-        codes = keep.tile([P, V], U32, name="codes", tag="active2", align_bytes=64)
-
-        def hand_on(v0, width):
+        def hand_on(c):
             nc.vector.quantize_mx(
-                out=codes[:, v0 : v0 + width].bitcast(FP8X4),
-                scales=out_bytes[PACK * (v0 // READ) :, v0 % READ : v0 % READ + width],
-                in_=rounded(v0, width),
+                out=codes[:, c * READ : (c + 1) * READ].bitcast(FP8X4), scales=out_bytes[PACK * c :, :], in_=rounded[c][:]
             )
 
         def store_words(v0, width):
             nc.sync.dma_start(out=out_words[:, v0 : v0 + width], in_=codes[:, v0 : v0 + width].bitcast(I32))
 
-        hand_on(0, READ)
-        store_words(0, READ)
-
-        ends = (3 * READ, 3 * READ + HALF)
-        z_end = [keep.tile([P, PACK * HALF], BF16, name="z_end%d" % h, align_bytes=64) for h in range(2)]
-        for h in range(2):
-            nc.vector.tensor_copy(out=woven(z_end[h][:]), in_=planes(rows(3)[:, :, h * HALF : (h + 1) * HALF]))
-        operands = [quantise(ends[h], HALF, z_end[h][:]) for h in range(2)]
-        banks_end = [[multiply(operand, 0, HALF, pair.start, 2) for operand in operands] for pair in row_pairs]
-
-        hand_on(READ, READ)
-        round_on_vector(2 * READ, res2[:, :, :HALF])
-        hand_on(2 * READ, READ)
-        store_words(READ, 2 * READ)
-
-        res3 = result_tile("res_end")
-        for pair, pair_banks in zip(row_pairs, banks_end):
-            for h in range(2):
-                nc.scalar.copy(out=res3[:, pair, h * HALF : (h + 1) * HALF], in_=pair_banks[h][:])
-            nc.sync.dma_start(out=out_planes[:, pair, ends[0] :], in_=res3[:, pair, :])
-        for h in range(2):
-            round_on_vector(ends[h], res3[:, :, h * HALF : (h + 1) * HALF])
-        for v0 in ends:
-            hand_on(v0, HALF)
-        store_words(ends[0], READ)
+        for c in range(chunks - 1):
+            read_last(c)
+        activate(0)
+        banks = [multiply(0)]
+        read_last(3)
+        activate(1)
+        banks.append(multiply(1))
+        activate(2)
+        activate(3)
+        unload(0, banks[0], 0, nc.vector.tensor_copy)
+        store(0, row_pairs[0])
+        banks.append(multiply(2))
+        unload(0, banks[0], 1, nc.vector.tensor_copy)
+        store(0, row_pairs[1])
+        banks.append(multiply(3))
+        for c in range(1, chunks):
+            for b in range(2):
+                unload(c, banks[c], b, nc.scalar.copy)
+                store(c, row_pairs[b])
+        round_chunk(0)
+        round_chunk(1)
+        hand_on(0)
+        round_chunk(2)
+        hand_on(1)
+        store_words(0, 2 * READ)
+        round_chunk(3)
+        hand_on(2)
+        hand_on(3)
+        store_words(2 * READ, 2 * READ)
 
         for q in range(PACK):
             queue = nc.sync if q % 2 == 0 else nc.scalar

@@ -87,20 +87,23 @@ def tile_picked_pageread_silu_po_kernel(
             in_=w2_raw_bytes[:].rearrange("p (m t) -> p t m", t=PACK),
         )
 
-        picks = S // PICK
-        picked_bytes = [keep.tile([P, PICK], U8, name="picked_bytes%d" % g, align_bytes=64) for g in range(picks)]
-        picked_codes = [keep.tile([P, PICK], U32, name="picked_codes%d" % g, align_bytes=64) for g in range(picks)]
+        picked_bytes = keep.tile([P, S], U8, name="picked_bytes", align_bytes=64)
+        picked_codes = keep.tile([P, S], U32, name="picked_codes", align_bytes=64)
 
         def entries(lst, start, count):
             return lst[:, start // PER_COL : (start + count) // PER_COL]
 
-        for g in range(picks):
-            nc.vector.tensor_copy(out=picked_bytes[g][:], in_=x_bytes[:].indirect(entries(offs_sb, g * PICK, PICK)))
+        for start in range(0, S, PICK):
+            nc.vector.tensor_copy(
+                out=picked_bytes[:, start : start + PICK], in_=x_bytes[:].indirect(entries(offs_sb, start, PICK))
+            )
 
         w1_bf = keep.tile([P, PACK * H], BF16, name="w1_bf", align_bytes=64)
         w1_dst = w1_bf[:].rearrange("p (t m j) -> p m j t", t=PACK, j=PACK)
         w1_src = w1_raw[:].rearrange("p j (m t) -> p m j t", t=PACK)
         nc.vector.tensor_copy(out=w1_dst[:, :CAST], in_=w1_src[:, :CAST])
+        warm = keep.tile([P, 1], F32, name="warm")
+        nc.scalar.activation(out=warm[:], in_=w1_raw[:, 0, 0:1], func=SILU)
         for pair in row_pairs:
             nc.scalar.copy(out=w1_dst[:, CAST:, pair], in_=w1_src[:, CAST:, pair])
 
@@ -108,31 +111,32 @@ def tile_picked_pageread_silu_po_kernel(
         w1_bytes = keep.tile([P, H], U8, name="w1_bytes", align_bytes=64)
         nc.vector.quantize_mx(out=w1_codes[:].bitcast(FP8X4), scales=w1_bytes[:], in_=w1_bf[:])
 
-        for g in range(picks):
-            nc.vector.tensor_copy(out=picked_codes[g][:], in_=x_codes[:].indirect(entries(offs_sb, g * PICK, PICK)))
+        pieces = ((0, LEAD), (LEAD, PICK), (LEAD + PICK, LEAD))
+        for start, count in pieces:
+            nc.vector.tensor_copy(
+                out=picked_codes[:, start : start + count], in_=x_codes[:].indirect(entries(offs_sb, start, count))
+            )
 
         y = [keep.tile([P, S], F32, name="y%d" % t, align_bytes=64) for t in range(PACK)]
 
         def project(t, start, count):
-            g, cols, tokens = start // PICK, slice(t * P, (t + 1) * P), slice(start % PICK, start % PICK + count)
+            cols, tokens = slice(t * P, (t + 1) * P), slice(start, start + count)
             acc = psum.tile([P, count], F32, name="acc", bufs=BANKS)
             nc.tensor.matmul_mx(
                 out=acc[:],
                 lhsT=w1_codes[:, cols].bitcast(FP8X4),
                 lhsT_scale=w1_bytes[:, cols],
-                rhs=picked_codes[g][:, tokens].bitcast(FP8X4),
-                rhs_scale=picked_bytes[g][:, tokens],
+                rhs=picked_codes[:, tokens].bitcast(FP8X4),
+                rhs_scale=picked_bytes[:, tokens],
                 start=True,
                 stop=True,
             )
             nc.scalar.copy(out=y[t][:, start : start + count], in_=acc[:])
 
-        project(0, 0, LEAD)
-        project(0, LEAD, PICK - LEAD)
-        project(0, PICK, PICK)
+        for start, count in pieces:
+            project(0, start, count)
         for t in range(1, PACK):
-            for g in range(picks):
-                project(t, g * PICK, PICK)
+            project(t, 0, S)
 
         def scatter(t, start, count):
             nc.vector.tensor_copy(
@@ -144,8 +148,8 @@ def tile_picked_pageread_silu_po_kernel(
         for t in range(1, PACK):
             scatter(t, 0, S)
 
-        def read_on_scalar(dst, t, start, count):
-            nc.scalar.activation(out=dst, in_=page[t][:].indirect(entries(rd_sb, start, count)), func=COPY)
+        def read_on_scalar(dst, window, start, count):
+            nc.scalar.activation(out=dst, in_=window[:].indirect(entries(rd_sb, start, count)), func=COPY)
 
         def side_by_side(ap):
             return ap.rearrange("p (c t) -> p c t", t=PACK)
@@ -157,37 +161,36 @@ def tile_picked_pageread_silu_po_kernel(
             return ap.rearrange("p t (c i) -> p c t i", i=4)
 
         chunks = V // READ
-        z = [keep.tile([P, PACK * READ], BF16, name="z%d" % c, align_bytes=64) for c in range(chunks)]
-
-        late = keep.tile([P, 2 * chunks - 1, READ], F32, name="late", tag="w1_codes", align_bytes=64)
-        early = keep.tile([P, 2, chunks, READ], F32, name="early", align_bytes=64)
+        holders = ("w1_codes", "picked_codes", "w1_bytes", "picked_bytes")
+        late = [keep.tile([P, 2 * READ], F32, name="late%d" % c, tag=holders[c], align_bytes=64) for c in range(chunks)]
+        z = [keep.tile([P, PACK * READ], BF16, name="z%d" % c, align_bytes=64)[:] for c in range(chunks)]
+        early = [keep.tile([P, 2, WIDE], F32, name="early%d" % h, align_bytes=64) for h in range(2)]
         for t in range(2):
-            read_on_scalar(late[:, 0:2, :].rearrange("p r c -> p (r c)"), t, 0, WIDE)
-            read_on_scalar(late[:, 3, :], t, 2 * READ, READ)
-            read_on_scalar(late[:, 5, :], t, 3 * READ, READ)
-            nc.scalar.activation(out=early[:, t, 0:2, :], in_=late[:, 0:2, :], func=SILU)
-            nc.scalar.activation(out=early[:, t, 2:4, :], in_=late[:, 3:6:2, :], func=SILU)
+            for h in range(2):
+                read_on_scalar(late[h][:], page[t], h * WIDE, WIDE)
+            for h in range(2):
+                nc.scalar.activation(out=early[h][:, t, :], in_=late[h][:], func=SILU)
         for c in range(chunks):
             nc.gpsimd.tensor_scalar(
-                out=side_by_side(z[c][:])[:, :, row_pairs[0]],
-                in0=early[:, :, c, :].rearrange("p t c -> p c t"),
+                out=side_by_side(z[c])[:, :, row_pairs[0]],
+                in0=early[c // 2][:, :, c % 2 * READ : (c % 2 + 1) * READ].rearrange("p t c -> p c t"),
                 scalar1=1.0,
                 scalar2=-0.0,
                 op0=mybir.AluOpType.mult,
                 op1=mybir.AluOpType.add,
             )
-
-        late_row = (1, 3, 5, 0)
-        for c in (0, 3, 1, 2):
-            read_on_scalar(late[:, late_row[c], :], 2, c * READ, READ)
+        for c in range(chunks):
+            read_on_scalar(late[c][:, :READ], page[2], c * READ, READ)
 
         def read_last(c):
-            nc.vector.tensor_copy(out=late[:, late_row[c] + 1, :], in_=page[3][:].indirect(entries(rd_sb, c * READ, READ)))
+            nc.vector.tensor_copy(out=late[c][:, READ : 2 * READ], in_=page[3][:].indirect(entries(rd_sb, c * READ, READ)))
 
-        def activate(c):
-            src = late[:, late_row[c] : late_row[c] + 2, :]
+        def activate(c, start, width):
+            src = late[c][:, : 2 * READ].rearrange("p (t c) -> p c t", t=2)
             nc.scalar.activation(
-                out=side_by_side(z[c][:])[:, :, row_pairs[1]], in_=src.rearrange("p t c -> p c t"), func=SILU
+                out=side_by_side(z[c])[:, start : start + width, row_pairs[1]],
+                in_=src[:, start : start + width, :],
+                func=SILU,
             )
 
         out_planes = out_0.rearrange("(p t) v -> p t v", t=PACK)
@@ -197,35 +200,35 @@ def tile_picked_pageread_silu_po_kernel(
         res = [keep.tile([P, PACK, READ], F32, name="res%d" % c, align_bytes=64) for c in range(chunks)]
         rounded = [keep.tile([P, PACK * READ], BF16, name="rounded%d" % c, align_bytes=64) for c in range(chunks)]
 
-        def multiply(c):
-            z_codes = keep.tile([P, READ], U32, name="z_codes%d" % c, align_bytes=64)
-            z_bytes = keep.tile([P, READ], U8, name="z_bytes%d" % c, align_bytes=64)
-            nc.vector.quantize_mx(out=z_codes[:].bitcast(FP8X4), scales=z_bytes[:], in_=z[c][:])
+        def multiply(c, blocks):
+            z_codes = keep.tile([P, READ], U32, name="z_codes", bufs=2, align_bytes=64)
+            z_bytes = keep.tile([P, READ], U8, name="z_bytes", bufs=2, align_bytes=64)
+            nc.vector.quantize_mx(out=z_codes[:].bitcast(FP8X4), scales=z_bytes[:], in_=z[c])
             banks = []
-            for pair in row_pairs:
-                acc = psum.tile([P, 2, READ], F32, name="acc", bufs=BANKS)
-                for e in range(2):
-                    t = pair.start + e
+            for rows, cols in blocks:
+                acc = psum.tile([P, rows.stop - rows.start, cols.stop - cols.start], F32, name="acc", bufs=BANKS)
+                for e, t in enumerate(range(rows.start, rows.stop)):
                     nc.tensor.matmul_mx(
                         out=acc[:, e, :],
                         lhsT=w2_codes[:, 2 * t * P : 2 * (t + 1) * P].bitcast(FP4X4),
                         lhsT_scale=w2_bytes[:, t * P : (t + 1) * P],
-                        rhs=z_codes[:].bitcast(FP8X4),
-                        rhs_scale=z_bytes[:],
+                        rhs=z_codes[:, cols].bitcast(FP8X4),
+                        rhs_scale=z_bytes[:, cols],
                         start=True,
                         stop=True,
                     )
-                banks.append(acc)
+                banks.append((rows, cols, acc))
             return banks
 
-        def unload(c, banks, b, copy):
-            copy(out=res[c][:, row_pairs[b], :], in_=banks[b][:])
+        def unload(c, bank, copy):
+            rows, cols, acc = bank
+            copy(out=res[c][:, rows, cols], in_=acc[:])
 
-        def store(c, rows):
-            nc.sync.dma_start(out=out_planes[:, rows, c * READ : (c + 1) * READ], in_=res[c][:, rows, :])
+        def store(c, rows, cols):
+            nc.sync.dma_start(out=out_planes[:, rows, c * READ : (c + 1) * READ][:, :, cols], in_=res[c][:, rows, cols])
 
-        def round_chunk(c):
-            nc.vector.tensor_copy(out=woven(rounded[c][:]), in_=planes(res[c][:]))
+        def round_columns(c, start, width, copy):
+            copy(out=woven(rounded[c][:, PACK * start : PACK * (start + width)]), in_=planes(res[c][:, :, start : start + width]))
 
         def hand_on(c):
             nc.vector.quantize_mx(
@@ -235,35 +238,45 @@ def tile_picked_pageread_silu_po_kernel(
         def store_words(v0, width):
             nc.sync.dma_start(out=out_words[:, v0 : v0 + width], in_=codes[:, v0 : v0 + width].bitcast(I32))
 
-        for c in range(chunks - 1):
+        read_on_scalar(late[2][:, READ:], page[3], 2 * READ, READ)
+        for c in (0, 1, 3):
             read_last(c)
-        activate(0)
-        banks = [multiply(0)]
-        read_last(3)
-        activate(1)
-        banks.append(multiply(1))
-        activate(2)
-        activate(3)
-        unload(0, banks[0], 0, nc.vector.tensor_copy)
-        store(0, row_pairs[0])
-        banks.append(multiply(2))
-        unload(0, banks[0], 1, nc.vector.tensor_copy)
-        store(0, row_pairs[1])
-        banks.append(multiply(3))
-        for c in range(1, chunks):
-            for b in range(2):
-                unload(c, banks[c], b, nc.scalar.copy)
-                store(c, row_pairs[b])
-        round_chunk(0)
-        round_chunk(1)
+        for c in range(chunks):
+            activate(c, 0, READ)
+        whole = slice(0, READ)
+        by_plane = [(slice(t, t + 1), whole) for t in range(PACK)]
+        by_pair = [(pair, whole) for pair in row_pairs]
+        by_half = [(slice(0, PACK), slice(start, start + HALF)) for start in (0, HALF)]
+
+        def unload_planes(c, banks, copy):
+            for pair in row_pairs:
+                for bank in banks[pair]:
+                    unload(c, bank, copy)
+                store(c, pair, whole)
+
+        banks = [multiply(0, by_plane), multiply(1, by_plane)]
+        unload_planes(0, banks[0], nc.vector.tensor_copy)
+        banks.extend((multiply(2, by_pair), multiply(3, by_half)))
+        unload_planes(1, banks[1], nc.scalar.copy)
+        for bank in banks[2]:
+            unload(2, bank, nc.scalar.copy)
+            store(2, bank[0], whole)
+        unload(3, banks[3][0], nc.scalar.copy)
+        store(3, *by_half[0])
+        nc.scalar.copy(out=side_by_side(rounded[3][:, PACK * HALF :]), in_=banks[3][1][2][:].rearrange("p t c -> p c t"))
+        unload(3, banks[3][1], nc.scalar.copy)
+        round_columns(0, 0, READ, nc.vector.tensor_copy)
+        round_columns(1, 0, READ, nc.vector.tensor_copy)
         hand_on(0)
-        round_chunk(2)
         hand_on(1)
         store_words(0, 2 * READ)
-        round_chunk(3)
+        round_columns(2, 0, READ, nc.vector.tensor_copy)
+        round_columns(3, 0, HALF, nc.vector.tensor_copy)
         hand_on(2)
+        store_words(2 * READ, READ)
+        store(3, *by_half[1])
         hand_on(3)
-        store_words(2 * READ, 2 * READ)
+        store_words(3 * READ, READ)
 
         for q in range(PACK):
             queue = nc.sync if q % 2 == 0 else nc.scalar

@@ -161,26 +161,46 @@ def tile_picked_pageread_silu_po_kernel(
             return ap.rearrange("p t (c i) -> p c t i", i=4)
 
         chunks = V // READ
-        holders = ("w1_codes", "picked_codes", "w1_bytes", "picked_bytes")
-        late = [keep.tile([P, 2 * READ], F32, name="late%d" % c, tag=holders[c], align_bytes=64) for c in range(chunks)]
-        z = [keep.tile([P, PACK * READ], BF16, name="z%d" % c, align_bytes=64)[:] for c in range(chunks)]
+        holders = ("w1_codes", "picked_codes", "w1_bytes")
+        late = [keep.tile([P, 2 * READ], F32, name="late%d" % c, tag=holders[c], align_bytes=64) for c in range(3)]
+        late.append(keep.tile([P, 3 * READ], F32, name="late3", tag="picked_bytes", align_bytes=64))
+        z = [late[3][:, READ:].bitcast(BF16)]
+        z.extend(keep.tile([P, PACK * READ], BF16, name="z%d" % c, align_bytes=64)[:] for c in range(1, chunks))
         early = [keep.tile([P, 2, WIDE], F32, name="early%d" % h, align_bytes=64) for h in range(2)]
-        for t in range(2):
-            for h in range(2):
-                read_on_scalar(late[h][:], page[t], h * WIDE, WIDE)
-            for h in range(2):
-                nc.scalar.activation(out=early[h][:, t, :], in_=late[h][:], func=SILU)
-        for c in range(chunks):
-            nc.gpsimd.tensor_scalar(
-                out=side_by_side(z[c])[:, :, row_pairs[0]],
-                in0=early[c // 2][:, :, c % 2 * READ : (c % 2 + 1) * READ].rearrange("p t c -> p c t"),
-                scalar1=1.0,
-                scalar2=-0.0,
-                op0=mybir.AluOpType.mult,
-                op1=mybir.AluOpType.add,
-            )
-        for c in range(chunks):
+
+        def read_early(t, h):
+            read_on_scalar(late[(2 * t + h) % 3][:], page[t], h * WIDE, WIDE)
+
+        def activate_early(t, h):
+            nc.scalar.activation(out=early[h][:, t, :], in_=late[(2 * t + h) % 3][:], func=SILU)
+
+        def weave_early(h):
+            for c in (2 * h, 2 * h + 1):
+                nc.gpsimd.tensor_scalar(
+                    out=side_by_side(z[c])[:, :, row_pairs[0]],
+                    in0=early[h][:, :, c % 2 * READ : (c % 2 + 1) * READ].rearrange("p t c -> p c t"),
+                    scalar1=1.0,
+                    scalar2=-0.0,
+                    op0=mybir.AluOpType.mult,
+                    op1=mybir.AluOpType.add,
+                )
+
+        def read_third(c):
             read_on_scalar(late[c][:, :READ], page[2], c * READ, READ)
+
+        read_early(0, 0)
+        read_early(0, 1)
+        activate_early(0, 0)
+        read_early(1, 0)
+        activate_early(0, 1)
+        activate_early(1, 0)
+        weave_early(0)
+        read_early(1, 1)
+        read_third(1)
+        activate_early(1, 1)
+        weave_early(1)
+        for c in (2, 0, 3):
+            read_third(c)
 
         def read_last(c):
             nc.vector.tensor_copy(out=late[c][:, READ : 2 * READ], in_=page[3][:].indirect(entries(rd_sb, c * READ, READ)))
@@ -197,38 +217,52 @@ def tile_picked_pageread_silu_po_kernel(
         out_words = out_1[0].rearrange("p c r -> p (c r)").bitcast(I32)
         out_bytes = keep.tile([P, READ], U8, name="out_bytes", align_bytes=64)
         codes = keep.tile([P, V], U32, name="codes", align_bytes=64)
-        res = [keep.tile([P, PACK, READ], F32, name="res%d" % c, align_bytes=64) for c in range(chunks)]
+        res = [keep.tile([P, PACK, width], F32, name="res%d" % v0, align_bytes=64) for v0, width in ((0, READ), (READ, READ), (WIDE, WIDE))]
         rounded = [keep.tile([P, PACK * READ], BF16, name="rounded%d" % c, align_bytes=64) for c in range(chunks)]
 
-        def multiply(c, blocks):
-            z_codes = keep.tile([P, READ], U32, name="z_codes", bufs=2, align_bytes=64)
-            z_bytes = keep.tile([P, READ], U8, name="z_bytes", bufs=2, align_bytes=64)
-            nc.vector.quantize_mx(out=z_codes[:].bitcast(FP8X4), scales=z_bytes[:], in_=z[c])
+        def operand(width, tag):
+            return (
+                keep.tile([P, width], U32, name="z_codes", tag="z_codes" + tag, align_bytes=64),
+                keep.tile([P, width], U8, name="z_bytes", tag="z_bytes" + tag, align_bytes=64),
+            )
+
+        def quantise(c, tiles, start):
+            z_codes, z_bytes = tiles
+            nc.vector.quantize_mx(
+                out=z_codes[:, start : start + READ].bitcast(FP8X4), scales=z_bytes[:, start : start + READ], in_=z[c]
+            )
+
+        def multiply(tiles, width):
+            z_codes, z_bytes = tiles
             banks = []
-            for rows, cols in blocks:
-                acc = psum.tile([P, rows.stop - rows.start, cols.stop - cols.start], F32, name="acc", bufs=BANKS)
-                for e, t in enumerate(range(rows.start, rows.stop)):
-                    nc.tensor.matmul_mx(
-                        out=acc[:, e, :],
-                        lhsT=w2_codes[:, 2 * t * P : 2 * (t + 1) * P].bitcast(FP4X4),
-                        lhsT_scale=w2_bytes[:, t * P : (t + 1) * P],
-                        rhs=z_codes[:, cols].bitcast(FP8X4),
-                        rhs_scale=z_bytes[:, cols],
-                        start=True,
-                        stop=True,
-                    )
-                banks.append((rows, cols, acc))
+            for t in range(PACK):
+                acc = psum.tile([P, width], F32, name="acc", bufs=BANKS)
+                nc.tensor.matmul_mx(
+                    out=acc[:],
+                    lhsT=w2_codes[:, 2 * t * P : 2 * (t + 1) * P].bitcast(FP4X4),
+                    lhsT_scale=w2_bytes[:, t * P : (t + 1) * P],
+                    rhs=z_codes[:].bitcast(FP8X4),
+                    rhs_scale=z_bytes[:],
+                    start=True,
+                    stop=True,
+                )
+                banks.append(acc)
             return banks
 
-        def unload(c, bank, copy):
-            rows, cols, acc = bank
-            copy(out=res[c][:, rows, cols], in_=acc[:])
+        def unload_pairs(c, banks, copy):
+            for pair in row_pairs:
+                for t in range(pair.start, pair.stop):
+                    copy(out=res[c][:, t, :], in_=banks[t][:])
+                nc.sync.dma_start(out=out_planes[:, pair, c * READ : (c + 1) * READ], in_=res[c][:, pair, :])
 
-        def store(c, rows, cols):
-            nc.sync.dma_start(out=out_planes[:, rows, c * READ : (c + 1) * READ][:, :, cols], in_=res[c][:, rows, cols])
+        def unload_plane(t, banks, copy):
+            copy(out=res[2][:, t, :], in_=banks[t][:])
+            nc.sync.dma_start(out=out_planes[:, t, WIDE:], in_=res[2][:, t, :])
 
-        def round_columns(c, start, width, copy):
-            copy(out=woven(rounded[c][:, PACK * start : PACK * (start + width)]), in_=planes(res[c][:, :, start : start + width]))
+        def round_columns(v0, width, copy):
+            c, start = v0 // READ, v0 % READ
+            src = res[c][:, :, start : start + width] if c < 2 else res[2][:, :, v0 - WIDE : v0 - WIDE + width]
+            copy(out=woven(rounded[c][:, PACK * start : PACK * (start + width)]), in_=planes(src))
 
         def hand_on(c):
             nc.vector.quantize_mx(
@@ -238,45 +272,39 @@ def tile_picked_pageread_silu_po_kernel(
         def store_words(v0, width):
             nc.sync.dma_start(out=out_words[:, v0 : v0 + width], in_=codes[:, v0 : v0 + width].bitcast(I32))
 
-        read_on_scalar(late[2][:, READ:], page[3], 2 * READ, READ)
-        for c in (0, 1, 3):
+        for c in range(3):
             read_last(c)
-        for c in range(chunks):
+        activate(0, 0, READ)
+        first = operand(READ, "a")
+        quantise(0, first, 0)
+        banks0 = multiply(first, READ)
+        read_last(3)
+        for c in range(1, chunks):
             activate(c, 0, READ)
-        whole = slice(0, READ)
-        by_plane = [(slice(t, t + 1), whole) for t in range(PACK)]
-        by_pair = [(pair, whole) for pair in row_pairs]
-        by_half = [(slice(0, PACK), slice(start, start + HALF)) for start in (0, HALF)]
-
-        def unload_planes(c, banks, copy):
-            for pair in row_pairs:
-                for bank in banks[pair]:
-                    unload(c, bank, copy)
-                store(c, pair, whole)
-
-        banks = [multiply(0, by_plane), multiply(1, by_plane)]
-        unload_planes(0, banks[0], nc.vector.tensor_copy)
-        banks.extend((multiply(2, by_pair), multiply(3, by_half)))
-        unload_planes(1, banks[1], nc.scalar.copy)
-        for bank in banks[2]:
-            unload(2, bank, nc.scalar.copy)
-            store(2, bank[0], whole)
-        unload(3, banks[3][0], nc.scalar.copy)
-        store(3, *by_half[0])
-        nc.scalar.copy(out=side_by_side(rounded[3][:, PACK * HALF :]), in_=banks[3][1][2][:].rearrange("p t c -> p c t"))
-        unload(3, banks[3][1], nc.scalar.copy)
-        round_columns(0, 0, READ, nc.vector.tensor_copy)
-        round_columns(1, 0, READ, nc.vector.tensor_copy)
+        second = operand(READ, "b")
+        quantise(1, second, 0)
+        banks1 = multiply(second, READ)
+        unload_pairs(0, banks0, nc.vector.tensor_copy)
+        third = operand(WIDE, "a")
+        quantise(2, third, 0)
+        quantise(3, third, READ)
+        banks2 = multiply(third, WIDE)
+        unload_pairs(1, banks1, nc.scalar.copy)
+        round_columns(0, READ, nc.vector.tensor_copy)
+        round_columns(READ, READ, nc.vector.tensor_copy)
+        unload_plane(0, banks2, nc.scalar.copy)
+        unload_plane(1, banks2, nc.vector.tensor_copy)
+        unload_plane(2, banks2, nc.scalar.copy)
+        unload_plane(3, banks2, nc.scalar.copy)
         hand_on(0)
         hand_on(1)
-        store_words(0, 2 * READ)
-        round_columns(2, 0, READ, nc.vector.tensor_copy)
-        round_columns(3, 0, HALF, nc.vector.tensor_copy)
-        hand_on(2)
-        store_words(2 * READ, READ)
-        store(3, *by_half[1])
+        store_words(0, WIDE)
+        round_columns(2 * READ, HALF, nc.scalar.copy)
+        round_columns(3 * READ, READ, nc.vector.tensor_copy)
+        round_columns(2 * READ + HALF, HALF, nc.vector.tensor_copy)
         hand_on(3)
-        store_words(3 * READ, READ)
+        hand_on(2)
+        store_words(WIDE, WIDE)
 
         for q in range(PACK):
             queue = nc.sync if q % 2 == 0 else nc.scalar

@@ -20,6 +20,7 @@ P = 128
 PACK = 4
 QUADRANT = 32
 SCALE_ROWS = 16
+SPREAD = 8
 PER_COL = 16
 BANKS = 8
 PICK = 256
@@ -27,6 +28,7 @@ LEAD = 128
 CAST = 80
 WIDE = 512
 READ = 256
+NEAR = 64
 HALF = READ // 2
 
 
@@ -43,60 +45,44 @@ def tile_picked_pageread_silu_po_kernel(
         rd_sb = keep.tile([P, V // PER_COL], U16, name="rd_sb")
         x_codes = keep.tile([P, T], U32, name="x_codes", align_bytes=64)
         x_bytes = keep.tile([P, T], U8, name="x_bytes", align_bytes=64)
-        w2_raw = keep.tile([P, 2 * N], U8, name="w2_raw", align_bytes=64)
-        w2_raw_bytes = keep.tile([P, N], U8, name="w2_raw_bytes", align_bytes=64)
         w1_raw = keep.tile([P, PACK, H], F32, name="w1_raw", align_bytes=64)
-        page = [keep.tile([P, U], F32, name="page%d" % t, align_bytes=64) for t in range(PACK)]
-
-        def scale_rows(tile, r):
-            return tile[r:P:QUADRANT, :].bitcast(I32)
-
-        def dram_scale_rows(scales, r):
-            return scales[0, r:SCALE_ROWS:PACK, :].bitcast(I32)
-
-        nc.vector.memset(x_bytes[:].bitcast(I32), 0)
-        nc.vector.memset(w2_raw_bytes[:].bitcast(I32), 0)
-
-        row_pairs = (slice(0, 2), slice(2, PACK))
-        w1_rows = w1.rearrange("(p j) c -> p j c", j=PACK)
-        nc.sync.dma_start(out=w1_raw[:, row_pairs[0], :], in_=w1_rows[:, row_pairs[0], :])
-        nc.sync.dma_start(offs_sb[:], offs)
-        for r in range(PACK):
-            nc.sync.dma_start(out=scale_rows(x_bytes, r), in_=dram_scale_rows(x_scales, r))
-        nc.sync.dma_start(out=w1_raw[:, row_pairs[1], :], in_=w1_rows[:, row_pairs[1], :])
-        nc.sync.dma_start(out=x_codes[:].bitcast(I32), in_=x_words[0].rearrange("p c r -> p (c r)").bitcast(I32))
-        nc.sync.dma_start(slot_sb[:], slot)
-        mem_planes = mem.rearrange("(p t) u -> p t u", t=PACK)
-        for t in range(2):
-            nc.sync.dma_start(out=page[t][:], in_=mem_planes[:, t, :])
-        nc.sync.dma_start(rd_sb[:], rd)
-        nc.sync.dma_start(out=w2_raw[:].bitcast(I32), in_=w2_words[0].bitcast(I32))
-        for r in range(PACK):
-            nc.sync.dma_start(out=scale_rows(w2_raw_bytes, r), in_=dram_scale_rows(w2_scales, r))
-        for t in range(2, PACK):
-            nc.sync.dma_start(out=page[t][:], in_=mem_planes[:, t, :])
-
-        w2_codes = keep.tile([P, 2 * N], U8, name="w2_codes", align_bytes=64)
-        w2_bytes = keep.tile([P, N], U8, name="w2_bytes", align_bytes=64)
-        nc.gpsimd.tensor_copy(
-            out=w2_codes[:].rearrange("p (t m b) -> p t m b", t=PACK, b=2),
-            in_=w2_raw[:].rearrange("p (m t b) -> p t m b", t=PACK, b=2),
-        )
-        nc.gpsimd.tensor_copy(
-            out=w2_bytes[:].rearrange("p (t m) -> p t m", t=PACK),
-            in_=w2_raw_bytes[:].rearrange("p (m t) -> p t m", t=PACK),
-        )
-
+        spread_bytes = keep.tile([P, S], U8, name="spread_bytes", align_bytes=64)
         picked_bytes = keep.tile([P, S], U8, name="picked_bytes", align_bytes=64)
         picked_codes = keep.tile([P, S], U32, name="picked_codes", align_bytes=64)
+
+        def scale_rows(ap, r):
+            return ap[r:P:QUADRANT, :].bitcast(I32)
 
         def entries(lst, start, count):
             return lst[:, start // PER_COL : (start + count) // PER_COL]
 
-        for start in range(0, S, PICK):
-            nc.vector.tensor_copy(
-                out=picked_bytes[:, start : start + PICK], in_=x_bytes[:].indirect(entries(offs_sb, start, PICK))
-            )
+        nc.gpsimd.memset(x_bytes[:].bitcast(I32), 0)
+        nc.vector.memset(picked_bytes[:].bitcast(I32), 0)
+
+        row_pairs = (slice(0, 2), slice(2, PACK))
+        w1_rows = w1.rearrange("(p j) c -> p j c", j=PACK)
+        nc.sync.dma_start(out=w1_raw[:, 0, :], in_=w1_rows[:, 0, :])
+        nc.sync.dma_start(offs_sb[:], offs)
+        nc.sync.dma_start(out=x_bytes[0:P:SPREAD, :].bitcast(I32), in_=x_scales[0].bitcast(I32))
+        nc.sync.dma_start(out=w1_raw[:, 1:, :], in_=w1_rows[:, 1:, :])
+        nc.sync.dma_start(out=x_codes[:].bitcast(I32), in_=x_words[0].rearrange("p c r -> p (c r)").bitcast(I32))
+        nc.sync.dma_start(slot_sb[:], slot)
+        nc.sync.dma_start(rd_sb[:], rd)
+
+        nc.vector.tensor_copy(out=spread_bytes[:], in_=x_bytes[:].indirect(offs_sb[:]))
+        for r in range(PACK):
+            queue = nc.sync if r % 2 == 0 else nc.scalar
+            queue.dma_start(out=scale_rows(picked_bytes[:], r), in_=scale_rows(spread_bytes[:], SPREAD * r))
+
+        mem_planes = mem.rearrange("(p t) u -> p t u", t=PACK)
+        page = []
+
+        def load_page(tag):
+            t = len(page)
+            page.append(keep.tile([P, U], F32, name="page%d" % t, tag=tag, align_bytes=64))
+            nc.sync.dma_start(out=page[t][:], in_=mem_planes[:, t, :])
+
+        load_page("x_bytes")
 
         w1_bf = keep.tile([P, PACK * H], BF16, name="w1_bf", align_bytes=64)
         w1_dst = w1_bf[:].rearrange("p (t m j) -> p m j t", t=PACK, j=PACK)
@@ -104,18 +90,37 @@ def tile_picked_pageread_silu_po_kernel(
         nc.vector.tensor_copy(out=w1_dst[:, :CAST], in_=w1_src[:, :CAST])
         warm = keep.tile([P, 1], F32, name="warm")
         nc.scalar.activation(out=warm[:], in_=w1_raw[:, 0, 0:1], func=SILU)
-        for pair in row_pairs:
-            nc.scalar.copy(out=w1_dst[:, CAST:, pair], in_=w1_src[:, CAST:, pair])
+        nc.scalar.copy(out=w1_dst[:, CAST:], in_=w1_src[:, CAST:])
+        load_page("w1_raw")
 
         w1_codes = keep.tile([P, H], U32, name="w1_codes", align_bytes=64)
         w1_bytes = keep.tile([P, H], U8, name="w1_bytes", align_bytes=64)
         nc.vector.quantize_mx(out=w1_codes[:].bitcast(FP8X4), scales=w1_bytes[:], in_=w1_bf[:])
+        load_page("w1_bf")
+
+        w2_raw = keep.tile([P, 3 * N], U8, name="w2_raw", tag="spread_bytes", align_bytes=64)
+        nc.gpsimd.memset(w2_raw[:, 2 * N :].bitcast(I32), 0)
+        nc.sync.dma_start(out=w2_raw[:, : 2 * N].bitcast(I32), in_=w2_words[0].bitcast(I32))
+        for r in range(PACK):
+            nc.sync.dma_start(out=scale_rows(w2_raw[:, 2 * N :], r), in_=w2_scales[0, r:SCALE_ROWS:PACK, :].bitcast(I32))
+        w2_codes = keep.tile([P, 2 * N], U8, name="w2_codes", align_bytes=64)
+        w2_bytes = keep.tile([P, N], U8, name="w2_bytes", align_bytes=64)
+        nc.gpsimd.tensor_copy(
+            out=w2_codes[:].rearrange("p (t m b) -> p t m b", t=PACK, b=2),
+            in_=w2_raw[:, : 2 * N].rearrange("p (m t b) -> p t m b", t=PACK, b=2),
+        )
+        nc.gpsimd.tensor_copy(
+            out=w2_bytes[:].rearrange("p (t m) -> p t m", t=PACK),
+            in_=w2_raw[:, 2 * N :].rearrange("p (m t) -> p t m", t=PACK),
+        )
 
         pieces = ((0, LEAD), (LEAD, PICK), (LEAD + PICK, LEAD))
         for start, count in pieces:
             nc.vector.tensor_copy(
                 out=picked_codes[:, start : start + count], in_=x_codes[:].indirect(entries(offs_sb, start, count))
             )
+
+        load_page("x_codes")
 
         y = [keep.tile([P, S], F32, name="y%d" % t, align_bytes=64) for t in range(PACK)]
 
@@ -163,9 +168,8 @@ def tile_picked_pageread_silu_po_kernel(
         chunks = V // READ
         holders = ("w1_codes", "picked_codes", "w1_bytes")
         late = [keep.tile([P, 2 * READ], F32, name="late%d" % c, tag=holders[c], align_bytes=64) for c in range(3)]
-        late.append(keep.tile([P, 3 * READ], F32, name="late3", tag="picked_bytes", align_bytes=64))
-        z = [late[3][:, READ:].bitcast(BF16)]
-        z.extend(keep.tile([P, PACK * READ], BF16, name="z%d" % c, align_bytes=64)[:] for c in range(1, chunks))
+        late.append(keep.tile([P, (1 + 2 * chunks) * READ], F32, name="late3", tag="spread_bytes", align_bytes=64))
+        z = [late[3][:, (1 + 2 * c) * READ : (3 + 2 * c) * READ].bitcast(BF16) for c in range(chunks)]
         early = [keep.tile([P, 2, WIDE], F32, name="early%d" % h, align_bytes=64) for h in range(2)]
 
         def read_early(t, h):
@@ -226,38 +230,49 @@ def tile_picked_pageread_silu_po_kernel(
                 keep.tile([P, width], U8, name="z_bytes", tag="z_bytes" + tag, align_bytes=64),
             )
 
-        def quantise(c, tiles, start):
+        def quantise(src, tiles, start):
             z_codes, z_bytes = tiles
-            nc.vector.quantize_mx(
-                out=z_codes[:, start : start + READ].bitcast(FP8X4), scales=z_bytes[:, start : start + READ], in_=z[c]
+            cols = slice(start, start + src.shape[1] // PACK)
+            nc.vector.quantize_mx(out=z_codes[:, cols].bitcast(FP8X4), scales=z_bytes[:, cols], in_=src)
+
+        def new_banks(width):
+            return [psum.tile([P, width], F32, name="acc", bufs=BANKS) for t in range(PACK)]
+
+        def multiply(acc, t, tiles):
+            z_codes, z_bytes = tiles
+            nc.tensor.matmul_mx(
+                out=acc,
+                lhsT=w2_codes[:, 2 * t * P : 2 * (t + 1) * P].bitcast(FP4X4),
+                lhsT_scale=w2_bytes[:, t * P : (t + 1) * P],
+                rhs=z_codes[:].bitcast(FP8X4),
+                rhs_scale=z_bytes[:],
+                start=True,
+                stop=True,
             )
 
-        def multiply(tiles, width):
-            z_codes, z_bytes = tiles
-            banks = []
+        def multiply_planes(tiles, width):
+            banks = new_banks(width)
             for t in range(PACK):
-                acc = psum.tile([P, width], F32, name="acc", bufs=BANKS)
-                nc.tensor.matmul_mx(
-                    out=acc[:],
-                    lhsT=w2_codes[:, 2 * t * P : 2 * (t + 1) * P].bitcast(FP4X4),
-                    lhsT_scale=w2_bytes[:, t * P : (t + 1) * P],
-                    rhs=z_codes[:].bitcast(FP8X4),
-                    rhs_scale=z_bytes[:],
-                    start=True,
-                    stop=True,
-                )
-                banks.append(acc)
+                multiply(banks[t][:], t, tiles)
             return banks
 
-        def unload_pairs(c, banks, copy):
-            for pair in row_pairs:
-                for t in range(pair.start, pair.stop):
+        def unload(c, banks, copy, groups):
+            for rows in groups:
+                for t in range(rows.start, rows.stop):
                     copy(out=res[c][:, t, :], in_=banks[t][:])
-                nc.sync.dma_start(out=out_planes[:, pair, c * READ : (c + 1) * READ], in_=res[c][:, pair, :])
+                nc.sync.dma_start(out=out_planes[:, rows, c * READ : (c + 1) * READ], in_=res[c][:, rows, :])
 
-        def unload_plane(t, banks, copy):
-            copy(out=res[2][:, t, :], in_=banks[t][:])
-            nc.sync.dma_start(out=out_planes[:, t, WIDE:], in_=res[2][:, t, :])
+        def multiply_pair(pair, tiles):
+            acc = psum.tile([P, 2, READ], F32, name="acc", bufs=BANKS)
+            for e in range(2):
+                multiply(acc[:, e, :], pair.start + e, tiles)
+            return acc
+
+        def unload_pair(c, pair, acc, copy):
+            copy(out=res[2][:, pair, (c - 2) * READ : (c - 1) * READ], in_=acc[:])
+
+        def store_late(pair):
+            nc.sync.dma_start(out=out_planes[:, pair, WIDE:], in_=res[2][:, pair, :])
 
         def round_columns(v0, width, copy):
             c, start = v0 // READ, v0 % READ
@@ -274,36 +289,44 @@ def tile_picked_pageread_silu_po_kernel(
 
         for c in range(3):
             read_last(c)
-        activate(0, 0, READ)
-        first = operand(READ, "a")
-        quantise(0, first, 0)
-        banks0 = multiply(first, READ)
+        halves = [operand(HALF, tag) for tag in ("c", "a")]
+        for h in range(2):
+            activate(0, h * HALF, HALF)
+            quantise(z[0][:, PACK * h * HALF : PACK * (h + 1) * HALF], halves[h], 0)
+        banks0 = new_banks(READ)
+        for pair in row_pairs:
+            for h in range(2):
+                for t in range(pair.start, pair.stop):
+                    multiply(banks0[t][:, h * HALF : (h + 1) * HALF], t, halves[h])
         read_last(3)
         for c in range(1, chunks):
             activate(c, 0, READ)
         second = operand(READ, "b")
-        quantise(1, second, 0)
-        banks1 = multiply(second, READ)
-        unload_pairs(0, banks0, nc.vector.tensor_copy)
-        third = operand(WIDE, "a")
-        quantise(2, third, 0)
-        quantise(3, third, READ)
-        banks2 = multiply(third, WIDE)
-        unload_pairs(1, banks1, nc.scalar.copy)
+        quantise(z[1], second, 0)
+        banks1 = multiply_planes(second, READ)
+        unload(0, banks0, nc.vector.tensor_copy, [slice(t, t + 1) for t in range(PACK)])
+        third, fourth = operand(READ, "a"), operand(READ, "c")
+        quantise(z[2], third, 0)
+        quantise(z[3], fourth, 0)
+        front, back = row_pairs
+        late_banks = [multiply_pair(pair, tiles) for pair in row_pairs for tiles in (third, fourth)]
+        unload(1, banks1, nc.scalar.copy, row_pairs)
         round_columns(0, READ, nc.vector.tensor_copy)
+        unload_pair(2, front, late_banks[0], nc.scalar.copy)
+        unload_pair(3, front, late_banks[1], nc.vector.tensor_copy)
+        store_late(front)
+        unload_pair(2, back, late_banks[2], nc.scalar.copy)
+        unload_pair(3, back, late_banks[3], nc.scalar.copy)
+        store_late(back)
         round_columns(READ, READ, nc.vector.tensor_copy)
-        unload_plane(0, banks2, nc.scalar.copy)
-        unload_plane(1, banks2, nc.vector.tensor_copy)
-        unload_plane(2, banks2, nc.scalar.copy)
-        unload_plane(3, banks2, nc.scalar.copy)
+        round_columns(2 * READ, READ, nc.vector.tensor_copy)
         hand_on(0)
         hand_on(1)
         store_words(0, WIDE)
-        round_columns(2 * READ, HALF, nc.scalar.copy)
-        round_columns(3 * READ, READ, nc.vector.tensor_copy)
-        round_columns(2 * READ + HALF, HALF, nc.vector.tensor_copy)
-        hand_on(3)
+        round_columns(3 * READ + NEAR, READ - NEAR, nc.scalar.copy)
+        round_columns(3 * READ, NEAR, nc.vector.tensor_copy)
         hand_on(2)
+        hand_on(3)
         store_words(WIDE, WIDE)
 
         for q in range(PACK):

@@ -20,7 +20,6 @@ P = 128
 PACK = 4
 QUADRANT = 32
 SCALE_ROWS = 16
-SPREAD = 8
 PER_COL = 16
 BANKS = 8
 PICK = 256
@@ -28,7 +27,6 @@ LEAD = 128
 CAST = 80
 WIDE = 512
 READ = 256
-NEAR = 64
 HALF = READ // 2
 
 
@@ -45,44 +43,60 @@ def tile_picked_pageread_silu_po_kernel(
         rd_sb = keep.tile([P, V // PER_COL], U16, name="rd_sb")
         x_codes = keep.tile([P, T], U32, name="x_codes", align_bytes=64)
         x_bytes = keep.tile([P, T], U8, name="x_bytes", align_bytes=64)
+        w2_raw = keep.tile([P, 2 * N], U8, name="w2_raw", align_bytes=64)
+        w2_raw_bytes = keep.tile([P, N], U8, name="w2_raw_bytes", align_bytes=64)
         w1_raw = keep.tile([P, PACK, H], F32, name="w1_raw", align_bytes=64)
-        spread_bytes = keep.tile([P, S], U8, name="spread_bytes", align_bytes=64)
+        page = [keep.tile([P, U], F32, name="page%d" % t, align_bytes=64) for t in range(PACK)]
+
+        def scale_rows(tile, r):
+            return tile[r:P:QUADRANT, :].bitcast(I32)
+
+        def dram_scale_rows(scales, r):
+            return scales[0, r:SCALE_ROWS:PACK, :].bitcast(I32)
+
+        nc.vector.memset(x_bytes[:].bitcast(I32), 0)
+        nc.vector.memset(w2_raw_bytes[:].bitcast(I32), 0)
+
+        row_pairs = (slice(0, 2), slice(2, PACK))
+        w1_rows = w1.rearrange("(p j) c -> p j c", j=PACK)
+        nc.sync.dma_start(out=w1_raw[:, row_pairs[0], :], in_=w1_rows[:, row_pairs[0], :])
+        nc.sync.dma_start(offs_sb[:], offs)
+        for r in range(PACK):
+            nc.sync.dma_start(out=scale_rows(x_bytes, r), in_=dram_scale_rows(x_scales, r))
+        nc.sync.dma_start(out=w1_raw[:, row_pairs[1], :], in_=w1_rows[:, row_pairs[1], :])
+        nc.sync.dma_start(out=x_codes[:].bitcast(I32), in_=x_words[0].rearrange("p c r -> p (c r)").bitcast(I32))
+        nc.sync.dma_start(slot_sb[:], slot)
+        mem_planes = mem.rearrange("(p t) u -> p t u", t=PACK)
+        for t in range(2):
+            nc.sync.dma_start(out=page[t][:], in_=mem_planes[:, t, :])
+        nc.sync.dma_start(rd_sb[:], rd)
+        nc.sync.dma_start(out=w2_raw[:].bitcast(I32), in_=w2_words[0].bitcast(I32))
+        for r in range(PACK):
+            nc.sync.dma_start(out=scale_rows(w2_raw_bytes, r), in_=dram_scale_rows(w2_scales, r))
+        for t in range(2, PACK):
+            nc.sync.dma_start(out=page[t][:], in_=mem_planes[:, t, :])
+
+        w2_codes = keep.tile([P, 2 * N], U8, name="w2_codes", align_bytes=64)
+        w2_bytes = keep.tile([P, N], U8, name="w2_bytes", align_bytes=64)
+        nc.gpsimd.tensor_copy(
+            out=w2_codes[:].rearrange("p (t m b) -> p t m b", t=PACK, b=2),
+            in_=w2_raw[:].rearrange("p (m t b) -> p t m b", t=PACK, b=2),
+        )
+        nc.gpsimd.tensor_copy(
+            out=w2_bytes[:].rearrange("p (t m) -> p t m", t=PACK),
+            in_=w2_raw_bytes[:].rearrange("p (m t) -> p t m", t=PACK),
+        )
+
         picked_bytes = keep.tile([P, S], U8, name="picked_bytes", align_bytes=64)
         picked_codes = keep.tile([P, S], U32, name="picked_codes", align_bytes=64)
-
-        def scale_rows(ap, r):
-            return ap[r:P:QUADRANT, :].bitcast(I32)
 
         def entries(lst, start, count):
             return lst[:, start // PER_COL : (start + count) // PER_COL]
 
-        nc.gpsimd.memset(x_bytes[:].bitcast(I32), 0)
-        nc.vector.memset(picked_bytes[:].bitcast(I32), 0)
-
-        row_pairs = (slice(0, 2), slice(2, PACK))
-        w1_rows = w1.rearrange("(p j) c -> p j c", j=PACK)
-        nc.sync.dma_start(out=w1_raw[:, 0, :], in_=w1_rows[:, 0, :])
-        nc.sync.dma_start(offs_sb[:], offs)
-        nc.sync.dma_start(out=x_bytes[0:P:SPREAD, :].bitcast(I32), in_=x_scales[0].bitcast(I32))
-        nc.sync.dma_start(out=w1_raw[:, 1:, :], in_=w1_rows[:, 1:, :])
-        nc.sync.dma_start(out=x_codes[:].bitcast(I32), in_=x_words[0].rearrange("p c r -> p (c r)").bitcast(I32))
-        nc.sync.dma_start(slot_sb[:], slot)
-        nc.sync.dma_start(rd_sb[:], rd)
-
-        nc.vector.tensor_copy(out=spread_bytes[:], in_=x_bytes[:].indirect(offs_sb[:]))
-        for r in range(PACK):
-            queue = nc.sync if r % 2 == 0 else nc.scalar
-            queue.dma_start(out=scale_rows(picked_bytes[:], r), in_=scale_rows(spread_bytes[:], SPREAD * r))
-
-        mem_planes = mem.rearrange("(p t) u -> p t u", t=PACK)
-        page = []
-
-        def load_page(tag):
-            t = len(page)
-            page.append(keep.tile([P, U], F32, name="page%d" % t, tag=tag, align_bytes=64))
-            nc.sync.dma_start(out=page[t][:], in_=mem_planes[:, t, :])
-
-        load_page("x_bytes")
+        for start in range(0, S, PICK):
+            nc.vector.tensor_copy(
+                out=picked_bytes[:, start : start + PICK], in_=x_bytes[:].indirect(entries(offs_sb, start, PICK))
+            )
 
         w1_bf = keep.tile([P, PACK * H], BF16, name="w1_bf", align_bytes=64)
         w1_dst = w1_bf[:].rearrange("p (t m j) -> p m j t", t=PACK, j=PACK)
@@ -90,37 +104,18 @@ def tile_picked_pageread_silu_po_kernel(
         nc.vector.tensor_copy(out=w1_dst[:, :CAST], in_=w1_src[:, :CAST])
         warm = keep.tile([P, 1], F32, name="warm")
         nc.scalar.activation(out=warm[:], in_=w1_raw[:, 0, 0:1], func=SILU)
-        nc.scalar.copy(out=w1_dst[:, CAST:], in_=w1_src[:, CAST:])
-        load_page("w1_raw")
+        for pair in row_pairs:
+            nc.scalar.copy(out=w1_dst[:, CAST:, pair], in_=w1_src[:, CAST:, pair])
 
         w1_codes = keep.tile([P, H], U32, name="w1_codes", align_bytes=64)
         w1_bytes = keep.tile([P, H], U8, name="w1_bytes", align_bytes=64)
         nc.vector.quantize_mx(out=w1_codes[:].bitcast(FP8X4), scales=w1_bytes[:], in_=w1_bf[:])
-        load_page("w1_bf")
-
-        w2_raw = keep.tile([P, 3 * N], U8, name="w2_raw", tag="spread_bytes", align_bytes=64)
-        nc.gpsimd.memset(w2_raw[:, 2 * N :].bitcast(I32), 0)
-        nc.sync.dma_start(out=w2_raw[:, : 2 * N].bitcast(I32), in_=w2_words[0].bitcast(I32))
-        for r in range(PACK):
-            nc.sync.dma_start(out=scale_rows(w2_raw[:, 2 * N :], r), in_=w2_scales[0, r:SCALE_ROWS:PACK, :].bitcast(I32))
-        w2_codes = keep.tile([P, 2 * N], U8, name="w2_codes", align_bytes=64)
-        w2_bytes = keep.tile([P, N], U8, name="w2_bytes", align_bytes=64)
-        nc.gpsimd.tensor_copy(
-            out=w2_codes[:].rearrange("p (t m b) -> p t m b", t=PACK, b=2),
-            in_=w2_raw[:, : 2 * N].rearrange("p (m t b) -> p t m b", t=PACK, b=2),
-        )
-        nc.gpsimd.tensor_copy(
-            out=w2_bytes[:].rearrange("p (t m) -> p t m", t=PACK),
-            in_=w2_raw[:, 2 * N :].rearrange("p (m t) -> p t m", t=PACK),
-        )
 
         pieces = ((0, LEAD), (LEAD, PICK), (LEAD + PICK, LEAD))
         for start, count in pieces:
             nc.vector.tensor_copy(
                 out=picked_codes[:, start : start + count], in_=x_codes[:].indirect(entries(offs_sb, start, count))
             )
-
-        load_page("x_codes")
 
         y = [keep.tile([P, S], F32, name="y%d" % t, align_bytes=64) for t in range(PACK)]
 
@@ -168,8 +163,9 @@ def tile_picked_pageread_silu_po_kernel(
         chunks = V // READ
         holders = ("w1_codes", "picked_codes", "w1_bytes")
         late = [keep.tile([P, 2 * READ], F32, name="late%d" % c, tag=holders[c], align_bytes=64) for c in range(3)]
-        late.append(keep.tile([P, (1 + 2 * chunks) * READ], F32, name="late3", tag="spread_bytes", align_bytes=64))
-        z = [late[3][:, (1 + 2 * c) * READ : (3 + 2 * c) * READ].bitcast(BF16) for c in range(chunks)]
+        late.append(keep.tile([P, 3 * READ], F32, name="late3", tag="picked_bytes", align_bytes=64))
+        z = [late[3][:, READ:].bitcast(BF16)]
+        z.extend(keep.tile([P, PACK * READ], BF16, name="z%d" % c, align_bytes=64)[:] for c in range(1, chunks))
         early = [keep.tile([P, 2, WIDE], F32, name="early%d" % h, align_bytes=64) for h in range(2)]
 
         def read_early(t, h):
@@ -222,7 +218,7 @@ def tile_picked_pageread_silu_po_kernel(
         out_bytes = keep.tile([P, READ], U8, name="out_bytes", align_bytes=64)
         codes = keep.tile([P, V], U32, name="codes", align_bytes=64)
         res = [keep.tile([P, PACK, width], F32, name="res%d" % v0, align_bytes=64) for v0, width in ((0, READ), (READ, READ), (WIDE, WIDE))]
-        rounded = [keep.tile([P, PACK * READ], BF16, name="rounded%d" % c, align_bytes=64) for c in range(chunks)]
+        rounded = {c: keep.tile([P, PACK * READ], BF16, name="rounded%d" % c, align_bytes=64) for c in range(1, chunks)}
 
         def operand(width, tag):
             return (
@@ -256,11 +252,9 @@ def tile_picked_pageread_silu_po_kernel(
                 multiply(banks[t][:], t, tiles)
             return banks
 
-        def unload(c, banks, copy, groups):
-            for rows in groups:
-                for t in range(rows.start, rows.stop):
-                    copy(out=res[c][:, t, :], in_=banks[t][:])
-                nc.sync.dma_start(out=out_planes[:, rows, c * READ : (c + 1) * READ], in_=res[c][:, rows, :])
+        def unload(c, t, banks, copy):
+            copy(out=res[c][:, t, :], in_=banks[t][:])
+            nc.sync.dma_start(out=out_planes[:, t, c * READ : (c + 1) * READ], in_=res[c][:, t, :])
 
         def multiply_pair(pair, tiles):
             acc = psum.tile([P, 2, READ], F32, name="acc", bufs=BANKS)
@@ -304,27 +298,38 @@ def tile_picked_pageread_silu_po_kernel(
         second = operand(READ, "b")
         quantise(z[1], second, 0)
         banks1 = multiply_planes(second, READ)
-        unload(0, banks0, nc.vector.tensor_copy, [slice(t, t + 1) for t in range(PACK)])
+        on_vector, on_scalar = nc.vector.tensor_copy, nc.scalar.copy
+        for t in range(3):
+            unload(0, t, banks0, on_vector)
+        unload(0, 3, banks0, on_scalar)
         third, fourth = operand(READ, "a"), operand(READ, "c")
         quantise(z[2], third, 0)
         quantise(z[3], fourth, 0)
         front, back = row_pairs
         late_banks = [multiply_pair(pair, tiles) for pair in row_pairs for tiles in (third, fourth)]
-        unload(1, banks1, nc.scalar.copy, row_pairs)
-        round_columns(0, READ, nc.vector.tensor_copy)
-        unload_pair(2, front, late_banks[0], nc.scalar.copy)
-        unload_pair(3, front, late_banks[1], nc.vector.tensor_copy)
+        for t in range(PACK):
+            unload(1, t, banks1, on_vector if t == 1 else on_scalar)
+        unload_pair(2, front, late_banks[0], on_vector)
+        unload_pair(3, front, late_banks[1], on_scalar)
         store_late(front)
-        unload_pair(2, back, late_banks[2], nc.scalar.copy)
-        unload_pair(3, back, late_banks[3], nc.scalar.copy)
+        unload_pair(2, back, late_banks[2], on_vector)
+        unload_pair(3, back, late_banks[3], on_scalar)
         store_late(back)
-        round_columns(READ, READ, nc.vector.tensor_copy)
-        round_columns(2 * READ, READ, nc.vector.tensor_copy)
+        rounded[0] = keep.tile([P, PACK * READ], BF16, name="rounded0", tag="z3", align_bytes=64)
+        nc.gpsimd.tensor_scalar(
+            out=side_by_side(rounded[0][:]),
+            in0=res[0][:].rearrange("p t c -> p c t"),
+            scalar1=1.0,
+            scalar2=-0.0,
+            op0=mybir.AluOpType.mult,
+            op1=mybir.AluOpType.add,
+        )
+        round_columns(READ, READ, on_vector)
+        round_columns(3 * READ, READ, on_scalar)
         hand_on(0)
+        round_columns(2 * READ, READ, on_vector)
         hand_on(1)
         store_words(0, WIDE)
-        round_columns(3 * READ + NEAR, READ - NEAR, nc.scalar.copy)
-        round_columns(3 * READ, NEAR, nc.vector.tensor_copy)
         hand_on(2)
         hand_on(3)
         store_words(WIDE, WIDE)

@@ -20,6 +20,7 @@ P = 128
 PACK = 4
 QUADRANT = 32
 SCALE_ROWS = 16
+SPREAD = 8
 PER_COL = 16
 BANKS = 8
 PICK = 256
@@ -43,60 +44,44 @@ def tile_picked_pageread_silu_po_kernel(
         rd_sb = keep.tile([P, V // PER_COL], U16, name="rd_sb")
         x_codes = keep.tile([P, T], U32, name="x_codes", align_bytes=64)
         x_bytes = keep.tile([P, T], U8, name="x_bytes", align_bytes=64)
-        w2_raw = keep.tile([P, 2 * N], U8, name="w2_raw", align_bytes=64)
-        w2_raw_bytes = keep.tile([P, N], U8, name="w2_raw_bytes", align_bytes=64)
         w1_raw = keep.tile([P, PACK, H], F32, name="w1_raw", align_bytes=64)
-        page = [keep.tile([P, U], F32, name="page%d" % t, align_bytes=64) for t in range(PACK)]
-
-        def scale_rows(tile, r):
-            return tile[r:P:QUADRANT, :].bitcast(I32)
-
-        def dram_scale_rows(scales, r):
-            return scales[0, r:SCALE_ROWS:PACK, :].bitcast(I32)
-
-        nc.vector.memset(x_bytes[:].bitcast(I32), 0)
-        nc.vector.memset(w2_raw_bytes[:].bitcast(I32), 0)
-
-        row_pairs = (slice(0, 2), slice(2, PACK))
-        w1_rows = w1.rearrange("(p j) c -> p j c", j=PACK)
-        nc.sync.dma_start(out=w1_raw[:, row_pairs[0], :], in_=w1_rows[:, row_pairs[0], :])
-        nc.sync.dma_start(offs_sb[:], offs)
-        for r in range(PACK):
-            nc.sync.dma_start(out=scale_rows(x_bytes, r), in_=dram_scale_rows(x_scales, r))
-        nc.sync.dma_start(out=w1_raw[:, row_pairs[1], :], in_=w1_rows[:, row_pairs[1], :])
-        nc.sync.dma_start(out=x_codes[:].bitcast(I32), in_=x_words[0].rearrange("p c r -> p (c r)").bitcast(I32))
-        nc.sync.dma_start(slot_sb[:], slot)
-        mem_planes = mem.rearrange("(p t) u -> p t u", t=PACK)
-        for t in range(2):
-            nc.sync.dma_start(out=page[t][:], in_=mem_planes[:, t, :])
-        nc.sync.dma_start(rd_sb[:], rd)
-        nc.sync.dma_start(out=w2_raw[:].bitcast(I32), in_=w2_words[0].bitcast(I32))
-        for r in range(PACK):
-            nc.sync.dma_start(out=scale_rows(w2_raw_bytes, r), in_=dram_scale_rows(w2_scales, r))
-        for t in range(2, PACK):
-            nc.sync.dma_start(out=page[t][:], in_=mem_planes[:, t, :])
-
-        w2_codes = keep.tile([P, 2 * N], U8, name="w2_codes", align_bytes=64)
-        w2_bytes = keep.tile([P, N], U8, name="w2_bytes", align_bytes=64)
-        nc.gpsimd.tensor_copy(
-            out=w2_codes[:].rearrange("p (t m b) -> p t m b", t=PACK, b=2),
-            in_=w2_raw[:].rearrange("p (m t b) -> p t m b", t=PACK, b=2),
-        )
-        nc.gpsimd.tensor_copy(
-            out=w2_bytes[:].rearrange("p (t m) -> p t m", t=PACK),
-            in_=w2_raw_bytes[:].rearrange("p (m t) -> p t m", t=PACK),
-        )
-
+        spread_bytes = keep.tile([P, S], U8, name="spread_bytes", align_bytes=64)
         picked_bytes = keep.tile([P, S], U8, name="picked_bytes", align_bytes=64)
         picked_codes = keep.tile([P, S], U32, name="picked_codes", align_bytes=64)
+
+        def scale_rows(ap, r):
+            return ap[r:P:QUADRANT, :].bitcast(I32)
 
         def entries(lst, start, count):
             return lst[:, start // PER_COL : (start + count) // PER_COL]
 
-        for start in range(0, S, PICK):
-            nc.vector.tensor_copy(
-                out=picked_bytes[:, start : start + PICK], in_=x_bytes[:].indirect(entries(offs_sb, start, PICK))
-            )
+        nc.gpsimd.memset(x_bytes[:].bitcast(I32), 0)
+        nc.vector.memset(picked_bytes[:].bitcast(I32), 0)
+
+        row_pairs = (slice(0, 2), slice(2, PACK))
+        w1_rows = w1.rearrange("(p j) c -> p j c", j=PACK)
+        nc.sync.dma_start(out=w1_raw[:, 0, :], in_=w1_rows[:, 0, :])
+        nc.sync.dma_start(offs_sb[:], offs)
+        nc.sync.dma_start(out=x_bytes[0:P:SPREAD, :].bitcast(I32), in_=x_scales[0].bitcast(I32))
+        nc.sync.dma_start(out=w1_raw[:, 1:, :], in_=w1_rows[:, 1:, :])
+        nc.sync.dma_start(out=x_codes[:].bitcast(I32), in_=x_words[0].rearrange("p c r -> p (c r)").bitcast(I32))
+        nc.sync.dma_start(slot_sb[:], slot)
+        nc.sync.dma_start(rd_sb[:], rd)
+
+        nc.vector.tensor_copy(out=spread_bytes[:], in_=x_bytes[:].indirect(offs_sb[:]))
+        for r in range(PACK):
+            queue = nc.sync if r % 2 == 0 else nc.scalar
+            queue.dma_start(out=scale_rows(picked_bytes[:], r), in_=scale_rows(spread_bytes[:], SPREAD * r))
+
+        mem_planes = mem.rearrange("(p t) u -> p t u", t=PACK)
+        page = []
+
+        def load_page(tag):
+            t = len(page)
+            page.append(keep.tile([P, U], F32, name="page%d" % t, tag=tag, align_bytes=64))
+            nc.sync.dma_start(out=page[t][:], in_=mem_planes[:, t, :])
+
+        load_page("x_bytes")
 
         w1_bf = keep.tile([P, PACK * H], BF16, name="w1_bf", align_bytes=64)
         w1_dst = w1_bf[:].rearrange("p (t m j) -> p m j t", t=PACK, j=PACK)
@@ -104,18 +89,37 @@ def tile_picked_pageread_silu_po_kernel(
         nc.vector.tensor_copy(out=w1_dst[:, :CAST], in_=w1_src[:, :CAST])
         warm = keep.tile([P, 1], F32, name="warm")
         nc.scalar.activation(out=warm[:], in_=w1_raw[:, 0, 0:1], func=SILU)
-        for pair in row_pairs:
-            nc.scalar.copy(out=w1_dst[:, CAST:, pair], in_=w1_src[:, CAST:, pair])
+        nc.scalar.copy(out=w1_dst[:, CAST:], in_=w1_src[:, CAST:])
+        load_page("w1_raw")
 
         w1_codes = keep.tile([P, H], U32, name="w1_codes", align_bytes=64)
         w1_bytes = keep.tile([P, H], U8, name="w1_bytes", align_bytes=64)
         nc.vector.quantize_mx(out=w1_codes[:].bitcast(FP8X4), scales=w1_bytes[:], in_=w1_bf[:])
+        load_page("w1_bf")
+
+        w2_raw = keep.tile([P, 3 * N], U8, name="w2_raw", tag="spread_bytes", align_bytes=64)
+        nc.gpsimd.memset(w2_raw[:, 2 * N :].bitcast(I32), 0)
+        nc.sync.dma_start(out=w2_raw[:, : 2 * N].bitcast(I32), in_=w2_words[0].bitcast(I32))
+        for r in range(PACK):
+            nc.sync.dma_start(out=scale_rows(w2_raw[:, 2 * N :], r), in_=w2_scales[0, r:SCALE_ROWS:PACK, :].bitcast(I32))
+        w2_codes = keep.tile([P, 2 * N], U8, name="w2_codes", align_bytes=64)
+        w2_bytes = keep.tile([P, N], U8, name="w2_bytes", align_bytes=64)
+        nc.gpsimd.tensor_copy(
+            out=w2_codes[:].rearrange("p (t m b) -> p t m b", t=PACK, b=2),
+            in_=w2_raw[:, : 2 * N].rearrange("p (m t b) -> p t m b", t=PACK, b=2),
+        )
+        nc.gpsimd.tensor_copy(
+            out=w2_bytes[:].rearrange("p (t m) -> p t m", t=PACK),
+            in_=w2_raw[:, 2 * N :].rearrange("p (m t) -> p t m", t=PACK),
+        )
 
         pieces = ((0, LEAD), (LEAD, PICK), (LEAD + PICK, LEAD))
         for start, count in pieces:
             nc.vector.tensor_copy(
                 out=picked_codes[:, start : start + count], in_=x_codes[:].indirect(entries(offs_sb, start, count))
             )
+
+        load_page("x_codes")
 
         y = [keep.tile([P, S], F32, name="y%d" % t, align_bytes=64) for t in range(PACK)]
 
@@ -163,9 +167,8 @@ def tile_picked_pageread_silu_po_kernel(
         chunks = V // READ
         holders = ("w1_codes", "picked_codes", "w1_bytes")
         late = [keep.tile([P, 2 * READ], F32, name="late%d" % c, tag=holders[c], align_bytes=64) for c in range(3)]
-        late.append(keep.tile([P, 3 * READ], F32, name="late3", tag="picked_bytes", align_bytes=64))
-        z = [late[3][:, READ:].bitcast(BF16)]
-        z.extend(keep.tile([P, PACK * READ], BF16, name="z%d" % c, align_bytes=64)[:] for c in range(1, chunks))
+        late.append(keep.tile([P, (1 + 2 * chunks) * READ], F32, name="late3", tag="spread_bytes", align_bytes=64))
+        z = [late[3][:, (1 + 2 * c) * READ : (3 + 2 * c) * READ].bitcast(BF16) for c in range(chunks)]
         early = [keep.tile([P, 2, WIDE], F32, name="early%d" % h, align_bytes=64) for h in range(2)]
 
         def read_early(t, h):
@@ -218,7 +221,8 @@ def tile_picked_pageread_silu_po_kernel(
         out_bytes = keep.tile([P, READ], U8, name="out_bytes", align_bytes=64)
         codes = keep.tile([P, V], U32, name="codes", align_bytes=64)
         res = [keep.tile([P, PACK, width], F32, name="res%d" % v0, align_bytes=64) for v0, width in ((0, READ), (READ, READ), (WIDE, WIDE))]
-        rounded = {c: keep.tile([P, PACK * READ], BF16, name="rounded%d" % c, align_bytes=64) for c in range(1, chunks)}
+        rounded = [z[3]]
+        rounded.extend(keep.tile([P, PACK * READ], BF16, name="rounded%d" % c, align_bytes=64)[:] for c in range(1, chunks))
 
         def operand(width, tag):
             return (
@@ -231,8 +235,8 @@ def tile_picked_pageread_silu_po_kernel(
             cols = slice(start, start + src.shape[1] // PACK)
             nc.vector.quantize_mx(out=z_codes[:, cols].bitcast(FP8X4), scales=z_bytes[:, cols], in_=src)
 
-        def new_banks(width):
-            return [psum.tile([P, width], F32, name="acc", bufs=BANKS) for t in range(PACK)]
+        def new_banks(width, count):
+            return [psum.tile([P, width], F32, name="acc", bufs=BANKS) for t in range(count)]
 
         def multiply(acc, t, tiles):
             z_codes, z_bytes = tiles
@@ -246,15 +250,8 @@ def tile_picked_pageread_silu_po_kernel(
                 stop=True,
             )
 
-        def multiply_planes(tiles, width):
-            banks = new_banks(width)
-            for t in range(PACK):
-                multiply(banks[t][:], t, tiles)
-            return banks
-
-        def unload(c, t, banks, copy):
-            copy(out=res[c][:, t, :], in_=banks[t][:])
-            nc.sync.dma_start(out=out_planes[:, t, c * READ : (c + 1) * READ], in_=res[c][:, t, :])
+        def store(c, rows):
+            nc.sync.dma_start(out=out_planes[:, rows, c * READ : (c + 1) * READ], in_=res[c][:, rows, :])
 
         def multiply_pair(pair, tiles):
             acc = psum.tile([P, 2, READ], F32, name="acc", bufs=BANKS)
@@ -275,7 +272,7 @@ def tile_picked_pageread_silu_po_kernel(
 
         def hand_on(c):
             nc.vector.quantize_mx(
-                out=codes[:, c * READ : (c + 1) * READ].bitcast(FP8X4), scales=out_bytes[PACK * c :, :], in_=rounded[c][:]
+                out=codes[:, c * READ : (c + 1) * READ].bitcast(FP8X4), scales=out_bytes[PACK * c :, :], in_=rounded[c]
             )
 
         def store_words(v0, width):
@@ -287,7 +284,7 @@ def tile_picked_pageread_silu_po_kernel(
         for h in range(2):
             activate(0, h * HALF, HALF)
             quantise(z[0][:, PACK * h * HALF : PACK * (h + 1) * HALF], halves[h], 0)
-        banks0 = new_banks(READ)
+        banks0 = new_banks(READ, PACK)
         for pair in row_pairs:
             for h in range(2):
                 for t in range(pair.start, pair.stop):
@@ -297,27 +294,35 @@ def tile_picked_pageread_silu_po_kernel(
             activate(c, 0, READ)
         second = operand(READ, "b")
         quantise(z[1], second, 0)
-        banks1 = multiply_planes(second, READ)
+        front, back = row_pairs
+        banks1 = new_banks(READ, 2)
+        for t in range(2):
+            multiply(banks1[t][:], t, second)
+        bank1_back = multiply_pair(back, second)
         on_vector, on_scalar = nc.vector.tensor_copy, nc.scalar.copy
-        for t in range(3):
-            unload(0, t, banks0, on_vector)
-        unload(0, 3, banks0, on_scalar)
+        for t in range(2):
+            on_vector(out=res[0][:, t, :], in_=banks0[t][:])
+            store(0, slice(t, t + 1))
+        on_vector(out=res[0][:, 2, :], in_=banks0[2][:])
+        on_scalar(out=res[0][:, 3, :], in_=banks0[3][:])
+        store(0, back)
         third, fourth = operand(READ, "a"), operand(READ, "c")
         quantise(z[2], third, 0)
         quantise(z[3], fourth, 0)
-        front, back = row_pairs
         late_banks = [multiply_pair(pair, tiles) for pair in row_pairs for tiles in (third, fourth)]
-        for t in range(PACK):
-            unload(1, t, banks1, on_vector if t == 1 else on_scalar)
+        on_scalar(out=res[1][:, 0, :], in_=banks1[0][:])
+        on_vector(out=res[1][:, 1, :], in_=banks1[1][:])
+        store(1, front)
+        on_scalar(out=res[1][:, back, :], in_=bank1_back[:])
+        store(1, back)
         unload_pair(2, front, late_banks[0], on_vector)
         unload_pair(3, front, late_banks[1], on_scalar)
         store_late(front)
         unload_pair(2, back, late_banks[2], on_vector)
         unload_pair(3, back, late_banks[3], on_scalar)
         store_late(back)
-        rounded[0] = keep.tile([P, PACK * READ], BF16, name="rounded0", tag="z3", align_bytes=64)
         nc.gpsimd.tensor_scalar(
-            out=side_by_side(rounded[0][:]),
+            out=side_by_side(rounded[0]),
             in0=res[0][:].rearrange("p t c -> p c t"),
             scalar1=1.0,
             scalar2=-0.0,
@@ -325,11 +330,12 @@ def tile_picked_pageread_silu_po_kernel(
             op1=mybir.AluOpType.add,
         )
         round_columns(READ, READ, on_vector)
-        round_columns(3 * READ, READ, on_scalar)
+        round_columns(2 * READ, HALF, on_scalar)
+        round_columns(2 * READ + HALF, HALF, on_vector)
         hand_on(0)
-        round_columns(2 * READ, READ, on_vector)
         hand_on(1)
         store_words(0, WIDE)
+        round_columns(3 * READ, READ, on_vector)
         hand_on(2)
         hand_on(3)
         store_words(WIDE, WIDE)

@@ -278,8 +278,9 @@ def tile_picked_pageread_silu_po_kernel(
         def store_words(v0, width):
             nc.sync.dma_start(out=out_words[:, v0 : v0 + width], in_=codes[:, v0 : v0 + width].bitcast(I32))
 
-        for c in range(3):
-            read_last(c)
+        read_last(0)
+        read_on_scalar(late[1][:, READ : 2 * READ], page[3], READ, READ)
+        read_last(2)
         halves = [operand(HALF, tag) for tag in ("c", "a")]
         for h in range(2):
             activate(0, h * HALF, HALF)

@@ -90,18 +90,18 @@ def tile_picked_pageread_silu_po_kernel(
         warm = keep.tile([P, 1], F32, name="warm")
         nc.scalar.activation(out=warm[:], in_=w1_raw[:, 0, 0:1], func=SILU)
         nc.scalar.copy(out=w1_dst[:, CAST:], in_=w1_src[:, CAST:])
-        load_page("w1_raw")
 
         w1_codes = keep.tile([P, H], U32, name="w1_codes", align_bytes=64)
         w1_bytes = keep.tile([P, H], U8, name="w1_bytes", align_bytes=64)
         nc.vector.quantize_mx(out=w1_codes[:].bitcast(FP8X4), scales=w1_bytes[:], in_=w1_bf[:])
-        load_page("w1_bf")
 
-        w2_raw = keep.tile([P, 3 * N], U8, name="w2_raw", tag="spread_bytes", align_bytes=64)
+        w2_raw = keep.tile([P, 3 * N], U8, name="w2_raw", tag="w1_raw", align_bytes=64)
         nc.gpsimd.memset(w2_raw[:, 2 * N :].bitcast(I32), 0)
         nc.sync.dma_start(out=w2_raw[:, : 2 * N].bitcast(I32), in_=w2_words[0].bitcast(I32))
         for r in range(PACK):
             nc.sync.dma_start(out=scale_rows(w2_raw[:, 2 * N :], r), in_=w2_scales[0, r:SCALE_ROWS:PACK, :].bitcast(I32))
+        load_page("w1_bf")
+        load_page("spread_bytes")
         w2_codes = keep.tile([P, 2 * N], U8, name="w2_codes", align_bytes=64)
         w2_bytes = keep.tile([P, N], U8, name="w2_bytes", align_bytes=64)
         nc.gpsimd.tensor_copy(
@@ -165,78 +165,63 @@ def tile_picked_pageread_silu_po_kernel(
             return ap.rearrange("p t (c i) -> p c t i", i=4)
 
         chunks = V // READ
-        holders = ("w1_codes", "picked_codes", "w1_bytes")
-        late = [keep.tile([P, 2 * READ], F32, name="late%d" % c, tag=holders[c], align_bytes=64) for c in range(3)]
-        late.append(keep.tile([P, (1 + 2 * chunks) * READ], F32, name="late3", tag="spread_bytes", align_bytes=64))
-        z = [late[3][:, (1 + 2 * c) * READ : (3 + 2 * c) * READ].bitcast(BF16) for c in range(chunks)]
-        early = [keep.tile([P, 2, WIDE], F32, name="early%d" % h, align_bytes=64) for h in range(2)]
+        lower = [keep.tile([P, WIDE], F32, name="lower", tag=tag, align_bytes=64) for tag in ("picked_codes", "w1_bytes")]
+        pitch = 3 * READ
+        upper = keep.tile([P, READ + 3 * pitch + 2 * V], F32, name="upper", tag="w1_codes", align_bytes=64)
+        z0 = READ + 3 * pitch
+        z = [upper[:, z0 + 2 * c * READ : z0 + 2 * (c + 1) * READ].bitcast(BF16) for c in range(chunks)]
+        early = [keep.tile([P, 2, width], F32, name="early%d" % width, align_bytes=64) for width in (WIDE, READ)]
+        last_row = [lower[0][:, READ:], lower[1][:, READ:], upper[:, 2 * pitch + WIDE : 3 * pitch], upper[:, z0 : z0 + READ]]
+        late_pair = [rows[:].rearrange("p (t c) -> p c t", t=2) for rows in lower]
+        late_pair.append(upper[:, 2 * pitch : 2 * pitch + 2 * WIDE].rearrange("p (t c) -> p c t", t=2)[:, :READ, :])
 
-        def read_early(t, h):
-            read_on_scalar(late[(2 * t + h) % 3][:], page[t], h * WIDE, WIDE)
+        def weave_early(c):
+            nc.gpsimd.tensor_scalar(
+                out=side_by_side(z[c])[:, :, row_pairs[0]],
+                in0=early[c // 2][:, :, c % 2 * READ : (c % 2 + 1) * READ].rearrange("p t c -> p c t"),
+                scalar1=1.0,
+                scalar2=-0.0,
+                op0=mybir.AluOpType.mult,
+                op1=mybir.AluOpType.add,
+            )
 
-        def activate_early(t, h):
-            nc.scalar.activation(out=early[h][:, t, :], in_=late[(2 * t + h) % 3][:], func=SILU)
-
-        def weave_early(h):
-            for c in (2 * h, 2 * h + 1):
-                nc.gpsimd.tensor_scalar(
-                    out=side_by_side(z[c])[:, :, row_pairs[0]],
-                    in0=early[h][:, :, c % 2 * READ : (c % 2 + 1) * READ].rearrange("p t c -> p c t"),
-                    scalar1=1.0,
-                    scalar2=-0.0,
-                    op0=mybir.AluOpType.mult,
-                    op1=mybir.AluOpType.add,
-                )
-
-        def read_third(c):
-            read_on_scalar(late[c][:, :READ], page[2], c * READ, READ)
-
-        read_early(0, 0)
-        read_early(0, 1)
-        activate_early(0, 0)
-        read_early(1, 0)
-        activate_early(0, 1)
-        activate_early(1, 0)
-        weave_early(0)
-        read_early(1, 1)
-        read_third(1)
-        activate_early(1, 1)
-        weave_early(1)
-        for c in (2, 0, 3):
-            read_third(c)
+        for t in range(2):
+            read_on_scalar(lower[t][:], page[t], 0, WIDE)
+            read_on_scalar(upper[:, t * pitch : t * pitch + WIDE], page[t], WIDE, WIDE)
+            nc.scalar.activation(out=early[0][:, t, :], in_=lower[t][:], func=SILU)
+            nc.scalar.activation(out=early[1][:, t, :], in_=upper[:, t * pitch : t * pitch + READ], func=SILU)
+        for c in range(3):
+            weave_early(c)
+        for c in range(2):
+            read_on_scalar(lower[c][:, :READ], page[2], c * READ, READ)
+        read_on_scalar(upper[:, 2 * pitch : 2 * pitch + WIDE], page[2], WIDE, WIDE)
 
         def read_last(c):
-            nc.vector.tensor_copy(out=late[c][:, READ : 2 * READ], in_=page[3][:].indirect(entries(rd_sb, c * READ, READ)))
+            nc.vector.tensor_copy(out=last_row[c], in_=page[3][:].indirect(entries(rd_sb, c * READ, READ)))
 
         def activate(c, start, width):
-            src = late[c][:, : 2 * READ].rearrange("p (t c) -> p c t", t=2)
+            if c == 3:
+                rows = upper[:, READ : READ + PACK * pitch].rearrange("p (t c) -> p t c", t=PACK)[:, :, :READ]
+                nc.scalar.activation(out=woven(z[c]), in_=planes(rows), func=SILU)
+                return
             nc.scalar.activation(
                 out=side_by_side(z[c])[:, start : start + width, row_pairs[1]],
-                in_=src[:, start : start + width, :],
+                in_=late_pair[c][:, start : start + width, :],
                 func=SILU,
             )
 
         out_planes = out_0.rearrange("(p t) v -> p t v", t=PACK)
         out_words = out_1[0].rearrange("p c r -> p (c r)").bitcast(I32)
-        out_bytes = keep.tile([P, READ], U8, name="out_bytes", align_bytes=64)
+        out_bytes = keep.tile([P, WIDE], U8, name="out_bytes", align_bytes=64)
         codes = keep.tile([P, V], U32, name="codes", align_bytes=64)
         res = [keep.tile([P, PACK, width], F32, name="res%d" % v0, align_bytes=64) for v0, width in ((0, READ), (READ, READ), (WIDE, WIDE))]
-        rounded = [z[3]]
-        rounded.extend(keep.tile([P, PACK * READ], BF16, name="rounded%d" % c, align_bytes=64)[:] for c in range(1, chunks))
 
-        def operand(width, tag):
-            return (
-                keep.tile([P, width], U32, name="z_codes", tag="z_codes" + tag, align_bytes=64),
-                keep.tile([P, width], U8, name="z_bytes", tag="z_bytes" + tag, align_bytes=64),
-            )
-
-        def quantise(src, tiles, start):
-            z_codes, z_bytes = tiles
-            cols = slice(start, start + src.shape[1] // PACK)
-            nc.vector.quantize_mx(out=z_codes[:, cols].bitcast(FP8X4), scales=z_bytes[:, cols], in_=src)
-
-        def new_banks(width, count):
-            return [psum.tile([P, width], F32, name="acc", bufs=BANKS) for t in range(count)]
+        def quantise(src, tag):
+            width = src.shape[1] // PACK
+            z_codes = keep.tile([P, width], U32, name="z_codes", tag="z_codes" + tag, align_bytes=64)
+            z_bytes = keep.tile([P, width], U8, name="z_bytes", tag="z_bytes" + tag, align_bytes=64)
+            nc.vector.quantize_mx(out=z_codes[:].bitcast(FP8X4), scales=z_bytes[:], in_=src)
+            return z_codes, z_bytes
 
         def multiply(acc, t, tiles):
             z_codes, z_bytes = tiles
@@ -250,8 +235,13 @@ def tile_picked_pageread_silu_po_kernel(
                 stop=True,
             )
 
-        def store(c, rows):
-            nc.sync.dma_start(out=out_planes[:, rows, c * READ : (c + 1) * READ], in_=res[c][:, rows, :])
+        def new_banks():
+            return [psum.tile([P, READ], F32, name="acc", bufs=BANKS) for t in range(PACK)]
+
+        def multiply_plane(t, tiles):
+            acc = psum.tile([P, READ], F32, name="acc", bufs=BANKS)
+            multiply(acc[:], t, tiles)
+            return acc
 
         def multiply_pair(pair, tiles):
             acc = psum.tile([P, 2, READ], F32, name="acc", bufs=BANKS)
@@ -259,33 +249,52 @@ def tile_picked_pageread_silu_po_kernel(
                 multiply(acc[:, e, :], pair.start + e, tiles)
             return acc
 
+        def store(c, rows):
+            nc.sync.dma_start(out=out_planes[:, rows, c * READ : (c + 1) * READ], in_=res[c][:, rows, :])
+
+        def unload(c, t, banks, copy):
+            copy(out=res[c][:, t, :], in_=banks[t][:])
+
         def unload_pair(c, pair, acc, copy):
             copy(out=res[2][:, pair, (c - 2) * READ : (c - 1) * READ], in_=acc[:])
+
+        def unload_late(c, t, acc, copy):
+            copy(out=res[2][:, t, (c - 2) * READ : (c - 1) * READ], in_=acc[:])
 
         def store_late(pair):
             nc.sync.dma_start(out=out_planes[:, pair, WIDE:], in_=res[2][:, pair, :])
 
-        def round_columns(v0, width, copy):
+        def round_columns(dst, v0, width, copy):
             c, start = v0 // READ, v0 % READ
             src = res[c][:, :, start : start + width] if c < 2 else res[2][:, :, v0 - WIDE : v0 - WIDE + width]
-            copy(out=woven(rounded[c][:, PACK * start : PACK * (start + width)]), in_=planes(src))
+            copy(out=woven(dst[:, PACK * start : PACK * (start + width)]), in_=planes(src))
 
-        def hand_on(c):
+        def hand_on(c, src):
             nc.vector.quantize_mx(
-                out=codes[:, c * READ : (c + 1) * READ].bitcast(FP8X4), scales=out_bytes[PACK * c :, :], in_=rounded[c]
+                out=codes[:, c * READ : (c + 1) * READ].bitcast(FP8X4),
+                scales=out_bytes[PACK * (c // 2) :, c % 2 * READ : (c % 2 + 1) * READ],
+                in_=src,
             )
 
         def store_words(v0, width):
             nc.sync.dma_start(out=out_words[:, v0 : v0 + width], in_=codes[:, v0 : v0 + width].bitcast(I32))
 
+        front, back = row_pairs
+
+        def round_on_gpsimd(dst, src):
+            nc.gpsimd.tensor_scalar(
+                out=dst, in0=src, scalar1=1.0, scalar2=-0.0, op0=mybir.AluOpType.mult, op1=mybir.AluOpType.add
+            )
+
+        on_vector, on_scalar = nc.vector.tensor_copy, nc.scalar.copy
         read_last(0)
-        read_on_scalar(late[1][:, READ : 2 * READ], page[3], READ, READ)
+        read_on_scalar(last_row[1], page[3], READ, READ)
         read_last(2)
-        halves = [operand(HALF, tag) for tag in ("c", "a")]
-        for h in range(2):
+        halves = []
+        for h, tag in enumerate("ab"):
             activate(0, h * HALF, HALF)
-            quantise(z[0][:, PACK * h * HALF : PACK * (h + 1) * HALF], halves[h], 0)
-        banks0 = new_banks(READ, PACK)
+            halves.append(quantise(z[0][:, PACK * h * HALF : PACK * (h + 1) * HALF], tag))
+        banks0 = new_banks()
         for pair in row_pairs:
             for h in range(2):
                 for t in range(pair.start, pair.stop):
@@ -293,57 +302,46 @@ def tile_picked_pageread_silu_po_kernel(
         read_last(3)
         for c in range(1, chunks):
             activate(c, 0, READ)
-        second = operand(READ, "b")
-        quantise(z[1], second, 0)
-        front, back = row_pairs
-        banks1 = new_banks(READ, 2)
-        for t in range(2):
-            multiply(banks1[t][:], t, second)
-        bank1_back = multiply_pair(back, second)
-        on_vector, on_scalar = nc.vector.tensor_copy, nc.scalar.copy
-        for t in range(2):
-            on_vector(out=res[0][:, t, :], in_=banks0[t][:])
+        unload(0, 0, banks0, on_vector)
+        store(0, slice(0, 1))
+        second = quantise(z[1], "e")
+        banks1 = [multiply_plane(t, second) for t in range(PACK)]
+        for t in range(1, PACK):
+            unload(0, t, banks0, on_vector)
             store(0, slice(t, t + 1))
-        on_vector(out=res[0][:, 2, :], in_=banks0[2][:])
-        on_scalar(out=res[0][:, 3, :], in_=banks0[3][:])
-        store(0, back)
-        third, fourth = operand(READ, "a"), operand(READ, "c")
-        quantise(z[2], third, 0)
-        quantise(z[3], fourth, 0)
-        late_banks = [multiply_pair(pair, tiles) for pair in row_pairs for tiles in (third, fourth)]
-        on_scalar(out=res[1][:, 0, :], in_=banks1[0][:])
-        on_vector(out=res[1][:, 1, :], in_=banks1[1][:])
-        store(1, front)
-        on_scalar(out=res[1][:, back, :], in_=bank1_back[:])
-        store(1, back)
-        unload_pair(2, front, late_banks[0], on_vector)
-        unload_pair(3, front, late_banks[1], on_scalar)
-        store_late(front)
-        unload_pair(2, back, late_banks[2], on_vector)
-        unload_pair(3, back, late_banks[3], on_scalar)
+        third = quantise(z[2], "c")
+        banks2 = [multiply_pair(pair, third) for pair in row_pairs]
+        fourth = quantise(z[3], "d")
+        banks3 = [multiply_plane(t, fourth) for t in range(2)] + [multiply_pair(back, fourth)]
+        for t in range(PACK):
+            unload(1, t, banks1, on_scalar)
+            store(1, slice(t, t + 1))
+        rounded = [z[3]]
+        round_on_gpsimd(side_by_side(rounded[0]), res[0][:].rearrange("p t c -> p c t"))
+        for k, pair in enumerate(row_pairs):
+            unload_pair(2, pair, banks2[k], on_vector)
+        unload_late(3, 0, banks3[0], on_scalar)
+        store_late(slice(0, 1))
+        unload_late(3, 1, banks3[1], on_vector)
+        store_late(slice(1, 2))
+        unload_pair(3, back, banks3[2], on_scalar)
         store_late(back)
-        nc.gpsimd.tensor_scalar(
-            out=side_by_side(rounded[0]),
-            in0=res[0][:].rearrange("p t c -> p c t"),
-            scalar1=1.0,
-            scalar2=-0.0,
-            op0=mybir.AluOpType.mult,
-            op1=mybir.AluOpType.add,
-        )
-        round_columns(READ, READ, on_vector)
-        round_columns(2 * READ, HALF, on_scalar)
-        round_columns(2 * READ + HALF, HALF, on_vector)
-        hand_on(0)
-        hand_on(1)
+        for c, tag in ((1, "z_codesd"), (2, "z_bytesd"), (3, "rounded3")):
+            rounded.append(keep.tile([P, PACK * READ], BF16, name="rounded", tag=tag, align_bytes=64)[:])
+        round_columns(rounded[1], READ, READ, on_vector)
+        hand_on(0, rounded[0])
+        round_columns(rounded[2], 2 * READ, READ, on_scalar)
+        round_columns(rounded[3], 3 * READ, HALF, on_vector)
+        round_columns(rounded[3], 3 * READ + HALF, HALF, on_scalar)
+        hand_on(1, rounded[1])
         store_words(0, WIDE)
-        round_columns(3 * READ, READ, on_vector)
-        hand_on(2)
-        hand_on(3)
+        hand_on(2, rounded[2])
+        hand_on(3, rounded[3])
         store_words(WIDE, WIDE)
 
         for q in range(PACK):
             queue = nc.sync if q % 2 == 0 else nc.scalar
             queue.dma_start(
-                out=out_2[0, PACK * q : PACK * (q + 1), :].bitcast(I32).rearrange("r (c v) -> c r v", c=PACK),
-                in_=out_bytes[QUADRANT * q : QUADRANT * q + SCALE_ROWS, :].bitcast(I32),
+                out=out_2[0, PACK * q : PACK * (q + 1), :].bitcast(I32).rearrange("r (c v) -> c r v", c=2),
+                in_=out_bytes[QUADRANT * q : QUADRANT * q + 2 * PACK, :].bitcast(I32),
             )

@@ -25,7 +25,7 @@ PER_COL = 16
 BANKS = 8
 PICK = 256
 LEAD = 128
-CAST = 80
+CAST = 96
 WIDE = 512
 READ = 256
 HALF = READ // 2

from contextlib import ExitStack

import concourse.mybir as mybir

K, T, S, V, N, U, H = 512, 2048, 512, 1024, 512, 1024, 512
FLOPS = 2 * K * H * S + 2 * H * N * V

F32 = mybir.dt.float32
BF16 = mybir.dt.bfloat16
I32 = mybir.dt.int32
U32 = mybir.dt.uint32
U16 = mybir.dt.uint16
U8 = mybir.dt.uint8
FP8X4 = mybir.dt.float8_e4m3fn_x4
FP4X4 = mybir.dt.float4_e2m1fn_x4
SILU = mybir.ActivationFunctionType.Silu
COPY = mybir.ActivationFunctionType.Copy

P = 128
PACK = 4
QUADRANT = 32
SCALE_ROWS = 16
SPREAD = 8
PER_COL = 16
BANKS = 8
PICK = 256
LEAD = 128
CAST = 96
WIDE = 512
READ = 256
HALF = READ // 2


def tile_picked_pageread_silu_po_kernel(
    tc, x_words, x_scales, w1, mem, w2_words, w2_scales, offs, slot, rd, out_0, out_1, out_2
):
    nc = tc.nc
    with ExitStack() as ctx:
        keep = ctx.enter_context(tc.tile_pool(name="keep", bufs=1))
        psum = ctx.enter_context(tc.psum_pool(name="psum", bufs=1))

        offs_sb = keep.tile([P, S // PER_COL], U16, name="offs_sb")
        slot_sb = keep.tile([P, S // PER_COL], U16, name="slot_sb")
        rd_sb = keep.tile([P, V // PER_COL], U16, name="rd_sb")
        x_codes = keep.tile([P, T], U32, name="x_codes", align_bytes=64)
        x_bytes = keep.tile([P, T], U8, name="x_bytes", align_bytes=64)
        w1_raw = keep.tile([P, PACK, H], F32, name="w1_raw", align_bytes=64)
        spread_bytes = keep.tile([P, S], U8, name="spread_bytes", align_bytes=64)
        picked_bytes = keep.tile([P, S], U8, name="picked_bytes", align_bytes=64)
        picked_codes = keep.tile([P, S], U32, name="picked_codes", align_bytes=64)

        def scale_rows(ap, r):
            return ap[r:P:QUADRANT, :].bitcast(I32)

        def entries(lst, start, count):
            return lst[:, start // PER_COL : (start + count) // PER_COL]

        nc.gpsimd.memset(x_bytes[:].bitcast(I32), 0)
        nc.vector.memset(picked_bytes[:].bitcast(I32), 0)

        row_pairs = (slice(0, 2), slice(2, PACK))
        w1_rows = w1.rearrange("(p j) c -> p j c", j=PACK)
        nc.sync.dma_start(out=w1_raw[:, 0, :], in_=w1_rows[:, 0, :])
        nc.sync.dma_start(offs_sb[:], offs)
        nc.sync.dma_start(out=x_bytes[0:P:SPREAD, :].bitcast(I32), in_=x_scales[0].bitcast(I32))
        nc.sync.dma_start(out=w1_raw[:, 1:, :], in_=w1_rows[:, 1:, :])
        nc.sync.dma_start(out=x_codes[:].bitcast(I32), in_=x_words[0].rearrange("p c r -> p (c r)").bitcast(I32))
        nc.sync.dma_start(slot_sb[:], slot)
        nc.sync.dma_start(rd_sb[:], rd)

        nc.vector.tensor_copy(out=spread_bytes[:], in_=x_bytes[:].indirect(offs_sb[:]))
        for r in range(PACK):
            queue = nc.sync if r % 2 == 0 else nc.scalar
            queue.dma_start(out=scale_rows(picked_bytes[:], r), in_=scale_rows(spread_bytes[:], SPREAD * r))

        mem_planes = mem.rearrange("(p t) u -> p t u", t=PACK)
        page = []

        def load_page(tag):
            t = len(page)
            page.append(keep.tile([P, U], F32, name="page%d" % t, tag=tag, align_bytes=64))
            nc.sync.dma_start(out=page[t][:], in_=mem_planes[:, t, :])

        load_page("x_bytes")

        w1_bf = keep.tile([P, PACK * H], BF16, name="w1_bf", align_bytes=64)
        w1_dst = w1_bf[:].rearrange("p (t m j) -> p m j t", t=PACK, j=PACK)
        w1_src = w1_raw[:].rearrange("p j (m t) -> p m j t", t=PACK)
        nc.vector.tensor_copy(out=w1_dst[:, :CAST], in_=w1_src[:, :CAST])
        warm = keep.tile([P, 1], F32, name="warm")
        nc.scalar.activation(out=warm[:], in_=w1_raw[:, 0, 0:1], func=SILU)
        nc.scalar.copy(out=w1_dst[:, CAST:], in_=w1_src[:, CAST:])

        w1_codes = keep.tile([P, H], U32, name="w1_codes", align_bytes=64)
        w1_bytes = keep.tile([P, H], U8, name="w1_bytes", align_bytes=64)
        nc.vector.quantize_mx(out=w1_codes[:].bitcast(FP8X4), scales=w1_bytes[:], in_=w1_bf[:])

        w2_raw = keep.tile([P, 3 * N], U8, name="w2_raw", tag="w1_raw", align_bytes=64)
        nc.gpsimd.memset(w2_raw[:, 2 * N :].bitcast(I32), 0)
        nc.sync.dma_start(out=w2_raw[:, : 2 * N].bitcast(I32), in_=w2_words[0].bitcast(I32))
        for r in range(PACK):
            nc.sync.dma_start(out=scale_rows(w2_raw[:, 2 * N :], r), in_=w2_scales[0, r:SCALE_ROWS:PACK, :].bitcast(I32))
        load_page("w1_bf")
        load_page("spread_bytes")
        w2_codes = keep.tile([P, 2 * N], U8, name="w2_codes", align_bytes=64)
        w2_bytes = keep.tile([P, N], U8, name="w2_bytes", align_bytes=64)
        nc.gpsimd.tensor_copy(
            out=w2_codes[:].rearrange("p (t m b) -> p t m b", t=PACK, b=2),
            in_=w2_raw[:, : 2 * N].rearrange("p (m t b) -> p t m b", t=PACK, b=2),
        )
        nc.gpsimd.tensor_copy(
            out=w2_bytes[:].rearrange("p (t m) -> p t m", t=PACK),
            in_=w2_raw[:, 2 * N :].rearrange("p (m t) -> p t m", t=PACK),
        )

        pieces = ((0, LEAD), (LEAD, PICK), (LEAD + PICK, LEAD))
        for start, count in pieces:
            nc.vector.tensor_copy(
                out=picked_codes[:, start : start + count], in_=x_codes[:].indirect(entries(offs_sb, start, count))
            )

        load_page("x_codes")

        y = [keep.tile([P, S], F32, name="y%d" % t, align_bytes=64) for t in range(PACK)]

        def project(t, start, count):
            cols, tokens = slice(t * P, (t + 1) * P), slice(start, start + count)
            acc = psum.tile([P, count], F32, name="acc", bufs=BANKS)
            nc.tensor.matmul_mx(
                out=acc[:],
                lhsT=w1_codes[:, cols].bitcast(FP8X4),
                lhsT_scale=w1_bytes[:, cols],
                rhs=picked_codes[:, tokens].bitcast(FP8X4),
                rhs_scale=picked_bytes[:, tokens],
                start=True,
                stop=True,
            )
            nc.scalar.copy(out=y[t][:, start : start + count], in_=acc[:])

        for start, count in pieces:
            project(0, start, count)
        for t in range(1, PACK):
            project(t, 0, S)

        def scatter(t, start, count):
            nc.vector.tensor_copy(
                out=page[t][:].indirect(entries(slot_sb, start, count)), in_=y[t][:, start : start + count]
            )

        scatter(0, 0, LEAD)
        scatter(0, LEAD, S - LEAD)
        for t in range(1, PACK):
            scatter(t, 0, S)

        def read_on_scalar(dst, window, start, count):
            nc.scalar.activation(out=dst, in_=window[:].indirect(entries(rd_sb, start, count)), func=COPY)

        def side_by_side(ap):
            return ap.rearrange("p (c t) -> p c t", t=PACK)

        def woven(ap):
            return ap.rearrange("p (c i t) -> p c t i", i=4, t=PACK)

        def planes(ap):
            return ap.rearrange("p t (c i) -> p c t i", i=4)

        chunks = V // READ
        lower = [keep.tile([P, WIDE], F32, name="lower", tag=tag, align_bytes=64) for tag in ("picked_codes", "w1_bytes")]
        pitch = 3 * READ
        upper = keep.tile([P, READ + 3 * pitch + 2 * V], F32, name="upper", tag="w1_codes", align_bytes=64)
        z0 = READ + 3 * pitch
        z = [upper[:, z0 + 2 * c * READ : z0 + 2 * (c + 1) * READ].bitcast(BF16) for c in range(chunks)]
        early = [keep.tile([P, 2, width], F32, name="early%d" % width, align_bytes=64) for width in (WIDE, READ)]
        last_row = [lower[0][:, READ:], lower[1][:, READ:], upper[:, 2 * pitch + WIDE : 3 * pitch], upper[:, z0 : z0 + READ]]
        late_pair = [rows[:].rearrange("p (t c) -> p c t", t=2) for rows in lower]
        late_pair.append(upper[:, 2 * pitch : 2 * pitch + 2 * WIDE].rearrange("p (t c) -> p c t", t=2)[:, :READ, :])

        def weave_early(c):
            nc.gpsimd.tensor_scalar(
                out=side_by_side(z[c])[:, :, row_pairs[0]],
                in0=early[c // 2][:, :, c % 2 * READ : (c % 2 + 1) * READ].rearrange("p t c -> p c t"),
                scalar1=1.0,
                scalar2=-0.0,
                op0=mybir.AluOpType.mult,
                op1=mybir.AluOpType.add,
            )

        for t in range(2):
            read_on_scalar(lower[t][:], page[t], 0, WIDE)
            read_on_scalar(upper[:, t * pitch : t * pitch + WIDE], page[t], WIDE, WIDE)
            nc.scalar.activation(out=early[0][:, t, :], in_=lower[t][:], func=SILU)
            nc.scalar.activation(out=early[1][:, t, :], in_=upper[:, t * pitch : t * pitch + READ], func=SILU)
        for c in range(3):
            weave_early(c)
        for c in range(2):
            read_on_scalar(lower[c][:, :READ], page[2], c * READ, READ)
        read_on_scalar(upper[:, 2 * pitch : 2 * pitch + WIDE], page[2], WIDE, WIDE)

        def read_last(c):
            nc.vector.tensor_copy(out=last_row[c], in_=page[3][:].indirect(entries(rd_sb, c * READ, READ)))

        def activate(c, start, width):
            if c == 3:
                rows = upper[:, READ : READ + PACK * pitch].rearrange("p (t c) -> p t c", t=PACK)[:, :, :READ]
                nc.scalar.activation(out=woven(z[c]), in_=planes(rows), func=SILU)
                return
            nc.scalar.activation(
                out=side_by_side(z[c])[:, start : start + width, row_pairs[1]],
                in_=late_pair[c][:, start : start + width, :],
                func=SILU,
            )

        out_planes = out_0.rearrange("(p t) v -> p t v", t=PACK)
        out_words = out_1[0].rearrange("p c r -> p (c r)").bitcast(I32)
        out_bytes = keep.tile([P, WIDE], U8, name="out_bytes", align_bytes=64)
        codes = keep.tile([P, V], U32, name="codes", align_bytes=64)
        res = [keep.tile([P, PACK, width], F32, name="res%d" % v0, align_bytes=64) for v0, width in ((0, READ), (READ, READ), (WIDE, WIDE))]

        def quantise(src, tag):
            width = src.shape[1] // PACK
            z_codes = keep.tile([P, width], U32, name="z_codes", tag="z_codes" + tag, align_bytes=64)
            z_bytes = keep.tile([P, width], U8, name="z_bytes", tag="z_bytes" + tag, align_bytes=64)
            nc.vector.quantize_mx(out=z_codes[:].bitcast(FP8X4), scales=z_bytes[:], in_=src)
            return z_codes, z_bytes

        def multiply(acc, t, tiles):
            z_codes, z_bytes = tiles
            nc.tensor.matmul_mx(
                out=acc,
                lhsT=w2_codes[:, 2 * t * P : 2 * (t + 1) * P].bitcast(FP4X4),
                lhsT_scale=w2_bytes[:, t * P : (t + 1) * P],
                rhs=z_codes[:].bitcast(FP8X4),
                rhs_scale=z_bytes[:],
                start=True,
                stop=True,
            )

        def new_banks():
            return [psum.tile([P, READ], F32, name="acc", bufs=BANKS) for t in range(PACK)]

        def multiply_plane(t, tiles):
            acc = psum.tile([P, READ], F32, name="acc", bufs=BANKS)
            multiply(acc[:], t, tiles)
            return acc

        def multiply_pair(pair, tiles):
            acc = psum.tile([P, 2, READ], F32, name="acc", bufs=BANKS)
            for e in range(2):
                multiply(acc[:, e, :], pair.start + e, tiles)
            return acc

        def store(c, rows):
            nc.sync.dma_start(out=out_planes[:, rows, c * READ : (c + 1) * READ], in_=res[c][:, rows, :])

        def unload(c, t, banks, copy):
            copy(out=res[c][:, t, :], in_=banks[t][:])

        def unload_pair(c, pair, acc, copy):
            copy(out=res[2][:, pair, (c - 2) * READ : (c - 1) * READ], in_=acc[:])

        def unload_late(c, t, acc, copy):
            copy(out=res[2][:, t, (c - 2) * READ : (c - 1) * READ], in_=acc[:])

        def store_late(pair):
            nc.sync.dma_start(out=out_planes[:, pair, WIDE:], in_=res[2][:, pair, :])

        def round_columns(dst, v0, width, copy):
            c, start = v0 // READ, v0 % READ
            src = res[c][:, :, start : start + width] if c < 2 else res[2][:, :, v0 - WIDE : v0 - WIDE + width]
            copy(out=woven(dst[:, PACK * start : PACK * (start + width)]), in_=planes(src))

        def hand_on(c, src):
            nc.vector.quantize_mx(
                out=codes[:, c * READ : (c + 1) * READ].bitcast(FP8X4),
                scales=out_bytes[PACK * (c // 2) :, c % 2 * READ : (c % 2 + 1) * READ],
                in_=src,
            )

        def store_words(v0, width):
            nc.sync.dma_start(out=out_words[:, v0 : v0 + width], in_=codes[:, v0 : v0 + width].bitcast(I32))

        front, back = row_pairs

        def round_on_gpsimd(dst, src):
            nc.gpsimd.tensor_scalar(
                out=dst, in0=src, scalar1=1.0, scalar2=-0.0, op0=mybir.AluOpType.mult, op1=mybir.AluOpType.add
            )

        on_vector, on_scalar = nc.vector.tensor_copy, nc.scalar.copy
        read_last(0)
        read_on_scalar(last_row[1], page[3], READ, READ)
        read_last(2)
        halves = []
        for h, tag in enumerate("ab"):
            activate(0, h * HALF, HALF)
            halves.append(quantise(z[0][:, PACK * h * HALF : PACK * (h + 1) * HALF], tag))
        banks0 = new_banks()
        for pair in row_pairs:
            for h in range(2):
                for t in range(pair.start, pair.stop):
                    multiply(banks0[t][:, h * HALF : (h + 1) * HALF], t, halves[h])
        read_last(3)
        for c in range(1, chunks):
            activate(c, 0, READ)
        unload(0, 0, banks0, on_vector)
        store(0, slice(0, 1))
        second = quantise(z[1], "e")
        banks1 = [multiply_plane(t, second) for t in range(PACK)]
        for t in range(1, PACK):
            unload(0, t, banks0, on_vector)
            store(0, slice(t, t + 1))
        third = quantise(z[2], "c")
        banks2 = [multiply_pair(pair, third) for pair in row_pairs]
        fourth = quantise(z[3], "d")
        banks3 = [multiply_plane(t, fourth) for t in range(2)] + [multiply_pair(back, fourth)]
        for t in range(PACK):
            unload(1, t, banks1, on_scalar)
            store(1, slice(t, t + 1))
        rounded = [z[3]]
        round_on_gpsimd(side_by_side(rounded[0]), res[0][:].rearrange("p t c -> p c t"))
        for k, pair in enumerate(row_pairs):
            unload_pair(2, pair, banks2[k], on_vector)
        unload_late(3, 0, banks3[0], on_scalar)
        store_late(slice(0, 1))
        unload_late(3, 1, banks3[1], on_vector)
        store_late(slice(1, 2))
        unload_pair(3, back, banks3[2], on_scalar)
        store_late(back)
        for c, tag in ((1, "z_codesd"), (2, "z_bytesd"), (3, "rounded3")):
            rounded.append(keep.tile([P, PACK * READ], BF16, name="rounded", tag=tag, align_bytes=64)[:])
        round_columns(rounded[1], READ, READ, on_vector)
        hand_on(0, rounded[0])
        round_columns(rounded[2], 2 * READ, READ, on_scalar)
        round_columns(rounded[3], 3 * READ, HALF, on_vector)
        round_columns(rounded[3], 3 * READ + HALF, HALF, on_scalar)
        hand_on(1, rounded[1])
        store_words(0, WIDE)
        hand_on(2, rounded[2])
        hand_on(3, rounded[3])
        store_words(WIDE, WIDE)

        for q in range(PACK):
            queue = nc.sync if q % 2 == 0 else nc.scalar
            queue.dma_start(
                out=out_2[0, PACK * q : PACK * (q + 1), :].bitcast(I32).rearrange("r (c v) -> c r v", c=2),
                in_=out_bytes[QUADRANT * q : QUADRANT * q + 2 * PACK, :].bitcast(I32),
            )
